import numpy as np, ml_dtypes
CORES = [23,119,17,113]
N = 4
BF = ml_dtypes.bfloat16
def gentries(a):
    return np.ascontiguousarray(a.reshape(8, 16, -1).transpose(0, 2, 1)).reshape(8, -1)
def gtable(e):
    e = np.asarray(e); return np.ascontiguousarray(e.reshape(8, -1, 16).transpose(0, 2, 1)).reshape(128, -1).astype(np.int32)
W, V, I, RO = 4096, 2048, 256, 4
P = V // I
def parts(rng):
    return (rng.integers(0, W, (N, 8, 16, W)), rng.integers(0, 256, (N, 8, 16, V)), rng.integers(0, 256, (N, 8, 16, I)),
            rng.integers(0, W, (N, 8, I)), rng.integers(0, 256, (N, 8, 16)))
def pack(S, X, x, s, w):
    return {"stm": np.ascontiguousarray(S.reshape(N, 128, W)).astype(np.int32), "vx": X.reshape(N, 128, V).astype(np.float32).astype(BF),
            "x0": x.reshape(N, 128, I).astype(np.float32).astype(BF), "s0": np.stack([gtable(a) for a in s]), "wt": w.reshape(N, 128, 1).astype(np.int32)}
def two(rng, lo, hi, shape):
    return np.where(rng.random(shape) < 0.5, lo, hi)
def tame(rng, S, w, cl):
    col = np.arange(W); ev = col[((col >> 4) & 1) == 0]
    off = np.where(cl, 0, rng.integers(1, 16, cl.shape))
    S[:, ev] = 32 * np.argsort(rng.random((16, W // 32, 16)), axis=1).reshape(16, W // 2) + 16 + ((ev + off) & 15)
    w[:] = 32 * rng.integers(1, 8, 16)
    return ev
def lay(rng, S, w, cl, no):
    off = rng.integers(1, 15, cl.shape); off = np.where(cl, 0, off + (off >= 16 - no))
    S[:] = 16 * rng.integers(0, W // 16, cl.shape) + ((np.arange(W) + off) & 15)
    w[:] = 32 * rng.integers(1, 8, 16)
def wake(S, X, w, k, c):
    if (S[k, c] & (V - 1)) == (S[k ^ 1, c] & (V - 1)): S[k ^ 1, c] = S[k ^ 1, c] ^ 16
    a = S[k, c] & (V - 1); b = S[k ^ 1, c] & (V - 1)
    X[0, b] = X[0, a] ^ 1
    if int(np.add.reduce(w * np.abs(X[:, a] - X[:, b]))) & (W - 1) == 0: w[0] = w[0] ^ 32
def setup_inputs(rng):
    return pack(*parts(rng))
def setup_inputs_corners(rng):
    S, X, x, s, w = parts(rng); M = W // 2; role = rng.permutation(N)
    for q in range(N):
        kinds = rng.permutation(8); gx = int(rng.integers(0, 8))
        for g in range(8):
            kind = int(kinds[g])
            if role[q] == 0 or role[q] == 2: kind = 0 if g % 2 == 0 else 2
            if role[q] == 1: kind = 1
            if role[q] == 2 and g == gx: kind = 8
            if kind == 6:
                S[q, g] = np.arange(W)[None, :]; s[q, g, 0] = W - 1; s[q, g, I - 1] = 0; continue
            if kind == 7:
                s[q, g] = two(rng, 0, W - 1, I); continue
            cl = np.zeros((16, M), bool); p = rng.permutation(M)
            if kind == 1: cl[:] = True
            if kind == 2: cl[15] = True
            if kind == 3: cl[0] = True; cl[15] = True
            if kind == 4: cl[14:] = rng.random(M) < 0.5
            if kind == 5: cl = np.argsort(rng.random((16, M)), axis=0) < rng.integers(0, 17, M)
            if kind == 8:
                n = int(rng.integers(15, 18)); cl[3, p[:n]] = True; cl[9, p[:n]] = True
            ev = tame(rng, S[q, g], w[q, g], cl)
            s[q, g] = rng.permutation(ev[p[:I]])
    return pack(S, X, x, s, w)
def setup_inputs_late(rng):
    S, X, x, s, w = parts(rng); odd = int(rng.integers(0, 2)); col = np.arange(W)
    for q in range(N):
        if q % 2 == odd:
            al = int(rng.integers(1, 16)); n = 16 * int(rng.integers(I // 16, 5 * I // 16)) + al
            fk = rng.permutation(8 * (I - 1)).reshape(8, I - 1) < n
            for g in range(8):
                m = np.where((col & 1) == 1, rng.integers(0, 2, W), rng.integers(2, 5, W)); m[W - 1] = 0
                lay(rng, S[q, g], w[q, g], np.argsort(rng.random((16, W)), axis=0) < m, al)
                s[q, g] = 2 * rng.integers(0, W // 2, I) + 1; s[q, g, :I - 1] -= fk[g].astype(np.int64); s[q, g, I - 1] = W - 1
            continue
        kinds = rng.permutation(8)
        for g in range(8):
            kind = int(kinds[g]) // 2; Sg, Xg, wg = S[q, g], X[q, g], w[q, g]
            if kind == 3: continue
            no = int(rng.integers(1, 16)); e = 16 * (1 + rng.permutation(W // 16 - 1)[:4])
            if kind == 0:
                lay(rng, Sg, wg, np.zeros((16, W), bool), no)
                k = int(rng.integers(0, 16)); c = int(rng.integers(0, W)); at = np.arange(c & 15, W, 16)
                Sg[k, at] = c; s[q, g] = rng.choice(at, I); wake(Sg, Xg, wg, k, c); continue
            lay(rng, Sg, wg, rng.random((16, W)) < 0.0625, no)
            if kind == 1:
                Sg[Sg == 0] = 16
                Sg[0, e[0]] = 0; Sg[0, e[1]] = 5; Sg[1, e[1]] = 0
                s[q, g, 0] = e[0]; s[q, g, 1] = e[1]; wake(Sg, Xg, wg, 0, 0)
            if kind == 2:
                ka = int(rng.integers(0, 15)); kb = int(rng.integers(ka + 1, 16))
                Sg[:, e] = 16 * rng.integers(0, W // 16, (16, 4)) + rng.integers(1, 16, (16, 4))
                Sg[ka, e] = 16 * rng.integers(1, W // 16, 4); Sg[kb, e] = 0
                z = np.abs(Xg[:, Sg[kb, 0] & (V - 1)] - Xg[:, Sg[kb ^ 1, 0] & (V - 1)])
                s[q, g, 1::2] = rng.choice(e, I // 2); x[q, g, :, 1::2] = z[:, None]
    return pack(S, X, x, s, w)
def setup_inputs_ties(rng):
    S, X, x, s, w = parts(rng)
    pool = np.argsort(rng.random((N, 8, W)), axis=-1)[..., :32]; pool[..., 0] = W - 1; pool[..., 1] = 0
    S = np.take_along_axis(pool[:, :, None, :], rng.integers(0, 32, (N, 8, 16, W)), 3)
    s = np.take_along_axis(pool, rng.integers(0, 32, (N, 8, I)), 2)
    few = np.take_along_axis(X[..., :5], rng.integers(0, 5, (N, 8, 1, V)), 3)
    X[:, ::2] = few[:, ::2]; x[:, 1::2] = x[:, 1::2, :, :1]
    return pack(S, X, x, s, w)
def setup_inputs_ends(rng):
    S, X, x, s, w = parts(rng)
    S = np.where(rng.random(S.shape) < 0.7, two(rng, 0, W - 1, S.shape), S)
    S[..., 0] = two(rng, 0, W - 1, (N, 8, 16)); S[..., W - 1] = two(rng, 0, W - 1, (N, 8, 16))
    S[:, :, [0, 1, 14, 15], 0] = np.array([0, W - 1, 0, W - 1]); S[:, :, [0, 1, 14, 15], W - 1] = np.array([0, W - 1, W - 1, 0])
    S[:, :, 4:6, 0] = 0; S[:, :, 4:6, W - 1] = W - 1
    q = 16 * rng.integers(1, W // 16 - 1, (N, 8)); S[:, :, 2, 0] = q; S[:, :, 2, W - 1] = q + 15
    for a in range(N):
        for g in range(8):
            S[a, g, 2:4, q[a, g]] = W - 1; S[a, g, 2:4, q[a, g] + 15] = 0
    S[:, :, 1, W - 2] = W - 1; S[:, :, 15, W - 2] = W - 1
    X = two(rng, 0, 255, X.shape); X[..., 0] = 0; X[..., V - 1] = 255
    x = two(rng, 0, 255, x.shape); w = two(rng, 0, 255, w.shape)
    w[:, 0] = 255; w[:, 7] = 255; w[:, 1::5] = 0; w[:, 1::5, 15] = 255; w[:, 1::5, 14] = 2
    s = np.where(rng.random(s.shape) < 0.8, two(rng, 0, W - 1, s.shape), s); s[N - 1] = two(rng, 0, W - 1, (8, I))
    s[:, 7, I - 1] = W - 1; s[:, 0, 2] = W - 1; s[:, 7, 1] = 0
    s[:, 1::5, 3] = W - 2; s[:, 1::5, I - 1] = W - 2; s[:, 1::5, I - 2] = W - 1; s[:, 1::5, 4] = W - 1
    return pack(S, X, x, s, w)
def setup_inputs_spread(rng):
    S, X, x, s, w = parts(rng)
    p = rng.choice(np.array([1.0, 1.5, 2.0, 4.0]), (N, 8, 1, 1)); fl = rng.random((N, 8, 1, 1)) < 0.5
    S = np.minimum((W * rng.random(S.shape) ** p).astype(np.int64), W - 1); S = np.where(fl, W - 1 - S, S)
    s = np.minimum((W * rng.random(s.shape) ** p[..., 0]).astype(np.int64), W - 1)
    X = np.minimum((np.exp2(8 * rng.random((N, 8, 1, V))) * rng.random(X.shape)).astype(np.int64), 255)
    x = np.minimum((np.exp2(8 * rng.random((N, 8, 1, I))) * rng.random(x.shape)).astype(np.int64), 255)
    w = np.minimum(np.exp2(8 * rng.random(w.shape)).astype(np.int64), 255)
    return pack(S, X, x, s, w)
def check_inputs(d):
    bad = []
    for k, lo, hi in (("stm", 0, W - 1), ("vx", 0, 255), ("x0", 0, 255), ("s0", 0, W - 1), ("wt", 0, 255)):
        v = np.asarray(d[k]).astype(np.float64)
        if not (np.min(v) >= lo and np.max(v) <= hi): bad.append("range of " + k)
        elif np.any(v != np.floor(v)): bad.append("whole numbers in " + k)
    return bad
def reference(stm, vx, x0, s0, wt):
    S = stm.astype(np.int64).reshape(N, 8, 16, W); X = vx.astype(np.float32).astype(np.int64).reshape(N, 8, 16, V)
    x = x0.astype(np.float32).astype(np.int64).reshape(N, 8, 16, I); w = wt.astype(np.int64).reshape(N, 8, 16, 1, 1)
    s = np.stack([gentries(a) for a in s0]).astype(np.int64)
    A = np.zeros(N, np.int64); mate = np.arange(16) ^ 1
    for t in range(RO):
        c = np.take_along_axis(S, s[:, :, None, :], 3)
        a = np.take_along_axis(S, c, 3) & (V - 1); b = np.take_along_axis(S[:, :, mate], c, 3) & (V - 1)
        z = np.abs(np.take_along_axis(X, a.reshape(N, 8, 1, 16 * I), 3) - np.take_along_axis(X, b.reshape(N, 8, 1, 16 * I), 3)).reshape(N, 8, 16, 16, I)
        u = np.add.reduce(w * z, axis=2) & (W - 1)
        claim = ((((u * u) >> 5) + u + c + A[:, None, None, None]) & 15) == (s & 15)[:, :, None, :]
        n = np.add.accumulate(claim.astype(np.int64), axis=2)
        has = n[:, :, 15] >= 1; fork = n[:, :, 15] >= 2
        k1 = np.argmax(claim & (n == 1), axis=2); k2 = np.argmax(claim & (n == 2), axis=2)
        c1 = np.take_along_axis(c, k1[:, :, None, :], 2)[:, :, 0]; c2 = np.take_along_axis(c, k2[:, :, None, :], 2)[:, :, 0]
        u1 = np.take_along_axis(u, k1[:, :, None, :], 2)[:, :, 0]
        z1 = np.take_along_axis(z, k1[:, :, None, None, :], 3)[:, :, :, 0]; z2 = np.take_along_axis(z, k2[:, :, None, None, :], 3)[:, :, :, 0]
        h = 1 + t % (N - 1)
        came = np.roll(fork, h, axis=0); cc = np.roll(c2, h, axis=0); cx = np.roll(np.abs(x - z2), h, axis=0)
        s = np.where(has, c1, np.where(came, cc, (5 * s + u[:, :, 0]) & (W - 1)))
        x = np.where(has[:, :, None], (x + z1) >> 1, np.where(came[:, :, None], cx, x))
        for r in range(N):
            for g in range(8):
                i = np.flatnonzero(has[r, g])
                X[r, g][:, P * i + (u1[r, g, i] & (P - 1))] = z1[r, g][:, i]
                col, at = np.unique(c1[r, g, i], return_index=True)
                i = i[at]; k = k1[r, g, i]
                S[r, g, k, col] = (S[r, g, k, col] + u1[r, g, i]) & (W - 1)
        A = np.add.reduce(fork.astype(np.int64), axis=(1, 2)) & 15
    return {"yt": np.add.reduce(S.reshape(N, 128, W // 256, 256), axis=2).astype(np.float32), "yv": X.reshape(N, 128, V).astype(np.float32).astype(BF),
            "yx": x.reshape(N, 128, I).astype(np.float32).astype(BF), "ys": np.stack([gtable(e) for e in s]).astype(np.float32)}

@@ -1,0 +1,594 @@
+from concourse.mybir import AluOpType as A, ActivationFunctionType as F
+
+STEPS = 4
+NCH = 4
+CW = 64
+GRP = ((0, 192), (192, 256))
+OFF = (0, 256, 768, 1536)
+MAGIC = 12582912.0
+SG_SCALAR = (1, 3)
+Y_TENSOR = (0,)
+LOADS = (0, 1536, 2816, 3712, 4096)
+XR, XD = 2560, 4608
+XCY, XCH = 256, 640
+
+PF = {}
+for _i, _nm in enumerate(("hm", "cand", "kb", "hm2", "m0", "nw", "ndv", "pm", "w1", "w2", "cm", "xm", "xi", "s5",
+                          "Ic", "I16", "I32", "KC", "Dc", "r16", "q16", "cM")):
+    PF[_nm] = ("lf", 16 * _i)
+for _i, _nm in enumerate(("sm", "n0i", "n0", "m1", "yi", "y7", "sL1", "sL2", "sL3", "sL4")):
+    PF[_nm] = ("li", 16 * _i)
+for _i, _nm in enumerate(("c1U", "posU", "WLU", "XLU", "sU0", "sU1", "sU2", "sU3")):
+    PF[_nm] = ("lu", 16 * _i)
+for _i, _nm in enumerate(("ui", "um", "tt", "tb", "nc", "nd")):
+    PF[_nm] = ("gi", 256 * _i)
+for _i, _nm in enumerate(("sq", "FU", "ha", "ki", "yto", "qn")):
+    PF[_nm] = ("gf", 256 * _i)
+
+SCRATCH = {
+    "lf": ("sbuf", [128, 22 * 16], "float32"),
+    "li": ("sbuf", [128, 10 * 16], "int32"),
+    "lu": ("sbuf", [128, 8 * 16], "uint16"),
+    "gi": ("sbuf", [128, 6 * 256], "int32"),
+    "gf": ("sbuf", [128, 6 * 256], "float32"),
+    "smA": ("sbuf", [128, 16], "float16"),
+    "sL0": ("sbuf", [128, 16], "int32"),
+    "Si": ("sbuf", [128, 4096], "int32"),
+    "Sw": ("sbuf", [128, 4352], "float32"),
+    "XX": ("sbuf", [128, 6656], "bfloat16"),
+    "on": ("sbuf", [128, 2048], "bfloat16"),
+    "DA": ("sbuf", [128, 16, 8, 16], "bfloat16"),
+    "DB": ("sbuf", [128, 16, 8, 16], "bfloat16"),
+    "LR": ("sbuf", [128, 16, 8, 16], "bfloat16"),
+    "WU": ("sbuf", [128, 16, 8, 16], "bfloat16"),
+    "ER": ("sbuf", [128, 16, 128], "bfloat16"),
+    "BG": ("sbuf", [128, 8], "bfloat16"),
+    "BH": ("sbuf", [128, 8], "bfloat16"),
+    "BI": ("sbuf", [128, 128], "bfloat16"),
+    "BM": ("sbuf", [128, 128], "bfloat16"),
+    "BM10": ("sbuf", [128, 128], "bfloat16"),
+    "BM8": ("sbuf", [128, 128], "bfloat16"),
+    "Id": ("sbuf", [128, 8, 16], "bfloat16"),
+    "IdN": ("sbuf", [128, 128], "bfloat16"),
+    "Id32": ("sbuf", [128, 128], "bfloat16"),
+    "IdM": ("sbuf", [128, 8, 16], "bfloat16"),
+    "CNT": ("sbuf", [128, 8, 16], "bfloat16"),
+    "CN2": ("sbuf", [128, 8, 16], "bfloat16"),
+    "half": ("sbuf", [128, 128], "float32"),
+    "mhalf": ("sbuf", [128, 256], "bfloat16"),
+    "RS": ("sbuf", [128, 2560], "bfloat16"),
+    "kr5": ("sbuf", [128, 256], "bfloat16"),
+    "pI": ("sbuf", [128, 1], "int32"),
+    "pJ": ("sbuf", [128, 1], "int32"),
+    "kcol": ("sbuf", [128, 1], "float32"),
+    "row0": ("sbuf", [128, 1], "float32"),
+    "c16": ("sbuf", [128, 1], "float32"),
+    "Jc": ("sbuf", [128, 2, 16], "bfloat16"),
+    "wI": ("sbuf", [128, 1], "int32"),
+    "wF": ("sbuf", [128, 1], "float32"),
+    "AD": ("sbuf", [128, 2560], "bfloat16"),
+    "SC": ("sbuf", [128, 2560], "bfloat16"),
+    "jk": ("sbuf", [128, 16], "bfloat16"),
+    "acc": ("sbuf", [128, 1], "float32"),
+    "S16": ("sbuf", [128, 4096], "float16"),
+    "yso": ("sbuf", [128, 16], "float32"),
+    "AB": ("sbuf", [128, 512], "uint16"),
+    "G": ("sbuf", [128, 4096], "float16"),
+    "Xa": ("sbuf", [128, 4096], "bfloat16"),
+    "WN": ("sbuf", [128, 16, 8, 16], "bfloat16"),
+    "W2": ("sbuf", [128, 16, 8, 16], "bfloat16"),
+    "yF": ("sbuf", [128, 256], "float16"),
+    "Fp": ("sbuf", [128, 256], "float16"),
+    "z2": ("sbuf", [128, 256], "bfloat16"),
+    "ab0": ("psum", [128, 512], "float32"),
+    "ab1": ("psum", [128, 512], "float32"),
+    "us0": ("psum", [128, 512], "float32"),
+    "us1": ("psum", [128, 512], "float32"),
+    "ec": ("psum", [128, 512], "float32"),
+    "qc": ("psum", [128, 512], "float32"),
+    "kr": ("psum", [128, 512], "float32"),
+    "L": ("psum", [128, 32, 16], "float32"),
+}
+for _t in range(STEPS):
+    SCRATCH["snd%d" % _t] = ("sbuf", [128, 16], "float32")
+    SCRATCH["rcv%d" % _t] = ("sbuf", [128, 16], "float32")
+    SCRATCH["Y%d" % _t] = ("sbuf", [128, 256], "bfloat16")
+for _t in range(STEPS + 1):
+    SCRATCH["XC%d" % _t] = ("sbuf", [128, 896], "bfloat16")
+for _p in range(2):
+    SCRATCH["D%d" % _p] = ("sbuf", [128, 4096], "bfloat16")
+    SCRATCH["Z%d" % _p] = ("sbuf", [128, 4096], "bfloat16")
+    SCRATCH["z1%d" % _p] = ("sbuf", [128, 256], "bfloat16")
+    SCRATCH["cU%d" % _p] = ("sbuf", [128, 256], "uint16")
+    SCRATCH["cF%d" % _p] = ("sbuf", [128, 256], "float16")
+for _g, (_a, _b) in enumerate(GRP):
+    _n = _b - _a
+    SCRATCH["Fb%d" % _g] = ("sbuf", [128, 2, _n], "float16")
+    SCRATCH["Qt%d" % _g] = ("sbuf", [128, 7, _n], "float16")
+    SCRATCH["JU%d" % _g] = ("sbuf", [128, 2, _n // 16], "uint16")
+
+SEMAPHORES = ["eV", "eS", "eP", "eG"] + ["m%d" % i for i in range(24)]
+for _t in range(STEPS):
+    SEMAPHORES += ["an%d" % _t, "ax%d" % _t, "ln%d" % _t, "lx%d" % _t]
+
+EST = {"cyc": 0.00083 * 1.2, "fix": 0.05, "ga": 1.55, "sc": 3.8, "pe": 0.00075 * 1.15, "wake": 0.12, "net": 3.0}
+BOOST = {}
+LOOK = 0.001
+RELU_V = (2, 3)
+PSUMS = ("ab0", "ab1", "us0", "us1", "ec", "qc", "kr", "L")
+WIDTH = {}
+for _k in SCRATCH:
+    _w = 1
+    for _d in SCRATCH[_k][1][1:]:
+        _w *= _d
+    WIDTH[_k] = _w
+
+
+def rng(x):
+    name, lo, hi = x if isinstance(x, tuple) else (x, None, None)
+    if name in PF:
+        b, o = PF[name]
+        if lo is None:
+            lo, hi = 0, (16 if b[0] == "l" else 256)
+        return (b, o + lo, o + hi)
+    if lo is None:
+        lo, hi = 0, WIDTH[name]
+    return (name, lo, hi)
+
+
+def build(core, T, topo, ops):
+    rank = T.rank_of(core)
+    cyc, fix = EST["cyc"], EST["fix"]
+    GA, SCT = EST["ga"], EST["sc"]
+
+    cls = ["x"]
+
+    def add(q, fn, dur, r, w, kind="c", sem=None, cnt=1):
+        ops.append({"q": q, "fn": fn, "dur": dur, "r": [rng(x) for x in r], "w": [rng(x) for x in w], "kind": kind, "sem": sem, "cnt": cnt, "cls": cls[0]})
+
+    def V(fn, n, r, w):
+        add("V", fn, fix + cyc * max(64, n), r, w)
+
+    def S(fn, n, r, w):
+        add("S", fn, fix + 0.01 + cyc * max(64, n), r, w)
+
+    def P(fn, n, r, w):
+        add("P", fn, 0.03 + EST["pe"] * n, r, w)
+
+    def G(fn, n, r, w):
+        add("G", fn, 0.17 + 2 * cyc * n, r, w)
+
+    ndma = [0]
+
+    def dma(q, out, in_, dur, r, w):
+        s = "m%d" % ndma[0]
+        ndma[0] += 1
+        add(q, lambda e: e.dma_start(out, in_), dur, r, w, "dma", s, 16)
+
+    def pf(name, lo=None, hi=None):
+        b, lo, hi = rng(name if lo is None else (name, lo, hi))
+        return T[b][:, lo:hi]
+
+    def ts(out, i0, s1, s2, op0, op1=None):
+        if op1 is None:
+            return lambda e: e.tensor_scalar(out, i0, s1, None, op0)
+        return lambda e: e.tensor_scalar(out, i0, s1, s2, op0, op1)
+
+    def tt(out, i0, i1, op):
+        return lambda e: e.tensor_tensor(out, i0, i1, op)
+
+    def cp(out, i0):
+        return lambda e: e.tensor_copy(out, i0)
+
+    def act(out, i0, f, **k):
+        return lambda e: e.activation(out, i0, f, **k)
+
+    def asel(out, i0, pat, op, base, cm):
+        return lambda e: e.affine_select(out, i0, pat, op, 0.0, base, cm)
+
+    def mms(calls):
+        def run(e):
+            last = None
+            for c in calls:
+                last = e.matmul(c[0], c[1], c[2], c[3], c[4])
+            return last
+        return run
+
+    dma("Y", T.sL0[:], T.s0[:], 2.0, [], ["sL0"])
+    for j in range(4):
+        a, b = LOADS[j], LOADS[j + 1]
+        dma("Y" if j % 2 == 0 else "S", T.Si[:, a:b], T.stm[:, a:b], 2.0 + (b * 7.0 / 4096), [], [("Si", a, b)])
+    dma("Y", T.wI[:], T.wt[:], 6.0, [], ["wI"])
+    dma("Y", T.XX[:, XR:XR + 2048], T.vx[:], 9.0, [], [("XX", XR, XR + 2048)])
+    dma("Y", T.XX[:, XD:XD + 2048], T.vx[:], 10.0, [], [("XX", XD, XD + 2048)])
+    dma("Y", T.XC0[:, 0:256], T.x0[:], 10.5, [], [("XC0", 0, 256)])
+
+    V(lambda e: e.memset(T.on[:], 1.0), 1024, [], ["on"])
+    G(asel(T.BH[:], T.on[:, 0:8], [[-16, 8]], A.is_ge, 0, 1), 8, ["on"], ["BH"])
+    G(asel(T.BG[:], T.BH[:], [[16, 8]], A.is_ge, 15, -1), 8, ["BH"], ["BG"])
+    G(asel(T.BI[:], T.on[:, 0:128], [[-16, 8], [0, 16]], A.is_ge, 0, 1), 128, ["on"], ["BI"])
+    G(asel(T.BM[:], T.BI[:], [[16, 8], [0, 16]], A.is_ge, 15, -1), 128, ["BI"], ["BM"])
+    G(lambda e: e.iota(T.pI[:], [[0, 1]], 0, 1), 1, [], ["pI"])
+    G(lambda e: e.iota(pf("r16"), [[1, 16]], 0, 0, allow_small_or_imprecise_dtypes=True), 16, [], ["r16"])
+    G(lambda e: e.iota(pf("q16"), [[16, 16]], 0, 0, allow_small_or_imprecise_dtypes=True), 16, [], ["q16"])
+    G(asel(T.DA[:], T.on[:], [[1000, 16], [-16, 8], [-1001, 16]], A.is_equal, 0, 1), 2048, ["on"], ["DA"])
+    G(asel(T.DB[:, 0::2, :, :], T.on[:, 0:1024], [[2000, 8], [-16, 8], [-1001, 16]], A.is_equal, -1, 1), 1024, ["on"], ["DB"])
+    G(asel(T.DB[:, 1::2, :, :], T.on[:, 0:1024], [[2000, 8], [-16, 8], [-1001, 16]], A.is_equal, 1001, 1), 1024, ["on"], ["DB"])
+    G(asel(T.CNT[:], T.BM[:], [[1, 128]], A.is_ge, -1, -1), 128, ["BM"], ["CNT"])
+    G(asel(T.Id[:], T.on[:, 0:128], [[-1, 128]], A.is_equal, 0, 1), 128, ["on"], ["Id"])
+    G(lambda e: e.iota(pf("ki"), [[1, 256]], -64, 0, allow_small_or_imprecise_dtypes=True), 256, [], ["ki"])
+    V(lambda e: e.memset(T.LR[:], 0.0), 1024, [], ["LR"])
+    V(ts(T.pJ[:], T.pI[:], 15, None, A.bitwise_and), 1, ["pI"], ["pJ"])
+    V(cp(T.kcol[:], T.pJ[:]), 1, ["pJ"], ["kcol"])
+    V(ts(pf("cM"), pf("r16"), T.kcol[:], -32.0, A.is_equal, A.mult), 16, ["r16", "kcol"], ["cM"])
+    for r in range(16):
+        S(act(T.LR[:, r, :, r], T.BG[:], F.Copy), 8, ["BG"], [("LR", 128 * r, 128 * r + 128)])
+        S(act(T.ER[:, r, :], T.BM[:], F.Copy, scale=pf("cM", r, r + 1)), 128, ["BM", "cM"], [("ER", 128 * r, 128 * r + 128)])
+    V(cp(T.wF[:], T.wI[:]), 1, ["wI"], ["wF"])
+    V(ts(T.WU[:], T.LR[:], T.wF[:], None, A.mult), 1024, ["LR", "wF"], ["WU"])
+    V(ts(T.WN[:], T.WU[:], -1.0, None, A.mult), 1024, ["WU"], ["WN"])
+    V(ts(T.W2[:], T.WU[:], 2.0, None, A.mult), 1024, ["WU"], ["W2"])
+    V(ts(pf("Ic"), pf("q16"), T.kcol[:], None, A.add), 16, ["q16", "kcol"], ["Ic"])
+    for nm, f, a in (("I16", 16.0, 0.0), ("I32", 32.0, 0.0), ("KC", -1.0 / 512, 0.25), ("Dc", 1.0, 12288.0)):
+        S(act(pf(nm), pf("Ic"), F.Identity, scale=f, bias=a), 16, ["Ic"], [nm])
+    for h in range(2):
+        S(act(T.Jc[:, h, :], pf("Ic"), F.Copy, scale=16.0), 16, ["Ic"], [("Jc", 16 * h, 16 * h + 16)])
+    V(ts(T.IdM[:], T.Id[:], -100.0, None, A.mult), 64, ["Id"], ["IdM"])
+    V(lambda e: e.memset(T.c16[:], 16.0), 1, [], ["c16"])
+    for nm, f in (("Id32", 32.0), ("IdN", -1.0)):
+        S(act(T[nm][:], T.Id[:], F.Copy, scale=f), 128, ["Id"], [nm])
+    for nm, f in (("BM10", 10240.0), ("BM8", 0.125)):
+        S(act(T[nm][:], T.BM[:], F.Copy, scale=f), 128, ["BM"], [nm])
+    V(tt(T.CN2[:], T.CNT[:], T.IdM[:], A.add), 256, ["CNT", "IdM"], ["CN2"])
+    S(act(T.kr5[:], pf("ki"), F.Copy, scale=1.0 / 512), 256, ["ki"], ["kr5"])
+    V(ts(T.row0[:], T.kcol[:], 0.0, None, A.is_equal), 1, ["kcol"], ["row0"])
+    V(lambda e: e.memset(T.RS[:], 0.0), 1280, [], ["RS"])
+    for ch in range(NCH):
+        o, w = OFF[ch], 64 * (ch + 1)
+        V(lambda e, o=o, w=w: e.memset(T.RS[:, o:o + 4 * w:w], 1048576.0), 8, [], [("RS", o, o + 4 * w)])
+    for t in range(STEPS):
+        V(lambda e, t=t: e.memset(T["XC%d" % t][:, 512:XCH], 0.0), 64, [], [("XC%d" % t, 512, XCH)])
+    V(lambda e: e.memset(T.half[:], 0.5), 128, [], ["half"])
+    V(lambda e: e.memset(T.mhalf[:], -0.5), 128, [], ["mhalf"])
+    V(cp(pf("sU0"), T.sL0[:]), 16, ["sL0"], ["sU0"])
+    for j in range(4):
+        a, b = LOADS[j], LOADS[j + 1]
+        V(cp(T.Sw[:, a:b], T.Si[:, a:b]), b - a, [("Si", a, b)], [("Sw", a, b)])
+
+    SW = ("Sw", 0, 4096)
+    XW = ("XX", XR, XR + 4096)
+
+    def step(t):
+        p = t % 2
+        n = str(t)
+        sLn, sUn = "sL" + n, "sU" + n
+        sL = T.sL0[:] if t == 0 else pf(sLn)
+        cU, cF, Z, D, z1 = T["cU%d" % p], T["cF%d" % p], T["Z%d" % p], T["D%d" % p], T["z1%d" % p]
+        cUn, cFn, Zn, Dn, z1n = "cU%d" % p, "cF%d" % p, "Z%d" % p, "D%d" % p, "z1%d" % p
+        XC, XCn = T["XC" + n], "XC" + n
+        swin = T.Sw[:, 0:4096]
+        xwin = T.XX[:, XR:XR + 4096]
+        for lo, hi in ((0, 64), (64, 256)):
+            V(cp(cU[:, lo:hi], swin.indirect(pf(sUn, lo // 16, hi // 16))), GA * (hi - lo), [SW, sUn], [(cUn, lo, hi)])
+        V(ts(pf("sm"), sL, 15, None, A.bitwise_and), 16, [sLn], ["sm"])
+        V(ts(pf("s5"), sL, 5.0, None, A.mult), 16, [sLn], ["s5"])
+        if t == 0:
+            V(ts(T.smA[:], pf("sm"), 8.0, None, A.add), 16, ["sm"], ["smA"])
+        else:
+            V(ts(T.smA[:], pf("sm"), T.L[:, 8, 0:1], 8.0, A.subtract, A.add), 16, ["sm", ("L", 128, 129)], ["smA"])
+        V(ts(cF[:], cU[:], -2048.0, None, A.add), 128, [cUn], [cFn])
+        for ch in range(NCH):
+            a, b = 1024 * ch, 1024 * ch + 1024
+            w = swin.indirect(cU[:, CW * ch:CW * ch + CW])
+            r, wr = [SW, (cUn, CW * ch, CW * ch + CW)], [("G", a, b)]
+            if ch in SG_SCALAR:
+                S(act(T.G[:, a:b], w, F.Identity, bias=-2048.0), GA * 1024, r, wr)
+            else:
+                V(ts(T.G[:, a:b], w, -2048.0, None, A.add), GA * 1024, r, wr)
+        calls = [(T.ec[:, 0:256], T.Id32[:], cF[:], True, False)]
+        for r in range(16):
+            calls.append((T.ec[:, r:256:16], T.ER[:, r, :], T.smA[:], False, r == 15))
+        calls.append((T.ec[:, 256:512], T.Id[:], cF[:], True, True))
+        P(mms(calls), 512 + 1024, ["Id32", "Id", "ER", "smA", cFn], ["ec"])
+
+        def chunk(ch):
+            a, b = 1024 * ch, 1024 * ch + 1024
+            abn = ("ab0", "ab1", "us1", "ab1")[ch]
+            ao = 256 if abn == "us1" else 0
+            ab = T[abn][:, ao:ao + 128]
+            A0, A1, A2 = 128 * ch, 128 * ch + 64, 128 * ch + 128
+            calls = []
+            for o, M in ((0, T.DA), (CW, T.DB)):
+                for k in range(16):
+                    calls.append((ab[:, o:o + CW], M[:, k, :, :], T.G[:, a + k:b:16], k == 0, k == 15))
+            P(mms(calls), 2048, ["DA", "DB", ("G", a, b)], [(abn, ao, ao + 128)])
+            V(ts(T.AB[:, A0:A2], ab, 2048.0, None, A.add), 128, [(abn, ao, ao + 128)], [("AB", A0, A2)])
+            S(act(T.Xa[:, a:b], xwin.indirect(T.AB[:, A0:A1]), F.Copy), GA * 1024, [XW, ("AB", A0, A1)], [("Xa", a, b)])
+            V(tt(D[:, a:b], xwin.indirect(T.AB[:, A1:A2]), T.Xa[:, a:b], A.subtract), GA * 1024, [XW, ("AB", A1, A2), ("Xa", a, b)], [(Dn, a, b)])
+            gi = [i for i in range(len(GRP)) if GRP[i][0] <= CW * ch < GRP[i][1]][0]
+            un, o = "us%d" % gi, CW * ch - GRP[gi][0]
+            uo = T[un][:, o:o + CW]
+            if ch in RELU_V:
+                V(ts(Z[:, a:b], D[:, a:b], 0.0, None, A.max), 512, [(Dn, a, b)], [(Zn, a, b)])
+                wn = [(uo, T.WN[:, k, :, :], D[:, a + k:b:16], k == 0, False) for k in range(16)]
+                w2 = [(uo, T.W2[:, k, :, :], Z[:, a + k:b:16], False, k == 15) for k in range(16)]
+                if GRP[gi][1] - GRP[gi][0] == CW:
+                    P(mms(wn), 1024, ["WN", (Dn, a, b), (un, 256, 384)], [(un, o, o + CW)])
+                    P(mms(w2), 1024, ["W2", (Zn, a, b), (un, o, o + CW), (un, 256, 384)], [(un, o, o + CW)])
+                else:
+                    P(mms(wn + w2), 2048, ["WN", "W2", (Dn, a, b), (Zn, a, b)], [(un, o, o + CW)])
+            else:
+                S(act(Z[:, a:b], D[:, a:b], F.Abs), 1024, [(Dn, a, b)], [(Zn, a, b)])
+                P(mms([(uo, T.WU[:, k, :, :], Z[:, a + k:b:16], k == 0, k == 15) for k in range(16)]), 1024, ["WU", (Zn, a, b)], [(un, o, o + CW)])
+
+        def claims(gi):
+            lo, hi = GRP[gi]
+            m, q0, q1, w = (hi - lo) // 16, lo // 16, hi // 16, hi - lo
+            x = str(gi)
+            us, usr = T["us" + x][:, 0:w], ("us" + x, 0, w)
+            Fb, Qt, JU = T["Fb" + x], T["Qt" + x], T["JU" + x]
+            qt = lambda j, k=1: ("Qt" + x, j * w, (j + k) * w)
+            fb = lambda j: ("Fb" + x, j * w, j * w + w)
+            H = lambda nm: (nm, lo, hi)
+            h = lambda nm: pf(nm, lo, hi)
+            Q = lambda nm: (nm, q0, q1)
+            q = lambda nm: pf(nm, q0, q1)
+            cc, ccr = T.ec[:, 256 + lo:256 + hi], ("ec", 256 + lo, 256 + hi)
+            qc, qcr = T.qc[:, lo:hi], ("qc", lo, hi)
+            if gi in Y_TENSOR:
+                S(act(h("sq"), us, F.Identity, scale=1.0 / 4096, bias=MAGIC), w, [usr], [H("sq")])
+                S(act(h("qn"), h("sq"), F.Identity, scale=-4096.0, bias=4096.0 * MAGIC), w, [H("sq")], [H("qn")])
+                V(tt(T.yF[:, lo:hi], h("qn"), us, A.add), w, [H("qn"), usr], [H("yF")])
+                S(act(h("sq"), T.yF[:, lo:hi], F.Square, bias=T.c16[:]), w, [H("yF"), "c16"], [H("sq")])
+            else:
+                V(ts(h("ui"), us, 2048.0, None, A.add), w, [usr], [H("ui")])
+                V(ts(h("um"), h("ui"), 4095, None, A.bitwise_and), w, [H("ui")], [H("um")])
+                V(ts(T.yF[:, lo:hi], h("um"), -2048.0, None, A.add), w, [H("um")], [H("yF")])
+                S(act(h("sq"), T.yF[:, lo:hi], F.Square, bias=T.c16[:]), w, [H("yF"), "c16"], [H("sq")])
+            V(tt(h("tt"), h("sq"), T.ec[:, lo:hi], A.add), w, [H("sq"), H("ec")], [H("tt")])
+            V(ts(h("tb"), h("tt"), 480, None, A.bitwise_and), w, [H("tt")], [H("tb")])
+            V(ts(Qt[:, 5, :], h("tb"), 0.0, None, A.is_equal), w, [H("tb")], [qt(5)])
+            P(mms([(qc, T.CN2[:], Qt[:, 5, :], True, True)]), w, ["CN2", qt(5)], [qcr])
+            S(act(Fb[:, 0, :], qc, F.Relu, scale=-1.0, bias=-99.0), w, [qcr], [fb(0)])
+            S(act(T.Fp[:, lo:hi], qc, F.Abs, bias=99.0), w, [qcr], [H("Fp")])
+            S(act(Fb[:, 1, :], T.Fp[:, lo:hi], F.Relu, scale=-1.0, bias=1.0), w, [H("Fp")], [fb(1)])
+            S(act(Qt[:, 6, :], T.yF[:, lo:hi], F.Copy, scale=T.row0[:]), w, [H("yF"), "row0"], [qt(6)])
+            V(tt(Qt[:, 2, :], Fb[:, 0, :], cc, A.mult), w, [fb(0), ccr], [qt(2)])
+            S(act(Qt[:, 0:2, :], Fb[:], F.Copy, scale=T.kcol[:]), 2 * w, ["Fb" + x, "kcol"], [qt(0, 2)])
+            V(tt(Qt[:, 3, :], Fb[:, 1, :], cc, A.mult), w, [fb(1), ccr], [qt(3)])
+            V(tt(Qt[:, 4, :], Fb[:, 0, :], T.yF[:, lo:hi], A.mult), 2 * w, [fb(0), H("yF")], [qt(4)])
+            V(tt(h("FU"), Fb[:, 0, :], us, A.mult), w, [fb(0), usr], [H("FU")])
+            P(mms([(T.kr[:, lo:hi], T.BM[:], Qt[:, 2, :], True, False), (T.kr[:, lo:hi], T.BM10[:], Fb[:, 0, :], False, False),
+                   (T.kr[:, lo:hi], T.BM8[:], Fb[:, 0, :], False, False), (T.kr[:, lo:hi], T.Id[:], T.kr5[:, lo:hi], False, True)]), 4 * w,
+              [qt(2), fb(0), "BM", "BM10", "BM8", "Id", "kr5"], [H("kr")])
+            lc = [(T.L[:, 0:7, q0:q1], T.LR[:, r, :, :], Qt[:, :, r::16], r == 0, False) for r in range(16)]
+            lc.append((T.L[:, 0:2, q0:q1], T.Id[:], T.Jc[:, :, q0:q1], False, True))
+            P(mms(lc), 16 * max(64, 7 * m) + 64, ["LR", "Qt" + x, "Id", "Jc"], [("L", 0, 112)])
+            V(ts(q("hm"), T.L[:, 5, q0:q1], 1.0, 10240.0, A.is_ge, A.mult), m, [("L", 80, 96)], [Q("hm")])
+            V(tt(q("cand"), T.L[:, 2, q0:q1], q("hm"), A.add), m, [("L", 32, 48), Q("hm")], [Q("cand")])
+            V(tt(q("kb"), q("KC"), q("cand"), A.subtract), m, ["KC", Q("cand")], [Q("kb")])
+            V(ts(q("c1U"), T.L[:, 2, q0:q1], 2048.0, None, A.add), m, [("L", 32, 48)], [Q("c1U")])
+            V(cp(JU[:], T.L[:, 0:2, q0:q1]), 2 * m, [("L", 0, 32)], ["JU" + x])
+            for j in range(q0, q1):
+                ch = j // 4
+                ww = CW * (ch + 1)
+                o = OFF[ch] + (j % 4) * ww
+                S(act(T.AD[:, o:o + ww], T.kr[:, 0:ww], F.Abs, bias=pf("kb", j, j + 1)), ww, [("kr", 0, ww), ("kb", j, j + 1)], [("AD", o, o + ww)])
+            a, b = OFF[q0 // 4], (OFF[q1 // 4] if q1 < 16 else 2560)
+            V(lambda e: e.tensor_tensor_scan(T.SC[:, a:b], T.RS[:, a:b], T.AD[:, a:b], 1048576.0, A.add, A.min), (b - a) // 2, [("RS", a, b), ("AD", a, b)], [("SC", a, b)])
+            for ch in range(q0 // 4, q1 // 4):
+                ww, o = CW * (ch + 1), OFF[ch]
+                V(ts(pf("nw", 4 * ch, 4 * ch + 4), T.SC[:, o + ww - 1:o + 4 * ww:ww], 0.25, None, A.is_lt), 4, [("SC", o, o + 4 * ww)], [("nw", 4 * ch, 4 * ch + 4)])
+            V(tt(q("ndv"), q("nw"), q("Dc"), A.mult), m, [Q("nw"), "Dc"], [Q("ndv")])
+            V(tt(q("pm"), q("ndv"), q("cand"), A.max), m, [Q("ndv"), Q("cand")], [Q("pm")])
+            V(ts(q("posU"), q("pm"), -8192.0, None, A.add), m, [Q("pm")], [Q("posU")])
+            V(tt(h("nc"), swin.indirect(q("c1U")), h("FU"), A.add), GA * w + 64, [SW, Q("c1U"), H("FU")], [H("nc")])
+            V(ts(h("nd"), h("nc"), 4095, None, A.bitwise_and), w, [H("nc")], [H("nd")])
+            S(act(z1[:, lo:hi], D[:].indirect(JU[:, 0, :]), F.Abs), GA * w, [Dn, "JU" + x], [(z1n, lo, hi)])
+            S(act(T.z2[:, lo:hi], D[:].indirect(JU[:, 1, :]), F.Abs), GA * w, [Dn, "JU" + x], [H("z2")])
+
+        for ch in range(4):
+            cls[0] = "k%d" % ch
+            chunk(ch)
+        for gi in range(len(GRP)):
+            cls[0] = "c%d" % gi
+            claims(gi)
+        for gi, (lo, hi) in enumerate(GRP):
+            cls[0] = "c%d" % gi
+            V(cp(T.Sw[:].indirect(pf("posU", lo // 16, hi // 16)), pf("nd", lo, hi)), SCT * (hi - lo), [("nd", lo, hi), ("posU", lo // 16, hi // 16)], ["Sw"])
+        cls[0] = "y"
+        LL = lambda j: ("L", 16 * j, 16 * j + 16)
+        S(act(T.jk[:], T.L[:, 5, :], F.Sign, bias=-1.5, accum_out=T.acc[:]), 200, [LL(5)], ["jk", "acc"])
+        V(ts(pf("hm2"), T.L[:, 5, :], 2.0, 6144.0, A.is_ge, A.mult), 16, [LL(5)], ["hm2"])
+        V(tt(T["snd" + n][:], T.L[:, 3, :], pf("hm2"), A.add), 16, [LL(3), "hm2"], ["snd" + n])
+        dst = T.cores[(rank + 1 + t % (len(T.cores) - 1)) % len(T.cores)]
+        rid, pid = topo.addr(dst)[0], topo.addr(dst)[1]
+        eng = topo.engines(core, dst)[:8]
+        mask = sum(1 << e for e in eng)
+        add("G", lambda e: e.remote_dma(T["rcv" + n][:], T["snd" + n][:], T.sem["an" + n], T.sem["ln" + n], pid, rid, mask), 1.0,
+            ["snd" + n], [], "send", "an" + n, len(eng))
+        add("N", None, EST["net"], ["snd" + n], ["rcv" + n], "recv", "an" + n, len(eng))
+        V(tt(pf("n0i"), T.L[:, 6, :], pf("s5"), A.add), 16, [LL(6), "s5"], ["n0i"])
+        V(ts(pf("n0"), pf("n0i"), 4095, None, A.bitwise_and), 16, ["n0i"], ["n0"])
+        V(tt(pf("m0"), pf("n0"), pf("cand"), A.max), 16, ["n0", "cand"], ["m0"])
+        V(ts(pf("yi"), T.L[:, 4, :], 4.0, None, A.mult), 16, [LL(4)], ["yi"])
+        V(ts(pf("y7"), pf("yi"), 28, None, A.bitwise_and), 16, ["yi"], ["y7"])
+        V(tt(pf("w1"), pf("hm"), pf("I32"), A.add), 16, ["hm", "I32"], ["w1"])
+        V(tt(pf("w2"), pf("w1"), pf("y7"), A.add), 16, ["w1", "y7"], ["w2"])
+        V(ts(pf("WLU"), pf("w2"), 0.25, None, A.mult), 16, ["w2"], ["WLU"])
+        V(cp(T.XX[:].indirect(pf("WLU")), z1[:]), SCT * 256, ["WLU", z1n], ["XX"])
+        xr = ("XX", XR, XR + 2048)
+        if t + 1 < STEPS:
+            dma("Y", T.XX[:, XD:XD + 2048], T.XX[:, XR:XR + 2048], 3.0, [xr], [("XX", XD, XD + 2048)])
+            P(mms([(T.L[:, 8, 0:1], T.half[:], T.acc[:], True, True)]), 256, ["half", "acc"], [("L", 128, 129)])
+        else:
+            dma("Y", T.yv[:], T.XX[:, XR:XR + 2048], 3.0, [xr], [])
+        sN = "sL%d" % (t + 1)
+        V(tt(pf("m1"), pf("m0"), T["rcv" + n][:], A.max), 16, ["m0", "rcv" + n], ["m1"])
+        V(ts(pf(sN), pf("m1"), 4095, None, A.bitwise_and), 16, ["m1"], [sN])
+        if t + 1 < STEPS:
+            V(cp(pf("sU%d" % (t + 1)), pf(sN)), 16, [sN], ["sU%d" % (t + 1)])
+        else:
+            V(cp(T.yso[:], pf(sN)), 16, [sN], ["yso"])
+            dma("Y", T.ys[:], T.yso[:], 2.0, ["yso"], [])
+        yr = ("qc", 256, 512)
+        P(mms([(T.qc[:, 256:512], T.Id[:], T.z2[:], True, False), (T.qc[:, 256:512], T.IdN[:], XC[:, 0:256], False, True)]), 512,
+          ["Id", "IdN", "z2", (XCn, 0, 256)], [yr])
+        S(act(T["Y" + n][:], T.qc[:, 256:512], F.Abs), 256, [yr], ["Y" + n])
+        add("G", lambda e: e.remote_dma(XC[:, XCY:XCY + 256], T["Y" + n][:], T.sem["ax" + n], T.sem["lx" + n], pid, rid, mask), 1.0,
+            ["Y" + n], [], "send", "ax" + n, len(eng))
+        add("N", None, EST["net"], ["Y" + n], [(XCn, XCY, XCY + 256)], "recv", "ax" + n, len(eng))
+        P(mms([(T.kr[:, 256:512], T.Id[:], z1[:], True, False), (T.kr[:, 256:512], T.Id[:], XC[:, 0:256], False, False),
+               (T.kr[:, 256:512], T.Id[:], T.mhalf[:], False, True)]), 768, ["Id", z1n, (XCn, 0, 256), "mhalf"], [("kr", 256, 512)])
+        S(act(pf("ha"), T.kr[:, 256:512], F.Identity, bias=MAGIC, scale=0.5), 256, [("kr", 256, 512)], ["ha"])
+        S(act(XC[:, XCH:XCH + 256], pf("ha"), F.Identity, bias=-MAGIC), 256, ["ha"], [(XCn, XCH, XCH + 256)])
+        V(ts(pf("cm"), T["rcv" + n][:], 4096.0, None, A.min), 16, ["rcv" + n], ["cm"])
+        V(tt(pf("xm"), pf("cm"), pf("hm"), A.max), 16, ["cm", "hm"], ["xm"])
+        V(tt(pf("xi"), pf("xm"), pf("I16"), A.add), 16, ["xm", "I16"], ["xi"])
+        V(ts(pf("XLU"), pf("xi"), 0.0625, None, A.mult), 16, ["xi"], ["XLU"])
+        nx = "XC%d" % (t + 1)
+        S(act(T[nx][:, 0:256], XC[:].indirect(pf("XLU")), F.Copy), GA * 256, [XCn, "XLU"], [(nx, 0, 256)])
+        if t + 1 == STEPS:
+            dma("Y", T.yx[:], T[nx][:, 0:256], 2.0, [(nx, 0, 256)], [])
+
+    for t in range(STEPS):
+        step(t)
+
+    for j in range(0, 16, 2):
+        a = 256 * j
+        r, w = [("Sw", a, a + 512)], [("S16", a, a + 512)]
+        if j % 4 == 0:
+            V(ts(T.S16[:, a:a + 512], T.Sw[:, a:a + 512], -2048.0, None, A.add), 512, r, w)
+        else:
+            S(act(T.S16[:, a:a + 512], T.Sw[:, a:a + 512], F.Identity, bias=-2048.0), 512, r, w)
+        P(mms([(T.ab0[:, 0:256], T.Id[:], T.S16[:, 256 * k:256 * k + 256], k == 0, k == 15) for k in (j, j + 1)]), 512,
+          ["Id", ("S16", a, a + 512), ("ab0", 0, 256)], [("ab0", 0, 256)])
+    V(ts(pf("yto"), T.ab0[:, 0:256], 32768.0, None, A.add), 256, [("ab0", 0, 256)], ["yto"])
+    dma("Y", T.yt[:], pf("yto"), 2.0, ["yto"], [])
+
+
+def depends(ops):
+    seen = {}
+    for i, o in enumerate(ops):
+        d = set()
+        acc = [(x, False) for x in o["r"]] + [(x, True) for x in o["w"]]
+        for (b, lo, hi), wr in acc:
+            for (j, l2, h2, w2) in seen.get(b, ()):
+                if (wr or w2) and lo < h2 and l2 < hi:
+                    d.add(j)
+                elif b in PSUMS and ops[j]["q"] != o["q"]:
+                    d.add(j)
+        for (b, lo, hi), wr in acc:
+            lst = seen.setdefault(b, [])
+            if wr and b not in PSUMS:
+                lst[:] = [x for x in lst if not (lo <= x[1] and x[2] <= hi)]
+            lst.append((i, lo, hi, wr))
+            if b in PSUMS and len(lst) > 60:
+                del lst[:len(lst) - 60]
+        d.discard(i)
+        o["d"] = sorted(d)
+
+
+def schedule(ops):
+    wake = EST["wake"]
+    n = len(ops)
+    succ = [[] for _ in range(n)]
+    need = [0] * n
+    for i, o in enumerate(ops):
+        for j in o["d"]:
+            succ[j].append(i)
+        need[i] = len(o["d"])
+    prio = [0.0] * n
+    for i in range(n - 1, -1, -1):
+        best = 0.0
+        for k in succ[i]:
+            best = max(best, prio[k] + wake)
+        prio[i] = best + ops[i]["dur"]
+    for i in range(n):
+        prio[i] += BOOST.get(ops[i]["cls"], 0.0)
+    free = {}
+    ready = [(0.0, i) for i in range(n) if need[i] == 0]
+    end = [0.0] * n
+    at = [0.0] * n
+    order = []
+    while ready:
+        cand = [(max(r, free.get(ops[i]["q"], 0.0)), -prio[i], i) for r, i in ready]
+        s0 = min(cand)[0]
+        s, _, i = min([c for c in cand if c[0] <= s0 + LOOK], key=lambda c: c[1])
+        ready = [x for x in ready if x[1] != i]
+        o = ops[i]
+        end[i] = s + o["dur"]
+        at[i] = s
+        if o["kind"] == "dma":
+            free[o["q"]] = s + 0.1
+        elif o["kind"] != "recv":
+            free[o["q"]] = end[i]
+        order.append(i)
+        for k in succ[i]:
+            need[k] -= 1
+            if need[k] == 0:
+                ready.append((max([end[j] + wake for j in ops[k]["d"]]), k))
+    return order, max(end), at, end
+
+
+def rank_program(g, core, T, topo):
+    if T.rank_of(core) is None:
+        return
+    ops = []
+    build(core, T, topo, ops)
+    depends(ops)
+    order = schedule(ops)[0]
+    eng = {"V": g.vector, "S": g.scalar, "P": g.tensor, "G": g, "Y": g.sync}
+    know = {}
+    for q in eng:
+        know[q] = {}
+    count = {}
+    token = {}
+    clock = {}
+
+    def learn(q, tok):
+        k = know[q]
+        for s, c in clock.get(tok, {}).items():
+            if k.get(s, 0) < c:
+                k[s] = c
+        if k.get(tok[0], 0) < tok[1]:
+            k[tok[0]] = tok[1]
+
+    for i in order:
+        o = ops[i]
+        if o["kind"] == "recv":
+            token[i] = (o["sem"], o["cnt"])
+            continue
+        q = o["q"]
+        e = eng[q]
+        want = {}
+        for j in o["d"]:
+            if ops[j]["kind"] == "send":
+                continue
+            s, c = token[j]
+            want[s] = max(want.get(s, 0), c)
+        for s in sorted(want, key=lambda s: -sum(clock.get((s, want[s]), {}).values())):
+            if know[q].get(s, 0) < want[s]:
+                e.wait_ge(T.sem[s], want[s])
+                learn(q, (s, want[s]))
+        ins = o["fn"](e)
+        if o["kind"] == "send":
+            continue
+        if o["kind"] == "dma":
+            ins.then_inc(T.sem[o["sem"]], 16)
+            token[i] = (o["sem"], 16)
+        else:
+            s = "e" + q
+            count[s] = count.get(s, 0) + 1
+            ins.then_inc(T.sem[s], 1)
+            token[i] = (s, count[s])
+        clock[token[i]] = dict(know[q])
+        clock[token[i]][token[i][0]] = token[i][1]
+    for s in sorted(count):
+        g.wait_ge(T.sem[s], count[s])
+    for o in ops:
+        if o["kind"] == "dma":
+            g.wait_ge(T.sem[o["sem"]], 16)
+        if o["kind"] == "send":
+            g.wait_ge(T.sem["l" + o["sem"][1:]], o["cnt"])
+            g.wait_ge(T.sem[o["sem"]], o["cnt"])

@@ -1,470 +1,518 @@
+import numpy as np
 from concourse.mybir import AluOpType as A, ActivationFunctionType as F
 
 STEPS = 4
-NCH = 4
-CW = 64
-GRP = ((0, 192), (192, 256))
-OFF = (0, 256, 768, 1536)
+CHUNKS = ((192, 256), (128, 192), (64, 128), (0, 64))
+PARTS = ((128, 256), (0, 128))
+U_BANK = ("b2", "b3")
+TURNS = (("G0", "a0", "a1", "G2", "G3", "a2", "a3", "z2"), ("G1", "d0", "z0", "d1", "z1", "d2", "d3", "z3"))
+G_ON = "SVSS"
+ABS_ON = "VVSV"
+AB_ON = "SSVV"
+C_CUTS = ((128, 256), (0, 128))
+E_CUTS = ((128, 256), (0, 128))
+OLD_ON = "S"
+HALF_ON = "V"
+ON = {"rq": "S", "Fc": "V", "c": "S", "cF": "S", "sF": "S", "JU": "S", "yi": "S", "WLU": "S", "XLU": "S", "sU": "V", "ch": "S", "pos": "V"}
+TT_U16 = True
+ROUNDS = 1
+X_COPY = "Y"
+SPLIT_AB = (0,)
 MAGIC = 12582912.0
-SG_SCALAR = (1, 3)
-Y_TENSOR = (0,)
-LOADS = (0, 1536, 2816, 3712, 4096)
-XR, XD = 2560, 4608
-XCY, XCH = 256, 640
-
-PF = {}
-for _i, _nm in enumerate(("hm", "cand", "kb", "hm2", "m0", "nw", "ndv", "pm", "w1", "w2", "cm", "xm", "xi", "s5",
-                          "Ic", "I16", "I32", "KC", "Dc", "r16", "q16", "cM")):
-    PF[_nm] = ("lf", 16 * _i)
-for _i, _nm in enumerate(("sm", "n0i", "n0", "m1", "yi", "y7", "sL1", "sL2", "sL3", "sL4")):
-    PF[_nm] = ("li", 16 * _i)
-for _i, _nm in enumerate(("c1U", "posU", "WLU", "XLU", "sU0", "sU1", "sU2", "sU3")):
-    PF[_nm] = ("lu", 16 * _i)
-for _i, _nm in enumerate(("ui", "um", "tt", "tb", "nc", "nd")):
-    PF[_nm] = ("gi", 256 * _i)
-for _i, _nm in enumerate(("sq", "FU", "ha", "ki", "yto", "qn")):
-    PF[_nm] = ("gf", 256 * _i)
+NT = 9
 
 SCRATCH = {
-    "lf": ("sbuf", [128, 22 * 16], "float32"),
-    "li": ("sbuf", [128, 10 * 16], "int32"),
-    "lu": ("sbuf", [128, 8 * 16], "uint16"),
-    "gi": ("sbuf", [128, 6 * 256], "int32"),
-    "gf": ("sbuf", [128, 6 * 256], "float32"),
-    "smA": ("sbuf", [128, 16], "float16"),
-    "sL0": ("sbuf", [128, 16], "int32"),
-    "Si": ("sbuf", [128, 4096], "int32"),
-    "Sw": ("sbuf", [128, 4352], "float32"),
-    "XX": ("sbuf", [128, 6656], "bfloat16"),
-    "on": ("sbuf", [128, 2048], "bfloat16"),
-    "DA": ("sbuf", [128, 16, 8, 16], "bfloat16"),
-    "DB": ("sbuf", [128, 16, 8, 16], "bfloat16"),
-    "LR": ("sbuf", [128, 16, 8, 16], "bfloat16"),
-    "WU": ("sbuf", [128, 16, 8, 16], "bfloat16"),
-    "ER": ("sbuf", [128, 16, 128], "bfloat16"),
-    "BG": ("sbuf", [128, 8], "bfloat16"),
-    "BH": ("sbuf", [128, 8], "bfloat16"),
-    "BI": ("sbuf", [128, 128], "bfloat16"),
-    "BM": ("sbuf", [128, 128], "bfloat16"),
-    "BM10": ("sbuf", [128, 128], "bfloat16"),
-    "BM8": ("sbuf", [128, 128], "bfloat16"),
-    "Id": ("sbuf", [128, 8, 16], "bfloat16"),
-    "IdN": ("sbuf", [128, 128], "bfloat16"),
-    "Id32": ("sbuf", [128, 128], "bfloat16"),
-    "IdM": ("sbuf", [128, 8, 16], "bfloat16"),
-    "CNT": ("sbuf", [128, 8, 16], "bfloat16"),
-    "CN2": ("sbuf", [128, 8, 16], "bfloat16"),
-    "half": ("sbuf", [128, 128], "float32"),
-    "mhalf": ("sbuf", [128, 256], "bfloat16"),
-    "RS": ("sbuf", [128, 2560], "bfloat16"),
-    "kr5": ("sbuf", [128, 256], "bfloat16"),
-    "pI": ("sbuf", [128, 1], "int32"),
-    "pJ": ("sbuf", [128, 1], "int32"),
-    "kcol": ("sbuf", [128, 1], "float32"),
-    "row0": ("sbuf", [128, 1], "float32"),
-    "c16": ("sbuf", [128, 1], "float32"),
-    "Jc": ("sbuf", [128, 2, 16], "bfloat16"),
-    "wI": ("sbuf", [128, 1], "int32"),
-    "wF": ("sbuf", [128, 1], "float32"),
-    "AD": ("sbuf", [128, 2560], "bfloat16"),
-    "SC": ("sbuf", [128, 2560], "bfloat16"),
-    "jk": ("sbuf", [128, 16], "bfloat16"),
-    "acc": ("sbuf", [128, 1], "float32"),
-    "S16": ("sbuf", [128, 4096], "float16"),
-    "yso": ("sbuf", [128, 16], "float32"),
-    "AB": ("sbuf", [128, 512], "uint16"),
+    "Si": ("sbuf", [128, 4352], "int32"),
+    "XX": ("sbuf", [128, 8192], "bfloat16"),
     "G": ("sbuf", [128, 4096], "float16"),
     "Xa": ("sbuf", [128, 4096], "bfloat16"),
+    "S16": ("sbuf", [128, 4096], "float16"),
+    "AB": ("sbuf", [128, 512], "uint16"),
+    "on": ("sbuf", [128, 2048], "bfloat16"),
+    "DA": ("sbuf", [128, 16, 8, 16], "bfloat16"),
+    "DB": ("sbuf", [128, 16, 128], "bfloat16"),
+    "ER": ("sbuf", [128, 16, 128], "bfloat16"),
+    "LR": ("sbuf", [128, 16, 8, 16], "bfloat16"),
+    "WU": ("sbuf", [128, 16, 8, 16], "bfloat16"),
     "WN": ("sbuf", [128, 16, 8, 16], "bfloat16"),
-    "W2": ("sbuf", [128, 16, 8, 16], "bfloat16"),
-    "yF": ("sbuf", [128, 256], "float16"),
-    "Fp": ("sbuf", [128, 256], "float16"),
+    "PM": ("sbuf", [128, 4, 4, 32], "bfloat16"),
+    "PF": ("sbuf", [128, 2, 128], "bfloat16"),
+    "UK": ("sbuf", [128, 4, 4, 32], "bfloat16"),
+    "BI": ("sbuf", [128, 128], "bfloat16"),
+    "BM": ("sbuf", [128, 4, 32], "bfloat16"),
+    "Id": ("sbuf", [128, 4, 32], "bfloat16"),
+    "SW": ("sbuf", [128, 128], "bfloat16"),
+    "CNT": ("sbuf", [128, 128], "bfloat16"),
+    "CN2": ("sbuf", [128, 128], "bfloat16"),
+    "mat": ("sbuf", [128, 8, 128], "bfloat16"),
+    "con": ("sbuf", [128, 4, 256], "bfloat16"),
+    "RM": ("sbuf", [128, 256], "bfloat16"),
+    "RS": ("sbuf", [128, 768], "bfloat16"),
+    "r256": ("sbuf", [128, 256], "float32"),
+    "JC": ("sbuf", [128, NT, 16], "float16"),
+    "KT": ("sbuf", [128, 3, 16], "float32"),
+    "EQ": ("sbuf", [128, 16], "float32"),
+    "q16": ("sbuf", [128, 16], "float32"),
+    "Ic": ("sbuf", [128, 16], "float32"),
+    "col": ("sbuf", [128, 8], "float32"),
+    "pI": ("sbuf", [128, 4], "int32"),
+    "wI": ("sbuf", [128, 1], "int32"),
+    "sL0": ("sbuf", [128, 16], "int32"),
+    "sL": ("sbuf", [128, 16], "int32"),
+    "sU": ("sbuf", [128, 16], "uint16"),
+    "sF": ("sbuf", [128, 16], "float16"),
+    "m0": ("sbuf", [128, 16], "float32"),
+    "m1": ("sbuf", [128, 16], "int32"),
+    "hm": ("sbuf", [128, 3, 16], "float32"),
+    "yi": ("sbuf", [128, 16], "int32"),
+    "y7": ("sbuf", [128, 16], "int32"),
+    "w2": ("sbuf", [128, 16], "float32"),
+    "WLU": ("sbuf", [128, 16], "uint16"),
+    "xt": ("sbuf", [128, 16], "int32"),
+    "xi": ("sbuf", [128, 16], "float32"),
+    "XLU": ("sbuf", [128, 16], "uint16"),
+    "posU": ("sbuf", [128, 16], "uint16"),
+    "jk": ("sbuf", [128, 16], "bfloat16"),
+    "accB": ("sbuf", [128, 128], "float16"),
+    "cU": ("sbuf", [128, 256], "uint16"),
+    "cF": ("sbuf", [128, 256], "float16"),
+    "rq": ("sbuf", [128, 256], "float16"),
+    "old": ("sbuf", [128, 256], "float32"),
+    "ch": ("sbuf", [128, 2, 16], "float16"),
+    "sq": ("sbuf", [128, 256], "float32"),
+    "tt": ("sbuf", [128, 256], "int32"),
+    "tb": ("sbuf", [128, 256], "int32"),
+    "Fc": ("sbuf", [128, 256], "float16"),
+    "nc": ("sbuf", [128, 256], "int32"),
+    "nd": ("sbuf", [128, 256], "int32"),
+    "RT": ("sbuf", [128, 4, 2, 32], "float32"),
+    "eq": ("sbuf", [128, 768], "bfloat16"),
+    "lose": ("sbuf", [128, 768], "bfloat16"),
+    "CN1": ("sbuf", [128, 128], "bfloat16"),
+    "c47": ("sbuf", [128, 256], "float16"),
+    "dump": ("sbuf", [128, 16], "float32"),
+    "pos": ("sbuf", [128, 16], "float32"),
+    "b4": ("psum", [128, 512], "float32"),
+    "z1": ("sbuf", [128, 256], "bfloat16"),
     "z2": ("sbuf", [128, 256], "bfloat16"),
-    "ab0": ("psum", [128, 512], "float32"),
-    "ab1": ("psum", [128, 512], "float32"),
-    "us0": ("psum", [128, 512], "float32"),
-    "us1": ("psum", [128, 512], "float32"),
-    "ec": ("psum", [128, 512], "float32"),
-    "qc": ("psum", [128, 512], "float32"),
-    "kr": ("psum", [128, 512], "float32"),
+    "ha": ("sbuf", [128, 256], "float32"),
+    "yto": ("sbuf", [128, 256], "float32"),
+    "yso": ("sbuf", [128, 16], "float32"),
+    "rcv": ("sbuf", [128, STEPS, 16], "float32"),
+    "Y": ("sbuf", [128, STEPS, 256], "bfloat16"),
+    "XC": ("sbuf", [128, (STEPS + 1) * 768], "bfloat16"),
     "L": ("psum", [128, 32, 16], "float32"),
 }
-for _t in range(STEPS):
-    SCRATCH["snd%d" % _t] = ("sbuf", [128, 16], "float32")
-    SCRATCH["rcv%d" % _t] = ("sbuf", [128, 16], "float32")
-    SCRATCH["Y%d" % _t] = ("sbuf", [128, 256], "bfloat16")
-for _t in range(STEPS + 1):
-    SCRATCH["XC%d" % _t] = ("sbuf", [128, 896], "bfloat16")
+for _b in (0, 1, 2, 3, 5, 7):
+    SCRATCH["b%d" % _b] = ("psum", [128, 16, 2, 16], "float32")
 for _p in range(2):
     SCRATCH["D%d" % _p] = ("sbuf", [128, 4096], "bfloat16")
     SCRATCH["Z%d" % _p] = ("sbuf", [128, 4096], "bfloat16")
-    SCRATCH["z1%d" % _p] = ("sbuf", [128, 256], "bfloat16")
-    SCRATCH["cU%d" % _p] = ("sbuf", [128, 256], "uint16")
-    SCRATCH["cF%d" % _p] = ("sbuf", [128, 256], "float16")
-for _g, (_a, _b) in enumerate(GRP):
+for _g, (_a, _b) in enumerate(PARTS):
     _n = _b - _a
-    SCRATCH["Fb%d" % _g] = ("sbuf", [128, 2, _n], "float16")
-    SCRATCH["Qt%d" % _g] = ("sbuf", [128, 7, _n], "float16")
-    SCRATCH["JU%d" % _g] = ("sbuf", [128, 2, _n // 16], "uint16")
+    SCRATCH["Qt%d" % _g] = ("sbuf", [128, NT * (_n // 32), 2, 16], "float16")
+    SCRATCH["JU%d" % _g] = ("sbuf", [128, 3 * _n // 16], "uint16")
+    SCRATCH["cs%d" % _g] = ("sbuf", [128, 2 * STEPS, _n // 16], "float32")
 
 SEMAPHORES = ["eV", "eS", "eP", "eG"] + ["m%d" % i for i in range(24)]
 for _t in range(STEPS):
-    SEMAPHORES += ["an%d" % _t, "ax%d" % _t, "ln%d" % _t, "lx%d" % _t]
+    SEMAPHORES += ["ax%d" % _t, "lx%d" % _t]
+    for _g in range(len(PARTS)):
+        SEMAPHORES += ["an%d_%d" % (_t, _g), "ln%d_%d" % (_t, _g)]
 
-EST = {"cyc": 0.00083 * 1.2, "fix": 0.05, "ga": 1.55, "sc": 3.8, "pe": 0.00075 * 1.15, "wake": 0.12, "net": 3.0}
-BOOST = {}
-LOOK = 0.001
-RELU_V = (2, 3)
-PSUMS = ("ab0", "ab1", "us0", "us1", "ec", "qc", "kr", "L")
-WIDTH = {}
-for _k in SCRATCH:
-    _w = 1
-    for _d in SCRATCH[_k][1][1:]:
-        _w *= _d
-    WIDTH[_k] = _w
-
-
-def rng(x):
-    name, lo, hi = x if isinstance(x, tuple) else (x, None, None)
-    if name in PF:
-        b, o = PF[name]
-        if lo is None:
-            lo, hi = 0, (16 if b[0] == "l" else 256)
-        return (b, o + lo, o + hi)
-    if lo is None:
-        lo, hi = 0, WIDTH[name]
-    return (name, lo, hi)
+EST = {"cyc": 0.00083 * 1.1, "V": 0.02, "S": 0.03, "ind": 0.04, "ga": 1.25, "sc": 3.3, "pe": 0.0005, "wake": 0.18, "net": 2.5, "dma": 1.5, "rate": 350e3}
+CASES = ({}, {"net": 4.0, "pe": 0.0007, "wake": 0.2})
+JITTER = 0.5
+SHIFTS = 7000
+PERIOD = 21.0
+MOVES = 2000
+MARGIN = 0.6
+EARLY = 0.3
+SIZE = {"float32": 4, "int32": 4, "bfloat16": 2, "float16": 2, "uint16": 2}
 
 
-def build(core, T, topo, ops):
+def build(core, T, topo, ops, EST):
     rank = T.rank_of(core)
-    cyc, fix = EST["cyc"], EST["fix"]
-    GA, SCT = EST["ga"], EST["sc"]
+    cyc = EST["cyc"]
+    cols, times, now = {}, {}, [-1]
 
-    cls = ["x"]
+    def at(name, *idx):
+        where, shape, dt = SCRATCH[name]
+        if name not in cols:
+            cols[name] = np.arange(int(np.prod(shape[1:]))).reshape(shape[1:])
+        idx = tuple(slice(*i) if isinstance(i, tuple) else i for i in idx)
+        c = cols[name][idx].reshape(-1)
+        bits = np.zeros(cols[name].size, np.uint8)
+        bits[c] = 1
+        m = int.from_bytes(np.packbits(bits, bitorder="little").tobytes(), "little")
+        ap = T[name][(slice(None),) + idx] if idx else T[name][:]
+        return {"ap": ap, "acc": (name, m), "n": int(c.size), "two": SIZE[dt] == 2, "ps": where == "psum", "off": None, "bytes": 128 * int(c.size) * SIZE[dt]}
 
-    def add(q, fn, dur, r, w, kind="c", sem=None, cnt=1):
-        ops.append({"q": q, "fn": fn, "dur": dur, "r": [rng(x) for x in r], "w": [rng(x) for x in w], "kind": kind, "sem": sem, "cnt": cnt, "cls": cls[0]})
+    def ind(win, off):
+        return dict(win, ap=win["ap"].indirect(off["ap"]), n=16 * off["n"], off=off["acc"])
 
-    def V(fn, n, r, w):
-        add("V", fn, fix + cyc * max(64, n), r, w)
+    def val(x):
+        return x["ap"] if isinstance(x, dict) else x
 
-    def S(fn, n, r, w):
-        add("S", fn, fix + 0.01 + cyc * max(64, n), r, w)
+    def add(q, fn, dur, outs, ins, kind="c", sem=None, cnt=1):
+        r = [x["acc"] for x in ins if isinstance(x, dict)] + [x["off"] for x in ins + outs if isinstance(x, dict) and x["off"]]
+        w = [x["acc"] for x in outs]
+        banks = set(x["acc"][0] for x in ins + outs if isinstance(x, dict) and x["ps"])
+        sig = (q, now[0] < 0) + tuple(x[0].rstrip("01") if x[0][0] in "DZ" else x[0] for x in w + r)
+        times[sig] = times.get(sig, 0) + 1
+        ops.append({"slot": (sig, times[sig]), "step": max(now[0], 0), "q": q, "fn": fn, "dur": dur, "r": r, "w": w, "kind": kind, "sem": sem, "cnt": cnt, "banks": banks, "after": [], "hard": []})
 
-    def P(fn, n, r, w):
-        add("P", fn, 0.03 + EST["pe"] * n, r, w)
+    def time(q, out, i0, per):
+        if out["off"]:
+            return EST[q] + EST["ind"] + cyc * EST["sc"] * out["n"]
+        if i0["off"]:
+            return EST[q] + EST["ind"] + cyc * EST["ga"] * i0["n"]
+        return EST[q] + cyc * max(64, per * out["n"])
 
-    def G(fn, n, r, w):
-        add("G", fn, 0.17 + 2 * cyc * n, r, w)
+    def ts(out, i0, s1, op0, s2=None, op1=None):
+        a = (val(out), val(i0), val(s1), val(s2), op0) + ((op1,) if op1 is not None else ())
+        add("V", lambda e: e.tensor_scalar(*a), time("V", out, i0, 0.5 if out["two"] and i0["two"] else 1), [out], [i0, s1, s2])
+
+    def tt(out, i0, i1, op):
+        add("V", lambda e: e.tensor_tensor(val(out), val(i0), val(i1), op), time("V", out, i0, 1 if i0["ps"] or i1["ps"] else 2), [out], [i0, i1])
+
+    def cp(out, i0):
+        add("V", lambda e: e.tensor_copy(val(out), val(i0)), time("V", out, i0, 0.5 if out["two"] and i0["two"] else 1), [out], [i0])
+
+    def fill(out, c):
+        add("V", lambda e: e.memset(val(out), c), time("V", out, out, 0.5 if out["two"] else 1), [out], [])
+
+    def act(out, i0, f, acc=None, **k):
+        kw = {n: val(v) for n, v in k.items()}
+        if acc:
+            kw["accum_out"] = val(acc)
+        add("S", lambda e: e.activation(val(out), val(i0), f, **kw), time("S", out, i0, 1), [out] + ([acc] if acc else []), [i0] + list(k.values()))
+
+    def plus(q, out, i0, c):
+        if q == "S":
+            act(out, i0, F.Identity, bias=c)
+        else:
+            ts(out, i0, c, A.add)
+
+    def move(q, out, i0):
+        if q == "S":
+            act(out, i0, F.Copy)
+        else:
+            cp(out, i0)
+
+    def mms(calls, start=True, stop=True):
+        first, m = [], 0
+        for j, c in enumerate(calls):
+            first.append(start and (j == 0 or c[0]["acc"][1] & ~m != 0))
+            if first[j]:
+                m = c[0]["acc"][1]
+        first.append(stop)
+
+        def run(e):
+            last = None
+            for j, c in enumerate(calls):
+                last = e.matmul(val(c[0]), val(c[1]), val(c[2]), first[j], first[j + 1])
+            return last
+        dur = 0.03 + EST["pe"] * sum(max(64, c[2]["n"]) * (1 if c[2]["two"] else 4) for c in calls)
+        outs = [c[0] for c in calls]
+        add("P", run, dur, outs, [c[1] for c in calls] + [c[2] for c in calls] + ([] if start else outs))
+
+    def asel(out, i0, pat, op, base, cm):
+        add("G", lambda e: e.affine_select(val(out), val(i0), pat, op, 0.0, base, cm), 0.17 + 2 * cyc * out["n"], [out], [i0])
+
+    def iota(out, pat, cm, **k):
+        add("G", lambda e: e.iota(val(out), pat, 0, cm, **k), 0.13 + 2 * cyc * out["n"], [out], [])
 
     ndma = [0]
 
-    def dma(q, out, in_, dur, r, w):
+    def dma(q, out, i0, extra=0.0):
         s = "m%d" % ndma[0]
         ndma[0] += 1
-        add(q, lambda e: e.dma_start(out, in_), dur, r, w, "dma", s, 16)
+        sb = out if isinstance(out, dict) else i0
+        add(q, lambda e: e.dma_start(val(out), val(i0)), EST["dma"] + extra + sb["bytes"] / EST["rate"], [out] if isinstance(out, dict) else [],
+            [i0], "dma", s, 16)
 
-    def pf(name, lo=None, hi=None):
-        b, lo, hi = rng(name if lo is None else (name, lo, hi))
-        return T[b][:, lo:hi]
-
-    def ts(out, i0, s1, s2, op0, op1=None):
-        if op1 is None:
-            return lambda e: e.tensor_scalar(out, i0, s1, None, op0)
-        return lambda e: e.tensor_scalar(out, i0, s1, s2, op0, op1)
-
-    def tt(out, i0, i1, op):
-        return lambda e: e.tensor_tensor(out, i0, i1, op)
-
-    def cp(out, i0):
-        return lambda e: e.tensor_copy(out, i0)
-
-    def act(out, i0, f, **k):
-        return lambda e: e.activation(out, i0, f, **k)
-
-    def asel(out, i0, pat, op, base, cm):
-        return lambda e: e.affine_select(out, i0, pat, op, 0.0, base, cm)
-
-    def mms(calls):
-        def run(e):
-            last = None
-            for c in calls:
-                last = e.matmul(c[0], c[1], c[2], c[3], c[4])
-            return last
-        return run
-
-    dma("Y", T.sL0[:], T.s0[:], 2.0, [], ["sL0"])
-    for j in range(4):
-        a, b = LOADS[j], LOADS[j + 1]
-        dma("Y" if j % 2 == 0 else "S", T.Si[:, a:b], T.stm[:, a:b], 2.0 + (b * 7.0 / 4096), [], [("Si", a, b)])
-    dma("Y", T.wI[:], T.wt[:], 6.0, [], ["wI"])
-    dma("Y", T.XX[:, XR:XR + 2048], T.vx[:], 9.0, [], [("XX", XR, XR + 2048)])
-    dma("Y", T.XX[:, XD:XD + 2048], T.vx[:], 10.0, [], [("XX", XD, XD + 2048)])
-    dma("Y", T.XC0[:, 0:256], T.x0[:], 10.5, [], [("XC0", 0, 256)])
-
-    V(lambda e: e.memset(T.on[:], 1.0), 1024, [], ["on"])
-    G(asel(T.BH[:], T.on[:, 0:8], [[-16, 8]], A.is_ge, 0, 1), 8, ["on"], ["BH"])
-    G(asel(T.BG[:], T.BH[:], [[16, 8]], A.is_ge, 15, -1), 8, ["BH"], ["BG"])
-    G(asel(T.BI[:], T.on[:, 0:128], [[-16, 8], [0, 16]], A.is_ge, 0, 1), 128, ["on"], ["BI"])
-    G(asel(T.BM[:], T.BI[:], [[16, 8], [0, 16]], A.is_ge, 15, -1), 128, ["BI"], ["BM"])
-    G(lambda e: e.iota(T.pI[:], [[0, 1]], 0, 1), 1, [], ["pI"])
-    G(lambda e: e.iota(pf("r16"), [[1, 16]], 0, 0, allow_small_or_imprecise_dtypes=True), 16, [], ["r16"])
-    G(lambda e: e.iota(pf("q16"), [[16, 16]], 0, 0, allow_small_or_imprecise_dtypes=True), 16, [], ["q16"])
-    G(asel(T.DA[:], T.on[:], [[1000, 16], [-16, 8], [-1001, 16]], A.is_equal, 0, 1), 2048, ["on"], ["DA"])
-    G(asel(T.DB[:, 0::2, :, :], T.on[:, 0:1024], [[2000, 8], [-16, 8], [-1001, 16]], A.is_equal, -1, 1), 1024, ["on"], ["DB"])
-    G(asel(T.DB[:, 1::2, :, :], T.on[:, 0:1024], [[2000, 8], [-16, 8], [-1001, 16]], A.is_equal, 1001, 1), 1024, ["on"], ["DB"])
-    G(asel(T.CNT[:], T.BM[:], [[1, 128]], A.is_ge, -1, -1), 128, ["BM"], ["CNT"])
-    G(asel(T.Id[:], T.on[:, 0:128], [[-1, 128]], A.is_equal, 0, 1), 128, ["on"], ["Id"])
-    G(lambda e: e.iota(pf("ki"), [[1, 256]], -64, 0, allow_small_or_imprecise_dtypes=True), 256, [], ["ki"])
-    V(lambda e: e.memset(T.LR[:], 0.0), 1024, [], ["LR"])
-    V(ts(T.pJ[:], T.pI[:], 15, None, A.bitwise_and), 1, ["pI"], ["pJ"])
-    V(cp(T.kcol[:], T.pJ[:]), 1, ["pJ"], ["kcol"])
-    V(ts(pf("cM"), pf("r16"), T.kcol[:], -32.0, A.is_equal, A.mult), 16, ["r16", "kcol"], ["cM"])
-    for r in range(16):
-        S(act(T.LR[:, r, :, r], T.BG[:], F.Copy), 8, ["BG"], [("LR", 128 * r, 128 * r + 128)])
-        S(act(T.ER[:, r, :], T.BM[:], F.Copy, scale=pf("cM", r, r + 1)), 128, ["BM", "cM"], [("ER", 128 * r, 128 * r + 128)])
-    V(cp(T.wF[:], T.wI[:]), 1, ["wI"], ["wF"])
-    V(ts(T.WU[:], T.LR[:], T.wF[:], None, A.mult), 1024, ["LR", "wF"], ["WU"])
-    V(ts(T.WN[:], T.WU[:], -1.0, None, A.mult), 1024, ["WU"], ["WN"])
-    V(ts(T.W2[:], T.WU[:], 2.0, None, A.mult), 1024, ["WU"], ["W2"])
-    V(ts(pf("Ic"), pf("q16"), T.kcol[:], None, A.add), 16, ["q16", "kcol"], ["Ic"])
-    for nm, f, a in (("I16", 16.0, 0.0), ("I32", 32.0, 0.0), ("KC", -1.0 / 512, 0.25), ("Dc", 1.0, 12288.0)):
-        S(act(pf(nm), pf("Ic"), F.Identity, scale=f, bias=a), 16, ["Ic"], [nm])
-    for h in range(2):
-        S(act(T.Jc[:, h, :], pf("Ic"), F.Copy, scale=16.0), 16, ["Ic"], [("Jc", 16 * h, 16 * h + 16)])
-    V(ts(T.IdM[:], T.Id[:], -100.0, None, A.mult), 64, ["Id"], ["IdM"])
-    V(lambda e: e.memset(T.c16[:], 16.0), 1, [], ["c16"])
-    for nm, f in (("Id32", 32.0), ("IdN", -1.0)):
-        S(act(T[nm][:], T.Id[:], F.Copy, scale=f), 128, ["Id"], [nm])
-    for nm, f in (("BM10", 10240.0), ("BM8", 0.125)):
-        S(act(T[nm][:], T.BM[:], F.Copy, scale=f), 128, ["BM"], [nm])
-    V(tt(T.CN2[:], T.CNT[:], T.IdM[:], A.add), 256, ["CNT", "IdM"], ["CN2"])
-    S(act(T.kr5[:], pf("ki"), F.Copy, scale=1.0 / 512), 256, ["ki"], ["kr5"])
-    V(ts(T.row0[:], T.kcol[:], 0.0, None, A.is_equal), 1, ["kcol"], ["row0"])
-    V(lambda e: e.memset(T.RS[:], 0.0), 1280, [], ["RS"])
-    for ch in range(NCH):
-        o, w = OFF[ch], 64 * (ch + 1)
-        V(lambda e, o=o, w=w: e.memset(T.RS[:, o:o + 4 * w:w], 1048576.0), 8, [], [("RS", o, o + 4 * w)])
-    for t in range(STEPS):
-        V(lambda e, t=t: e.memset(T["XC%d" % t][:, 512:XCH], 0.0), 64, [], [("XC%d" % t, 512, XCH)])
-    V(lambda e: e.memset(T.half[:], 0.5), 128, [], ["half"])
-    V(lambda e: e.memset(T.mhalf[:], -0.5), 128, [], ["mhalf"])
-    V(cp(pf("sU0"), T.sL0[:]), 16, ["sL0"], ["sU0"])
-    for j in range(4):
-        a, b = LOADS[j], LOADS[j + 1]
-        V(cp(T.Sw[:, a:b], T.Si[:, a:b]), b - a, [("Si", a, b)], [("Sw", a, b)])
-
-    SW = ("Sw", 0, 4096)
-    XW = ("XX", XR, XR + 4096)
-
-    def step(t):
-        p = t % 2
-        n = str(t)
-        sLn, sUn = "sL" + n, "sU" + n
-        sL = T.sL0[:] if t == 0 else pf(sLn)
-        cU, cF, Z, D, z1 = T["cU%d" % p], T["cF%d" % p], T["Z%d" % p], T["D%d" % p], T["z1%d" % p]
-        cUn, cFn, Zn, Dn, z1n = "cU%d" % p, "cF%d" % p, "Z%d" % p, "D%d" % p, "z1%d" % p
-        XC, XCn = T["XC" + n], "XC" + n
-        swin = T.Sw[:, 0:4096]
-        xwin = T.XX[:, XR:XR + 4096]
-        for lo, hi in ((0, 64), (64, 256)):
-            V(cp(cU[:, lo:hi], swin.indirect(pf(sUn, lo // 16, hi // 16))), GA * (hi - lo), [SW, sUn], [(cUn, lo, hi)])
-        V(ts(pf("sm"), sL, 15, None, A.bitwise_and), 16, [sLn], ["sm"])
-        V(ts(pf("s5"), sL, 5.0, None, A.mult), 16, [sLn], ["s5"])
-        if t == 0:
-            V(ts(T.smA[:], pf("sm"), 8.0, None, A.add), 16, ["sm"], ["smA"])
-        else:
-            V(ts(T.smA[:], pf("sm"), T.L[:, 8, 0:1], 8.0, A.subtract, A.add), 16, ["sm", ("L", 128, 129)], ["smA"])
-        V(ts(cF[:], cU[:], -2048.0, None, A.add), 128, [cUn], [cFn])
-        for ch in range(NCH):
-            a, b = 1024 * ch, 1024 * ch + 1024
-            w = swin.indirect(cU[:, CW * ch:CW * ch + CW])
-            r, wr = [SW, (cUn, CW * ch, CW * ch + CW)], [("G", a, b)]
-            if ch in SG_SCALAR:
-                S(act(T.G[:, a:b], w, F.Identity, bias=-2048.0), GA * 1024, r, wr)
-            else:
-                V(ts(T.G[:, a:b], w, -2048.0, None, A.add), GA * 1024, r, wr)
-        calls = [(T.ec[:, 0:256], T.Id32[:], cF[:], True, False)]
-        for r in range(16):
-            calls.append((T.ec[:, r:256:16], T.ER[:, r, :], T.smA[:], False, r == 15))
-        calls.append((T.ec[:, 256:512], T.Id[:], cF[:], True, True))
-        P(mms(calls), 512 + 1024, ["Id32", "Id", "ER", "smA", cFn], ["ec"])
-
-        def chunk(ch):
-            a, b = 1024 * ch, 1024 * ch + 1024
-            abn = ("ab0", "ab1", "us1", "ab1")[ch]
-            ao = 256 if abn == "us1" else 0
-            ab = T[abn][:, ao:ao + 128]
-            A0, A1, A2 = 128 * ch, 128 * ch + 64, 128 * ch + 128
-            calls = []
-            for o, M in ((0, T.DA), (CW, T.DB)):
-                for k in range(16):
-                    calls.append((ab[:, o:o + CW], M[:, k, :, :], T.G[:, a + k:b:16], k == 0, k == 15))
-            P(mms(calls), 2048, ["DA", "DB", ("G", a, b)], [(abn, ao, ao + 128)])
-            V(ts(T.AB[:, A0:A2], ab, 2048.0, None, A.add), 128, [(abn, ao, ao + 128)], [("AB", A0, A2)])
-            S(act(T.Xa[:, a:b], xwin.indirect(T.AB[:, A0:A1]), F.Copy), GA * 1024, [XW, ("AB", A0, A1)], [("Xa", a, b)])
-            V(tt(D[:, a:b], xwin.indirect(T.AB[:, A1:A2]), T.Xa[:, a:b], A.subtract), GA * 1024, [XW, ("AB", A1, A2), ("Xa", a, b)], [(Dn, a, b)])
-            gi = [i for i in range(len(GRP)) if GRP[i][0] <= CW * ch < GRP[i][1]][0]
-            un, o = "us%d" % gi, CW * ch - GRP[gi][0]
-            uo = T[un][:, o:o + CW]
-            if ch in RELU_V:
-                V(ts(Z[:, a:b], D[:, a:b], 0.0, None, A.max), 512, [(Dn, a, b)], [(Zn, a, b)])
-                wn = [(uo, T.WN[:, k, :, :], D[:, a + k:b:16], k == 0, False) for k in range(16)]
-                w2 = [(uo, T.W2[:, k, :, :], Z[:, a + k:b:16], False, k == 15) for k in range(16)]
-                if GRP[gi][1] - GRP[gi][0] == CW:
-                    P(mms(wn), 1024, ["WN", (Dn, a, b), (un, 256, 384)], [(un, o, o + CW)])
-                    P(mms(w2), 1024, ["W2", (Zn, a, b), (un, o, o + CW), (un, 256, 384)], [(un, o, o + CW)])
-                else:
-                    P(mms(wn + w2), 2048, ["WN", "W2", (Dn, a, b), (Zn, a, b)], [(un, o, o + CW)])
-            else:
-                S(act(Z[:, a:b], D[:, a:b], F.Abs), 1024, [(Dn, a, b)], [(Zn, a, b)])
-                P(mms([(uo, T.WU[:, k, :, :], Z[:, a + k:b:16], k == 0, k == 15) for k in range(16)]), 1024, ["WU", (Zn, a, b)], [(un, o, o + CW)])
-
-        def claims(gi):
-            lo, hi = GRP[gi]
-            m, q0, q1, w = (hi - lo) // 16, lo // 16, hi // 16, hi - lo
-            x = str(gi)
-            us, usr = T["us" + x][:, 0:w], ("us" + x, 0, w)
-            Fb, Qt, JU = T["Fb" + x], T["Qt" + x], T["JU" + x]
-            qt = lambda j, k=1: ("Qt" + x, j * w, (j + k) * w)
-            fb = lambda j: ("Fb" + x, j * w, j * w + w)
-            H = lambda nm: (nm, lo, hi)
-            h = lambda nm: pf(nm, lo, hi)
-            Q = lambda nm: (nm, q0, q1)
-            q = lambda nm: pf(nm, q0, q1)
-            cc, ccr = T.ec[:, 256 + lo:256 + hi], ("ec", 256 + lo, 256 + hi)
-            qc, qcr = T.qc[:, lo:hi], ("qc", lo, hi)
-            if gi in Y_TENSOR:
-                S(act(h("sq"), us, F.Identity, scale=1.0 / 4096, bias=MAGIC), w, [usr], [H("sq")])
-                S(act(h("qn"), h("sq"), F.Identity, scale=-4096.0, bias=4096.0 * MAGIC), w, [H("sq")], [H("qn")])
-                V(tt(T.yF[:, lo:hi], h("qn"), us, A.add), w, [H("qn"), usr], [H("yF")])
-                S(act(h("sq"), T.yF[:, lo:hi], F.Square, bias=T.c16[:]), w, [H("yF"), "c16"], [H("sq")])
-            else:
-                V(ts(h("ui"), us, 2048.0, None, A.add), w, [usr], [H("ui")])
-                V(ts(h("um"), h("ui"), 4095, None, A.bitwise_and), w, [H("ui")], [H("um")])
-                V(ts(T.yF[:, lo:hi], h("um"), -2048.0, None, A.add), w, [H("um")], [H("yF")])
-                S(act(h("sq"), T.yF[:, lo:hi], F.Square, bias=T.c16[:]), w, [H("yF"), "c16"], [H("sq")])
-            V(tt(h("tt"), h("sq"), T.ec[:, lo:hi], A.add), w, [H("sq"), H("ec")], [H("tt")])
-            V(ts(h("tb"), h("tt"), 480, None, A.bitwise_and), w, [H("tt")], [H("tb")])
-            V(ts(Qt[:, 5, :], h("tb"), 0.0, None, A.is_equal), w, [H("tb")], [qt(5)])
-            P(mms([(qc, T.CN2[:], Qt[:, 5, :], True, True)]), w, ["CN2", qt(5)], [qcr])
-            S(act(Fb[:, 0, :], qc, F.Relu, scale=-1.0, bias=-99.0), w, [qcr], [fb(0)])
-            S(act(T.Fp[:, lo:hi], qc, F.Abs, bias=99.0), w, [qcr], [H("Fp")])
-            S(act(Fb[:, 1, :], T.Fp[:, lo:hi], F.Relu, scale=-1.0, bias=1.0), w, [H("Fp")], [fb(1)])
-            S(act(Qt[:, 6, :], T.yF[:, lo:hi], F.Copy, scale=T.row0[:]), w, [H("yF"), "row0"], [qt(6)])
-            V(tt(Qt[:, 2, :], Fb[:, 0, :], cc, A.mult), w, [fb(0), ccr], [qt(2)])
-            S(act(Qt[:, 0:2, :], Fb[:], F.Copy, scale=T.kcol[:]), 2 * w, ["Fb" + x, "kcol"], [qt(0, 2)])
-            V(tt(Qt[:, 3, :], Fb[:, 1, :], cc, A.mult), w, [fb(1), ccr], [qt(3)])
-            V(tt(Qt[:, 4, :], Fb[:, 0, :], T.yF[:, lo:hi], A.mult), 2 * w, [fb(0), H("yF")], [qt(4)])
-            V(tt(h("FU"), Fb[:, 0, :], us, A.mult), w, [fb(0), usr], [H("FU")])
-            P(mms([(T.kr[:, lo:hi], T.BM[:], Qt[:, 2, :], True, False), (T.kr[:, lo:hi], T.BM10[:], Fb[:, 0, :], False, False),
-                   (T.kr[:, lo:hi], T.BM8[:], Fb[:, 0, :], False, False), (T.kr[:, lo:hi], T.Id[:], T.kr5[:, lo:hi], False, True)]), 4 * w,
-              [qt(2), fb(0), "BM", "BM10", "BM8", "Id", "kr5"], [H("kr")])
-            lc = [(T.L[:, 0:7, q0:q1], T.LR[:, r, :, :], Qt[:, :, r::16], r == 0, False) for r in range(16)]
-            lc.append((T.L[:, 0:2, q0:q1], T.Id[:], T.Jc[:, :, q0:q1], False, True))
-            P(mms(lc), 16 * max(64, 7 * m) + 64, ["LR", "Qt" + x, "Id", "Jc"], [("L", 0, 112)])
-            V(ts(q("hm"), T.L[:, 5, q0:q1], 1.0, 10240.0, A.is_ge, A.mult), m, [("L", 80, 96)], [Q("hm")])
-            V(tt(q("cand"), T.L[:, 2, q0:q1], q("hm"), A.add), m, [("L", 32, 48), Q("hm")], [Q("cand")])
-            V(tt(q("kb"), q("KC"), q("cand"), A.subtract), m, ["KC", Q("cand")], [Q("kb")])
-            V(ts(q("c1U"), T.L[:, 2, q0:q1], 2048.0, None, A.add), m, [("L", 32, 48)], [Q("c1U")])
-            V(cp(JU[:], T.L[:, 0:2, q0:q1]), 2 * m, [("L", 0, 32)], ["JU" + x])
-            for j in range(q0, q1):
-                ch = j // 4
-                ww = CW * (ch + 1)
-                o = OFF[ch] + (j % 4) * ww
-                S(act(T.AD[:, o:o + ww], T.kr[:, 0:ww], F.Abs, bias=pf("kb", j, j + 1)), ww, [("kr", 0, ww), ("kb", j, j + 1)], [("AD", o, o + ww)])
-            a, b = OFF[q0 // 4], (OFF[q1 // 4] if q1 < 16 else 2560)
-            V(lambda e: e.tensor_tensor_scan(T.SC[:, a:b], T.RS[:, a:b], T.AD[:, a:b], 1048576.0, A.add, A.min), (b - a) // 2, [("RS", a, b), ("AD", a, b)], [("SC", a, b)])
-            for ch in range(q0 // 4, q1 // 4):
-                ww, o = CW * (ch + 1), OFF[ch]
-                V(ts(pf("nw", 4 * ch, 4 * ch + 4), T.SC[:, o + ww - 1:o + 4 * ww:ww], 0.25, None, A.is_lt), 4, [("SC", o, o + 4 * ww)], [("nw", 4 * ch, 4 * ch + 4)])
-            V(tt(q("ndv"), q("nw"), q("Dc"), A.mult), m, [Q("nw"), "Dc"], [Q("ndv")])
-            V(tt(q("pm"), q("ndv"), q("cand"), A.max), m, [Q("ndv"), Q("cand")], [Q("pm")])
-            V(ts(q("posU"), q("pm"), -8192.0, None, A.add), m, [Q("pm")], [Q("posU")])
-            V(tt(h("nc"), swin.indirect(q("c1U")), h("FU"), A.add), GA * w + 64, [SW, Q("c1U"), H("FU")], [H("nc")])
-            V(ts(h("nd"), h("nc"), 4095, None, A.bitwise_and), w, [H("nc")], [H("nd")])
-            S(act(z1[:, lo:hi], D[:].indirect(JU[:, 0, :]), F.Abs), GA * w, [Dn, "JU" + x], [(z1n, lo, hi)])
-            S(act(T.z2[:, lo:hi], D[:].indirect(JU[:, 1, :]), F.Abs), GA * w, [Dn, "JU" + x], [H("z2")])
-
-        for ch in range(4):
-            cls[0] = "k%d" % ch
-            chunk(ch)
-        for gi in range(len(GRP)):
-            cls[0] = "c%d" % gi
-            claims(gi)
-        for gi, (lo, hi) in enumerate(GRP):
-            cls[0] = "c%d" % gi
-            V(cp(T.Sw[:].indirect(pf("posU", lo // 16, hi // 16)), pf("nd", lo, hi)), SCT * (hi - lo), [("nd", lo, hi), ("posU", lo // 16, hi // 16)], ["Sw"])
-        cls[0] = "y"
-        LL = lambda j: ("L", 16 * j, 16 * j + 16)
-        S(act(T.jk[:], T.L[:, 5, :], F.Sign, bias=-1.5, accum_out=T.acc[:]), 200, [LL(5)], ["jk", "acc"])
-        V(ts(pf("hm2"), T.L[:, 5, :], 2.0, 6144.0, A.is_ge, A.mult), 16, [LL(5)], ["hm2"])
-        V(tt(T["snd" + n][:], T.L[:, 3, :], pf("hm2"), A.add), 16, [LL(3), "hm2"], ["snd" + n])
-        dst = T.cores[(rank + 1 + t % (len(T.cores) - 1)) % len(T.cores)]
+    def send(out, i0, sem, dst):
         rid, pid = topo.addr(dst)[0], topo.addr(dst)[1]
         eng = topo.engines(core, dst)[:8]
         mask = sum(1 << e for e in eng)
-        add("G", lambda e: e.remote_dma(T["rcv" + n][:], T["snd" + n][:], T.sem["an" + n], T.sem["ln" + n], pid, rid, mask), 1.0,
-            ["snd" + n], [], "send", "an" + n, len(eng))
-        add("N", None, EST["net"], ["snd" + n], ["rcv" + n], "recv", "an" + n, len(eng))
-        V(tt(pf("n0i"), T.L[:, 6, :], pf("s5"), A.add), 16, [LL(6), "s5"], ["n0i"])
-        V(ts(pf("n0"), pf("n0i"), 4095, None, A.bitwise_and), 16, ["n0i"], ["n0"])
-        V(tt(pf("m0"), pf("n0"), pf("cand"), A.max), 16, ["n0", "cand"], ["m0"])
-        V(ts(pf("yi"), T.L[:, 4, :], 4.0, None, A.mult), 16, [LL(4)], ["yi"])
-        V(ts(pf("y7"), pf("yi"), 28, None, A.bitwise_and), 16, ["yi"], ["y7"])
-        V(tt(pf("w1"), pf("hm"), pf("I32"), A.add), 16, ["hm", "I32"], ["w1"])
-        V(tt(pf("w2"), pf("w1"), pf("y7"), A.add), 16, ["w1", "y7"], ["w2"])
-        V(ts(pf("WLU"), pf("w2"), 0.25, None, A.mult), 16, ["w2"], ["WLU"])
-        V(cp(T.XX[:].indirect(pf("WLU")), z1[:]), SCT * 256, ["WLU", z1n], ["XX"])
-        xr = ("XX", XR, XR + 2048)
-        if t + 1 < STEPS:
-            dma("Y", T.XX[:, XD:XD + 2048], T.XX[:, XR:XR + 2048], 3.0, [xr], [("XX", XD, XD + 2048)])
-            P(mms([(T.L[:, 8, 0:1], T.half[:], T.acc[:], True, True)]), 256, ["half", "acc"], [("L", 128, 129)])
+        add("G", lambda e: e.remote_dma(val(out), val(i0), T.sem["a" + sem], T.sem["l" + sem], pid, rid, mask), 0.6, [], [i0], "send", "a" + sem, len(eng))
+        add("N", None, EST["net"] + out["bytes"] / 60e3, [out], [i0], "recv", "a" + sem, len(eng))
+        ops[-1]["after"].append((len(ops) - 2, 0.0))
+        ops[-1]["hard"].append(len(ops) - 2)
+
+    dma("Y", at("sL0"), T.s0[:])
+    dma("Y", at("Si", (0, 4096)), T.stm[:])
+    dma("Y", at("wI"), T.wt[:], 6.0)
+    dma("Y", at("XX", (0, 2048)), T.vx[:], 6.0)
+    dma("Y", at("XX", (2048, 4096)), T.vx[:], 7.5)
+    dma("Y", at("XC", (0, 256)), T.x0[:], 9.0)
+    for j in range(1, 6):
+        ops[j]["after"].append((j - 1, 0.1 - ops[j - 1]["dur"]))
+        ops[j]["hard"].append(j - 1)
+
+    Id, BM, on = at("Id"), at("BM"), at("on", (0, 128))
+    kcol, dump, row0, c16, wF, acc, kfr, cm99 = [at("col", (j, j + 1)) for j in range(8)]
+    Id32, IdK, Id5, IdN, IdH, IdM, BMK, IdT = [at("mat", j) for j in range(8)]
+    fill(at("on"), 1.0)
+    iota(at("pI", (0, 1)), [[0, 1]], 1)
+    iota(at("q16"), [[16, 16]], 0, allow_small_or_imprecise_dtypes=True)
+    iota(at("r256"), [[0, 16], [1, 16]], 0, allow_small_or_imprecise_dtypes=True)
+    asel(Id, on, [[-1, 128]], A.is_equal, 0, 1)
+    asel(at("SW"), on, [[-2, 64], [1, 2]], A.is_equal, -1, 1)
+    asel(at("BI"), on, [[-16, 8], [0, 16]], A.is_ge, 0, 1)
+    asel(BM, at("BI"), [[16, 8], [0, 16]], A.is_ge, 15, -1)
+    asel(at("CNT"), BM, [[1, 128]], A.is_ge, -1, -1)
+    asel(at("DA"), at("on"), [[1000, 16], [-16, 8], [-1001, 16]], A.is_equal, 0, 1)
+    ts(at("pI", (2, 3)), at("pI", (0, 1)), 15, A.bitwise_and)
+    cp(kcol, at("pI", (2, 3)))
+    ts(row0, kcol, 0.0, A.is_equal, 4096.0, A.mult)
+    ts(kfr, kcol, 1.0 / 4096, A.mult)
+    fill(c16, 16.0)
+    fill(cm99, -99.0 * 4096)
+    cp(wF, at("wI"))
+    ts(at("EQ"), at("r256", (0, 16)), kcol, A.is_equal)
+    fill(at("LR"), 0.0)
+    for r in range(16):
+        ts(at("DB", r), at("SW"), at("EQ", (r ^ 1, (r ^ 1) + 1)), A.mult)
+        ts(at("ER", r), BM, at("EQ", (r, r + 1)), A.mult, -32.0, A.mult)
+        act(at("LR", r, (0, 8), r), at("BM", (0, 4), (0, 32, 16)), F.Copy)
+    ts(at("WU"), at("LR"), wF, A.mult, 1.0 / 4096, A.mult)
+    if "V" in ABS_ON:
+        ts(at("WN"), at("LR"), wF, A.mult, -1.0 / 4096, A.mult)
+    for m, f in ((Id32, 32.0), (IdK, 1.0 / 4096), (Id5, 5.0), (IdN, -1.0), (IdH, 0.5), (IdM, -100.0), (IdT, -2.0)):
+        act(m, Id, F.Copy, scale=f)
+    tt(at("CN2"), at("CNT"), IdM, A.add)
+    tt(BMK, Id, at("CNT"), A.subtract)
+    act(at("CN1"), BMK, F.Copy, scale=4096.0)
+    act(at("c47"), at("on", (0, 256)), F.Copy, scale=-2047.0)
+    for j, c in enumerate((32.0, 1024.0, -0.5, 6144.0)):
+        fill(at("con", j), c)
+    ts(at("RM"), at("r256"), kcol, A.is_ge, 0.5, A.mult)
+    fill(at("RS"), 1.0)
+    fill(at("RS", (0, 768, 32)), 0.0)
+    fill(at("PM"), 0.0)
+    fill(at("UK"), 0.0)
+    for a in range(2):
+        for b in range(2):
+            act(at("PM", 2 * a + b, (0, 4), (16 * b, 16 * b + 16)), at("BM", (0, 4), (16 * a, 16 * a + 16)), F.Copy)
+            act(at("UK", 2 * a + b, (0, 4), (16 * b, 16 * b + 16)), at("Id", (0, 4), (16 * a, 16 * a + 16)), F.Copy, scale=16384.0)
+    for a in range(2):
+        tt(at("PF", a), at("PM", 2 * a), at("PM", 2 * a + 1), A.add)
+    ts(at("Ic"), at("q16"), kcol, A.add)
+    ts(at("dump"), at("Ic"), 4096.0, A.add)
+    for j, (f, c) in enumerate(((16.0, 0.0), (16.0, 0.0), (0.0, 32768.0), (0.0, 2048.0), (0.0, 0.0), (0.0, 0.0), (-1.0 / 512, -1.0), (0.0, 14336.0), (0.0, 0.0))):
+        ts(at("JC", j), at("Ic"), f, A.mult, c, A.add)
+    for j, c in enumerate((16.0, 8.0, -4096.0)):
+        fill(at("KT", j), c)
+    act(at("accB"), on, F.Copy, scale=0.0625)
+    cp(at("sU"), at("sL0"))
+
+    swin, xwin = at("Si", (0, 4096)), at("XX", (0, 4096))
+
+    def step(t):
+        last = t + 1 == STEPS
+        D, Z = "D%d" % (t % 2), "Z%d" % (t % 2)
+        x0 = 768 * t
+        tag = {}
+        now[0] = t
+        times.clear()
+        dst = T.cores[(rank + 1 + t % (len(T.cores) - 1)) % len(T.cores)]
+        for lo, hi in C_CUTS:
+            move(ON["c"], at("cU", (lo, hi)), ind(swin, at("sU", (lo // 16, hi // 16))))
+        for lo, hi in E_CUTS:
+            plus(ON["sF"], at("sF", (lo // 16, hi // 16)), at("sU", (lo // 16, hi // 16)), -2048.0)
+            plus(ON["cF"], at("cF", (lo, hi)), at("cU", (lo, hi)), -2048.0)
+        for ch, (lo, hi) in enumerate(CHUNKS):
+            plus(G_ON[ch], at("G", (16 * lo, 16 * hi)), ind(swin, at("cU", (lo, hi))), -2048.0)
+            tag["G%d" % ch] = len(ops) - 1
+        for lo, hi in E_CUTS:
+            E = at("b4", (lo, hi))
+            mms([(E, Id32, at("cF", (lo, hi))), (E, at("accB"), at("con", 0, (lo, hi)))] +
+                [(at("b4", (lo + r, hi, 16)), at("ER", r), at("sF", (lo // 16, hi // 16))) for r in range(16)])
+            mms([(at("b5", (lo // 32, hi // 32)), IdK, at("cF", (lo, hi)))])
+
+        def chunk(ch):
+            lo, hi = CHUNKS[ch]
+            a, b, nb = 16 * lo, 16 * hi, (hi - lo) // 32
+            bank = "b%d" % (ch % 2)
+            oa, ob = at("AB", (2 * lo, lo + hi)), at("AB", (lo + hi, 2 * hi))
+            ca = [(at(bank, (0, nb)), at("DA", k), at("G", (a + k, b, 16))) for k in range(16)]
+            cb = [(at(bank, (nb, 2 * nb)), at("DB", k), at("G", (a + k, b, 16))) for k in range(16)]
+            if ch in SPLIT_AB:
+                other = "b%d" % ((ch + 1) % 2)
+                cb = [(at(other, (nb, 2 * nb)), c[1], c[2]) for c in cb]
+                mms(ca)
+                plus(AB_ON[ch], oa, at(bank, (0, nb)), 2048.0)
+                mms(cb)
+                plus(AB_ON[ch], ob, at(other, (nb, 2 * nb)), 2048.0)
+            else:
+                mms(ca)
+                mms(cb)
+                plus(AB_ON[ch], at("AB", (2 * lo, 2 * hi)), at(bank, (0, 2 * nb)), 2048.0)
+            act(at("Xa", (a, b)), ind(xwin, oa), F.Copy)
+            tag["a%d" % ch] = len(ops) - 1
+            tt(at(D, (a, b)), ind(xwin, ob), at("Xa", (a, b)), A.subtract)
+            tag["d%d" % ch] = len(ops) - 1
+            gi = [i for i in range(len(PARTS)) if PARTS[i][0] <= lo < PARTS[i][1]][0]
+            uo = at(U_BANK[gi], ((lo - PARTS[gi][0]) // 32, (hi - PARTS[gi][0]) // 32))
+            pre = [(uo, Id, at("con", 1, (lo, hi)))]
+            wu = [(uo, at("WU", k), at(Z, (a + k, b, 16))) for k in range(16)]
+            if ABS_ON[ch] == "V":
+                ts(at(Z, (a, b)), at(D, (a, b)), 0.0, A.max, 2.0, A.mult)
+                pre += [(uo, at("WN", k), at(D, (a + k, b, 16))) for k in range(16)]
+            else:
+                act(at(Z, (a, b)), at(D, (a, b)), F.Abs)
+            tag["z%d" % ch] = len(ops) - 1
+            if lo == PARTS[gi][0]:
+                mms(pre, True, False)
+                ops[-1]["r"].append(at(U_BANK[gi], (nb, 16) if hi < PARTS[gi][1] or gi else (nb, nb + 1))["acc"])
+                mms(wu, False, True)
+            else:
+                mms(pre + wu)
+
+        def claims(gi):
+            lo, hi = PARTS[gi]
+            q0, q1, b0, b1, nb, m = lo // 16, hi // 16, lo // 32, hi // 32, (hi - lo) // 32, (hi - lo) // 16
+            Qt, JU, cs = "Qt%d" % gi, "JU%d" % gi, "cs%d" % gi
+            h = lambda nm: at(nm, (lo, hi))
+            q = lambda nm: at(nm, (q0, q1))
+            qt = lambda j, k=1: at(Qt, (j * nb, (j + k) * nb))
+            L = lambda j, k=1: at("L", (j, j + k), (q0, q1))
+            y = at(U_BANK[gi], (0, nb))
+            move(ON["rq"], h("rq"), y)
+            tt(y, y, h("rq"), A.subtract)
+            act(h("sq"), y, F.Square, scale=4096.0, bias=c16)
+            tt(h("tt"), h("sq"), h("b4"), A.add)
+            ts(h("tb"), h("tt"), 480, A.bitwise_and)
+            if ON["Fc"] == "V":
+                ts(h("Fc"), h("tb"), 0.0, A.is_equal)
+            else:
+                act(h("Fc"), h("tb"), F.Relu, scale=-1.0, bias=1.0)
+            s1, s2 = at("b0", (4 + b0, 4 + b1)), at("b1", (4 + b0, 4 + b1))
+            mms([(s1, at("CN2"), h("Fc"))])
+            mms([(s2, at("CN2"), h("Fc"))])
+            act(qt(4), s1, F.Relu, scale=-4096.0, bias=cm99)
+            ts(qt(5), s2, -99.0, A.is_equal, 4096.0, A.mult)
+            act(qt(7), y, F.Copy, scale=row0)
+            s3 = at("b5", (8 + b0, 8 + b1))
+            mms([(s3, Id, h("cF")), (s3, Id, at("c47", (lo, hi))), (s3, at("CN1"), h("Fc"))])
+            ts(qt(2), s3, 0.0, A.max, -2048.0, A.add)
+            tt(qt(3), qt(5), at("b5", (b0, b1)), A.mult)
+            tt(qt(8), qt(4), y, A.mult)
+            act(qt(0, 2), qt(4, 2), F.Copy, scale=kfr)
+            act(qt(6), qt(4), F.Copy, scale=1.0 / 4096)
+            R, w, ub = at("b4", (256 + lo, 256 + hi)), hi - lo, U_BANK[gi]
+            mms([(R, BM, qt(2))])
+            B0, B1 = at("b7", (b0, b1)), at("b7", (8 + b0, 8 + b1))
+            mms([(B0, Id, h("RM"))] + [(at("b7", (b0, b1), a), at("PM", 2 * a + b), at(Qt, (2 * nb, 3 * nb), b)) for a in range(2) for b in range(2)] +
+                [(at("b7", (8 + b0, 8 + b1), a), at("PM", 2 * a + 1), at(Qt, (2 * nb, 3 * nb), 0)) for a in range(2)])
+            mms([(at(ub, (nb + b * nb // 2, nb + (b + 1) * nb // 2), a), at("PF", a), at(Qt, (2 * nb, 3 * nb, 2), b)) for b in range(2) for a in range(2)])
+            mms([(L(0, NT), Id, at("JC", (0, NT), (q0, q1))), (L(7), Id5, q("sF")), (L(2), IdN, at("on", (0, m)))] +
+                [(L(0, NT), at("LR", r), at(Qt, (0, NT * nb), (0, 2), r)) for r in range(16)])
+            ch = at("ch", (0, 2), (q0, q1))
+            plus(ON["ch"], ch, at("L", (2, 5, 2), (q0, q1)), -2048.0)
+            RT = at("RT", (lo // 64, hi // 64))
+            add("V", lambda e: e.transpose(val(RT), val(R)), time("V", RT, R, 1), [RT], [R])
+            e0 = 3 * lo
+            tt(at("eq", (e0, e0 + 2 * w, 2)), RT, B0, A.is_equal)
+            tt(at("eq", (e0 + 1, e0 + 2 * w, 2)), RT, B1, A.is_equal)
+            for b in range(2):
+                tt(at("eq", (e0 + 2 * w + b, e0 + 3 * w, 2)), at("RT", (lo // 64, hi // 64), 1), at(ub, (nb + b * nb // 2, nb + (b + 1) * nb // 2)), A.is_equal)
+            lose, eq, rs = at("lose", (e0, e0 + 3 * w)), at("eq", (e0, e0 + 3 * w)), at("RS", (0, 3 * w))
+            add("V", lambda e: e.tensor_tensor_scan(val(lose), val(rs), val(eq), 0.0, A.mult, A.max), time("V", lose, lose, 0.5), [lose], [rs, eq])
+            mms([(L(NT), Id, at("ch", 0, (q0, q1))), (L(NT), IdT, at("ch", 1, (q0, q1))), (L(NT), Id, at("con", 3, (0, m)))] +
+                [(at("L", NT, (q0 + a, q1, 2)), at("UK", 2 * a + b), at("lose", (e0 + 32 * b + 31, e0 + 2 * w, 64))) for a in range(2) for b in range(2)] +
+                [(at("L", NT, (q0 + 2 + a, q1, 4)), at("UK", 2 * a + b), at("lose", (e0 + 2 * w + 32 * b + 31, e0 + 3 * w, 64))) for a in range(2) for b in range(2)])
+            if TT_U16:
+                tt(q("posU"), L(NT), q("dump"), A.min)
+            else:
+                tt(q("pos"), L(NT), q("dump"), A.min)
+                move(ON["pos"], q("posU"), q("pos"))
+            if ON["JU"] == "S":
+                act(at(JU), L(0, 3), F.Relu)
+            else:
+                cp(at(JU), L(0, 3))
+            tt(at("hm", (0, 3), (q0, q1)), L(4, 3), at("KT", (0, 3), (q0, q1)), A.mult)
+            tt(at(cs, (2 * t, 2 * t + 2)), L(2, 2), at("hm", (0, 2), (q0, q1)), A.add)
+            send(at("rcv", t, (q0, q1)), at(cs, 2 * t + 1), "n%d_%d" % (t, gi), dst)
+            tt(q("m0"), L(7), at(cs, 2 * t), A.max)
+            move(OLD_ON, h("old"), ind(swin, at(JU, (2 * m, 3 * m))))
+            tt(h("nc"), h("old"), qt(8), A.add)
+            ts(h("nd"), h("nc"), 4095, A.bitwise_and)
+            act(h("z1"), ind(at(D), at(JU, (0, m))), F.Abs)
+            act(h("z2"), ind(at(D), at(JU, (m, 2 * m))), F.Abs)
+            move(ON["yi"], q("yi"), L(8))
+            ts(q("y7"), q("yi"), 7, A.bitwise_and)
+            if TT_U16:
+                tt(q("WLU"), q("y7"), at("hm", 2, (q0, q1)), A.add)
+            else:
+                tt(q("w2"), q("y7"), at("hm", 2, (q0, q1)), A.add)
+                move(ON["WLU"], q("WLU"), q("w2"))
+
+        for ch in range(len(CHUNKS)):
+            chunk(ch)
+        for gi in range(len(PARTS)):
+            tag["c%d" % gi] = len(ops)
+            claims(gi)
+        for names in TURNS:
+            for a, b in zip(names, names[1:]):
+                ops[tag[b]]["after"].append((tag[a], 0.0))
+        for j in range(3, -1, -1):
+            cp(ind(at("Si"), at("posU", (4 * j, 4 * j + 4))), at("nd", (64 * j, 64 * j + 64)))
+        for lo, hi in PARTS:
+            w = at("WLU", (lo // 16, hi // 16))
+            cp(ind(at("XX", (0, 6144)), w), at("z1", (lo, hi)))
+            if not last and X_COPY == "V":
+                cp(ind(at("XX", (2048, 8192)), w), at("z1", (lo, hi)))
+        if last:
+            dma("Y", T.yv[:], at("XX", (0, 2048)))
+        elif X_COPY == "Y":
+            dma("Y", at("XX", (2048, 4096)), at("XX", (0, 2048)))
+        for lo, hi in PARTS:
+            q = lambda nm: at(nm, (lo // 16, hi // 16))
+            tt(q("m1"), q("m0"), at("rcv", t, (lo // 16, hi // 16)), A.max)
+            ts(q("sL"), q("m1"), 4095, A.bitwise_and)
+            if not last:
+                move(ON["sU"], q("sU"), q("sL"))
+        if last:
+            cp(at("yso"), at("sL"))
+            dma("Y", T.ys[:], at("yso"))
         else:
-            dma("Y", T.yv[:], T.XX[:, XR:XR + 2048], 3.0, [xr], [])
-        sN = "sL%d" % (t + 1)
-        V(tt(pf("m1"), pf("m0"), T["rcv" + n][:], A.max), 16, ["m0", "rcv" + n], ["m1"])
-        V(ts(pf(sN), pf("m1"), 4095, None, A.bitwise_and), 16, ["m1"], [sN])
-        if t + 1 < STEPS:
-            V(cp(pf("sU%d" % (t + 1)), pf(sN)), 16, [sN], ["sU%d" % (t + 1)])
+            act(at("jk"), at("L", 5), F.Copy, acc=acc, scale=1.0 / 4096)
+            act(at("accB"), on, F.Identity, scale=0.0625, bias=acc)
+        xo, yh = at("XC", (x0, x0 + 256)), at("b3", (8, 16))
+        mms([(yh, Id, at("z2")), (yh, IdN, xo)])
+        act(at("Y", t), yh, F.Abs)
+        send(at("XC", (x0 + 256, x0 + 512)), at("Y", t), "x%d" % t, dst)
+        mms([(yh, IdH, at("z1")), (yh, IdH, xo), (yh, IdH, at("con", 2))])
+        xh = at("XC", (x0 + 512, x0 + 768))
+        if HALF_ON == "V":
+            ts(xh, yh, MAGIC, A.add, -MAGIC, A.add)
         else:
-            V(cp(T.yso[:], pf(sN)), 16, [sN], ["yso"])
-            dma("Y", T.ys[:], T.yso[:], 2.0, ["yso"], [])
-        yr = ("qc", 256, 512)
-        P(mms([(T.qc[:, 256:512], T.Id[:], T.z2[:], True, False), (T.qc[:, 256:512], T.IdN[:], XC[:, 0:256], False, True)]), 512,
-          ["Id", "IdN", "z2", (XCn, 0, 256)], [yr])
-        S(act(T["Y" + n][:], T.qc[:, 256:512], F.Abs), 256, [yr], ["Y" + n])
-        add("G", lambda e: e.remote_dma(XC[:, XCY:XCY + 256], T["Y" + n][:], T.sem["ax" + n], T.sem["lx" + n], pid, rid, mask), 1.0,
-            ["Y" + n], [], "send", "ax" + n, len(eng))
-        add("N", None, EST["net"], ["Y" + n], [(XCn, XCY, XCY + 256)], "recv", "ax" + n, len(eng))
-        P(mms([(T.kr[:, 256:512], T.Id[:], z1[:], True, False), (T.kr[:, 256:512], T.Id[:], XC[:, 0:256], False, False),
-               (T.kr[:, 256:512], T.Id[:], T.mhalf[:], False, True)]), 768, ["Id", z1n, (XCn, 0, 256), "mhalf"], [("kr", 256, 512)])
-        S(act(pf("ha"), T.kr[:, 256:512], F.Identity, bias=MAGIC, scale=0.5), 256, [("kr", 256, 512)], ["ha"])
-        S(act(XC[:, XCH:XCH + 256], pf("ha"), F.Identity, bias=-MAGIC), 256, ["ha"], [(XCn, XCH, XCH + 256)])
-        V(ts(pf("cm"), T["rcv" + n][:], 4096.0, None, A.min), 16, ["rcv" + n], ["cm"])
-        V(tt(pf("xm"), pf("cm"), pf("hm"), A.max), 16, ["cm", "hm"], ["xm"])
-        V(tt(pf("xi"), pf("xm"), pf("I16"), A.add), 16, ["xm", "I16"], ["xi"])
-        V(ts(pf("XLU"), pf("xi"), 0.0625, None, A.mult), 16, ["xi"], ["XLU"])
-        nx = "XC%d" % (t + 1)
-        S(act(T[nx][:, 0:256], XC[:].indirect(pf("XLU")), F.Copy), GA * 256, [XCn, "XLU"], [(nx, 0, 256)])
-        if t + 1 == STEPS:
-            dma("Y", T.yx[:], T[nx][:, 0:256], 2.0, [(nx, 0, 256)], [])
+            act(at("ha"), yh, F.Identity, bias=MAGIC)
+            act(xh, at("ha"), F.Identity, bias=-MAGIC)
+        ts(at("xt"), at("m1"), 7, A.arith_shift_right, 768, A.bitwise_and)
+        if TT_U16:
+            tt(at("XLU"), at("xt"), at("Ic"), A.add)
+        else:
+            tt(at("xi"), at("xt"), at("Ic"), A.add)
+            move(ON["XLU"], at("XLU"), at("xi"))
+        xn = at("XC", (x0 + 768, x0 + 1024))
+        act(xn, ind(at("XC", (x0, x0 + 768)), at("XLU")), F.Copy)
+        if last:
+            dma("Y", T.yx[:], xn)
 
     for t in range(STEPS):
         step(t)
 
+    yt = at("b0", (0, 8))
     for j in range(0, 16, 2):
         a = 256 * j
-        r, w = [("Sw", a, a + 512)], [("S16", a, a + 512)]
-        if j % 4 == 0:
-            V(ts(T.S16[:, a:a + 512], T.Sw[:, a:a + 512], -2048.0, None, A.add), 512, r, w)
-        else:
-            S(act(T.S16[:, a:a + 512], T.Sw[:, a:a + 512], F.Identity, bias=-2048.0), 512, r, w)
-        P(mms([(T.ab0[:, 0:256], T.Id[:], T.S16[:, 256 * k:256 * k + 256], k == 0, k == 15) for k in (j, j + 1)]), 512,
-          ["Id", ("S16", a, a + 512), ("ab0", 0, 256)], [("ab0", 0, 256)])
-    V(ts(pf("yto"), T.ab0[:, 0:256], 32768.0, None, A.add), 256, [("ab0", 0, 256)], ["yto"])
-    dma("Y", T.yt[:], pf("yto"), 2.0, ["yto"], [])
+        plus("VS"[j // 2 % 2], at("S16", (a, a + 512)), at("Si", (a, a + 512)), -2048.0)
+        mms([(yt, Id, at("S16", (256 * k, 256 * k + 256))) for k in (j, j + 1)], j == 0, j == 14)
+    ts(at("yto"), yt, 32768.0, A.add)
+    dma("Y", T.yt[:], at("yto"))
 
 
 def depends(ops):
@@ -472,72 +520,267 @@ def depends(ops):
     for i, o in enumerate(ops):
         d = set()
         acc = [(x, False) for x in o["r"]] + [(x, True) for x in o["w"]]
-        for (b, lo, hi), wr in acc:
-            for (j, l2, h2, w2) in seen.get(b, ()):
-                if (wr or w2) and lo < h2 and l2 < hi:
+        for (b, m), wr in acc:
+            for (j, m2, w2) in seen.get(b, ()):
+                if (wr or w2) and m & m2:
                     d.add(j)
-                elif b in PSUMS and ops[j]["q"] != o["q"]:
-                    d.add(j)
-        for (b, lo, hi), wr in acc:
+        for (b, m), wr in acc:
             lst = seen.setdefault(b, [])
-            if wr and b not in PSUMS:
-                lst[:] = [x for x in lst if not (lo <= x[1] and x[2] <= hi)]
-            lst.append((i, lo, hi, wr))
-            if b in PSUMS and len(lst) > 60:
-                del lst[:len(lst) - 60]
+            if wr:
+                lst[:] = [x for x in lst if x[1] & ~m]
+            lst.append((i, m, wr))
         d.discard(i)
-        o["d"] = sorted(d)
+        o["d"] = d
 
 
 def schedule(ops):
     wake = EST["wake"]
     n = len(ops)
+    dur = [o["dur"] for o in ops]
+    pred = [[(j, wake) for j in sorted(o["d"])] + o["after"] for o in ops]
     succ = [[] for _ in range(n)]
-    need = [0] * n
-    for i, o in enumerate(ops):
-        for j in o["d"]:
-            succ[j].append(i)
-        need[i] = len(o["d"])
-    prio = [0.0] * n
-    for i in range(n - 1, -1, -1):
-        best = 0.0
-        for k in succ[i]:
-            best = max(best, prio[k] + wake)
-        prio[i] = best + ops[i]["dur"]
     for i in range(n):
-        prio[i] += BOOST.get(ops[i]["cls"], 0.0)
-    free = {}
-    ready = [(0.0, i) for i in range(n) if need[i] == 0]
-    end = [0.0] * n
-    at = [0.0] * n
-    order = []
-    while ready:
-        cand = [(max(r, free.get(ops[i]["q"], 0.0)), -prio[i], i) for r, i in ready]
-        s0 = min(cand)[0]
-        s, _, i = min([c for c in cand if c[0] <= s0 + LOOK], key=lambda c: c[1])
-        ready = [x for x in ready if x[1] != i]
-        o = ops[i]
-        end[i] = s + o["dur"]
-        at[i] = s
-        if o["kind"] == "dma":
-            free[o["q"]] = s + 0.1
-        elif o["kind"] != "recv":
-            free[o["q"]] = end[i]
-        order.append(i)
-        for k in succ[i]:
-            need[k] -= 1
-            if need[k] == 0:
-                ready.append((max([end[j] + wake for j in ops[k]["d"]]), k))
-    return order, max(end), at, end
+        for j, lag in pred[i]:
+            succ[j].append((i, lag))
+
+    def place(before, after, key, back):
+        need = [len(p) for p in before]
+        ready = [i for i in range(n) if need[i] == 0]
+        at, busy = [0.0] * n, {}
+        while ready:
+            i = min(ready, key=lambda x: key[x])
+            ready.remove(i)
+            o, d = ops[i], dur[i]
+            s = max([at[j] + dur[j] + lag for j, lag in before[i]] + [0.0])
+            hold = (d - 0.1 if back else 0.0, d if back else 0.1) if o["kind"] == "dma" else (0.0, d)
+            res = [(o["q"], None, hold[0], hold[1])] if o["kind"] != "recv" else []
+            res += [(b, o["q"], -wake, d + wake) for b in o["banks"]]
+            moved = True
+            while moved:
+                moved = False
+                for r, own, a, b in res:
+                    lst = busy.get(r, ())
+                    k = len(lst) - 1
+                    while k >= 0 and lst[k][0] > s - 4.0:
+                        x = lst[k]
+                        if x[2] != own or own is None:
+                            if x[0] < s + b - 1e-9 and s + a < x[1] - 1e-9:
+                                s, moved = x[1] - a, True
+                                break
+                        k -= 1
+            at[i] = s
+            for r, own, a, b in res:
+                lst = busy.setdefault(r, [])
+                lst.append((s, s + d, own) if own else (s + a, s + b, None))
+                k = len(lst) - 1
+                while k > 0 and lst[k - 1][0] > lst[k][0]:
+                    lst[k - 1], lst[k] = lst[k], lst[k - 1]
+                    k -= 1
+            for k, lag in after[i]:
+                need[k] -= 1
+                if need[k] == 0:
+                    ready.append(k)
+        return at, max(at[i] + dur[i] for i in range(n))
+
+    key = [0.0] * n
+    for sweep in range(4):
+        for i in range(n - 1, -1, -1):
+            key[i] = -dur[i] + min([key[k] - lag for k, lag in succ[i]] + [0.0])
+    rng = np.random.default_rng(1)
+    best = None
+    for it in range(ROUNDS):
+        at, total = place(pred, succ, key, False)
+        if best is None or total < best[1]:
+            best = (at, total)
+        base = best[0] if it % 3 == 2 else at
+        jit = rng.random(n) * (JITTER if it % 3 == 2 else 0.0)
+        back = place(succ, pred, [-(base[i] + dur[i]) + float(jit[i]) for i in range(n)], True)[0]
+        key = [-(back[i] + dur[i]) for i in range(n)]
+    at = best[0]
+    return sorted(range(n), key=lambda i: (at[i], i))
+
+
+def improve(ops, order, cases):
+    n = len(ops)
+    names = sorted(set(o["q"] for o in ops) | set(b for o in ops for b in o["banks"]))
+    queue = [names.index(o["q"]) if o["kind"] != "recv" else -1 for o in ops]
+    banks = [[names.index(b) for b in sorted(o["banks"])] for o in ops]
+    pred = [sorted(o["d"]) for o in ops]
+    hard = [o["hard"] for o in ops]
+    allp = [set(pred[i]) | set(hard[i]) for i in range(n)]
+    isdma = [o["kind"] == "dma" for o in ops]
+
+    def run(order, dur, wake):
+        end, why = [0.0] * n, [-1] * n
+        free, last = [0.0] * len(names), [-1] * len(names)
+        user = [[] for _ in names]
+        issued = [0.0] * n
+        for i in order:
+            s, w = 0.0, -1
+            for j in pred[i]:
+                if end[j] > s:
+                    s, w = end[j], j
+            if w >= 0:
+                s += wake
+            for j in hard[i]:
+                if issued[j] > s:
+                    s, w = issued[j], j
+            q = queue[i]
+            if q >= 0 and free[q] > s:
+                s, w = free[q], -2 - last[q]
+            for b in banks[i]:
+                u = user[b]
+                keep = [i]
+                for j in u:
+                    if queue[j] != q:
+                        keep.append(j)
+                        if end[j] + wake > s:
+                            s, w = end[j] + wake, -2 - j
+                user[b] = keep
+            e = s + dur[i]
+            end[i], why[i] = e, w
+            issued[i] = s + 0.1 if isdma[i] else e
+            if q >= 0:
+                free[q], last[q] = issued[i], i
+        i = max(range(n), key=lambda x: end[x])
+        total, held = end[i] + EARLY * sum(end) / n, []
+        while why[i] != -1:
+            j = why[i] if why[i] >= 0 else -2 - why[i]
+            if why[i] < 0:
+                held.append((j, i))
+            i = j
+        return total, held, why, end
+
+    rng = np.random.default_rng(2)
+    slots = {}
+    slot = [slots.setdefault(o["slot"], len(slots)) for o in ops]
+    base = [PERIOD * o["step"] for o in ops]
+    end = run(order, *cases[0])[3]
+    first = [min(end[i] for i in range(n) if ops[i]["step"] == t and ops[i]["banks"]) for t in range(STEPS)]
+    key = [0.0] * len(slots)
+    for t in (3, 0, 2, 1):
+        for i in range(n):
+            if ops[i]["step"] == t:
+                key[slot[i]] = end[i] - cases[0][0][i] - first[t]
+    plist = [sorted(x) for x in allp]
+
+    def arrange(key):
+        full = [base[i] + key[slot[i]] for i in range(n)]
+        seen, out = [False] * n, []
+        for i in sorted(range(n), key=lambda x: full[x]):
+            stack = [i]
+            while stack:
+                x = stack[-1]
+                if seen[x]:
+                    stack.pop()
+                    continue
+                todo = [j for j in plist[x] if not seen[j]]
+                if todo:
+                    stack += sorted(todo, key=lambda y: -full[y])
+                else:
+                    seen[x] = True
+                    out.append(x)
+                    stack.pop()
+        return out, full
+
+    order, full = arrange(key)
+    now = [run(order, d, w) for d, w in cases]
+    cost = sum(x[0] for x in now)
+    best = (cost, order)
+    for it in range(SHIFTS):
+        held, why = now[int(rng.integers(len(cases)))][1:3]
+        new = list(key)
+        for rep in range(1 + int(rng.random() < 0.3)):
+            if held and rng.random() < 0.6:
+                j, i = held[int(rng.integers(len(held)))]
+            else:
+                i = int(rng.integers(n))
+                j = -2 - why[i] if why[i] < -1 else i
+            step = float(rng.random()) ** 2 * 2.0 + 0.001
+            if rng.random() < 0.6:
+                new[slot[i]] = full[j] - base[i] - step
+            else:
+                new[slot[j]] = full[i] - base[j] + step
+        trial, f2 = arrange(new)
+        res = [run(trial, d, w) for d, w in cases]
+        c = sum(x[0] for x in res)
+        if c <= cost + MARGIN * (1 - it / SHIFTS) * float(rng.random()):
+            key, full, now, cost = new, f2, res, c
+            if c < best[0]:
+                best = (c, trial)
+    order = best[1]
+    now = [run(order, d, w) for d, w in cases]
+    cost = sum(x[0] for x in now)
+    best = (cost, order)
+    for it in range(MOVES):
+        held, why = now[int(rng.integers(len(cases)))][1:3]
+        if held and rng.random() < 0.6:
+            j, i = held[int(rng.integers(len(held)))]
+        else:
+            i = int(rng.integers(n))
+            j = -2 - why[i]
+            if j < 0:
+                continue
+        a, b = order.index(j), order.index(i)
+        for hop in range(int(rng.integers(3))):
+            k = a - 1
+            while k >= 0 and queue[order[k]] != queue[j]:
+                k -= 1
+            if k >= 0:
+                a, j = k, order[k]
+        mid = order[a:b + 1]
+        if rng.random() < 0.5:
+            take = {i}
+            for x in reversed(mid):
+                if x in take:
+                    take |= allp[x]
+            if j in take:
+                continue
+            mid = [x for x in mid if x in take] + [x for x in mid if x not in take]
+        else:
+            take = {j}
+            for x in mid[1:]:
+                if allp[x] & take:
+                    take.add(x)
+            if i in take:
+                continue
+            mid = [x for x in mid if x not in take] + [x for x in mid if x in take]
+        trial = order[:a] + mid + order[b + 1:]
+        new = [run(trial, d, w) for d, w in cases]
+        c = sum(x[0] for x in new)
+        if c <= cost + MARGIN * (1 - it / MOVES) * float(rng.random()):
+            order, now, cost = trial, new, c
+            if c < best[0]:
+                best = (c, trial)
+    order = best[1]
+    extra, users = [], {}
+    for i in order:
+        for b in sorted(ops[i]["banks"]):
+            u = users.setdefault(b, {})
+            extra += [(i, j) for q, j in u.items() if q != ops[i]["q"]]
+            u[ops[i]["q"]] = i
+    return order, extra, best[0] / len(cases)
+
+
+PLAN = {}
 
 
 def rank_program(g, core, T, topo):
     if T.rank_of(core) is None:
         return
     ops = []
-    build(core, T, topo, ops)
+    build(core, T, topo, ops, EST)
     depends(ops)
-    order = schedule(ops)[0]
+    if "order" not in PLAN:
+        cases = []
+        for c in CASES:
+            other = []
+            build(core, T, topo, other, dict(EST, **c))
+            cases.append(([o["dur"] for o in other], dict(EST, **c)["wake"]))
+        PLAN["order"] = improve(ops, schedule(ops), cases)
+    order = PLAN["order"][0]
+    for i, j in PLAN["order"][1]:
+        ops[i]["d"].add(j)
     eng = {"V": g.vector, "S": g.scalar, "P": g.tensor, "G": g, "Y": g.sync}
     know = {}
     for q in eng:
@@ -567,7 +810,7 @@ def rank_program(g, core, T, topo):
                 continue
             s, c = token[j]
             want[s] = max(want.get(s, 0), c)
-        for s in sorted(want, key=lambda s: -sum(clock.get((s, want[s]), {}).values())):
+        for s in sorted(want, key=lambda s: (-sum(clock.get((s, want[s]), {}).values()), s)):
             if know[q].get(s, 0) < want[s]:
                 e.wait_ge(T.sem[s], want[s])
                 learn(q, (s, want[s]))

@@ -5,12 +5,16 @@ STEPS = 4
 CHUNKS = ((192, 256), (128, 192), (64, 128), (0, 64))
 PARTS = ((128, 256), (0, 128))
 U_BANK = ("b2", "b3")
-TURNS = (("G0", "a0", "a1", "G2", "G3", "a2", "a3", "z2"), ("G1", "d0", "z0", "d1", "z1", "d2", "d3", "z3"))
-G_ON = "SVSS"
+TURNS = (("G1", "G3"), ("a0", "a1", "a2", "a3"), ("G0", "G2"), ("d0", "d1", "d2", "d3"))
+G_ON = "VSVS"
 ABS_ON = "VVSV"
-AB_ON = "SSVV"
+AB_ON = "VVVV"
 C_CUTS = ((128, 256), (0, 128))
-E_CUTS = ((128, 256), (0, 128))
+E_CUTS = ((0, 256),)
+X_CUTS = ((128, 256), (0, 128))
+G_SUB = (1, 1, 1, 1)
+X_SUB = (1, 1, 1, 1)
+Z_SUB = (1, 1, 1, 1)
 OLD_ON = "S"
 HALF_ON = "V"
 ON = {"rq": "S", "Fc": "V", "c": "S", "cF": "S", "sF": "S", "JU": "S", "yi": "S", "WLU": "S", "XLU": "S", "sU": "V", "ch": "S", "pos": "V"}
@@ -28,13 +32,13 @@ SCRATCH = {
     "Xa": ("sbuf", [128, 4096], "bfloat16"),
     "S16": ("sbuf", [128, 4096], "float16"),
     "AB": ("sbuf", [128, 512], "uint16"),
-    "on": ("sbuf", [128, 2048], "bfloat16"),
-    "DA": ("sbuf", [128, 16, 8, 16], "bfloat16"),
-    "DB": ("sbuf", [128, 16, 128], "bfloat16"),
+    "on": ("sbuf", [128, 256], "bfloat16"),
+    "SEL": ("sbuf", [128, 16, 2, 8], "bfloat16"),
+    "GT": ("sbuf", [128, 512], "float16"),
+    "yT": ("sbuf", [128, 256], "float16"),
     "ER": ("sbuf", [128, 16, 128], "bfloat16"),
     "LR": ("sbuf", [128, 16, 8, 16], "bfloat16"),
-    "WU": ("sbuf", [128, 16, 8, 16], "bfloat16"),
-    "WN": ("sbuf", [128, 16, 8, 16], "bfloat16"),
+    "WG": ("sbuf", [128, 2, 8], "bfloat16"),
     "PM": ("sbuf", [128, 4, 4, 32], "bfloat16"),
     "PF": ("sbuf", [128, 2, 128], "bfloat16"),
     "UK": ("sbuf", [128, 4, 4, 32], "bfloat16"),
@@ -45,7 +49,8 @@ SCRATCH = {
     "CNT": ("sbuf", [128, 128], "bfloat16"),
     "CN2": ("sbuf", [128, 128], "bfloat16"),
     "mat": ("sbuf", [128, 8, 128], "bfloat16"),
-    "con": ("sbuf", [128, 4, 256], "bfloat16"),
+    "hi": ("sbuf", [128, 512], "bfloat16"),
+    "con": ("sbuf", [128, 5, 256], "bfloat16"),
     "RM": ("sbuf", [128, 256], "bfloat16"),
     "RS": ("sbuf", [128, 768], "bfloat16"),
     "r256": ("sbuf", [128, 256], "float32"),
@@ -120,15 +125,23 @@ for _t in range(STEPS):
     for _g in range(len(PARTS)):
         SEMAPHORES += ["an%d_%d" % (_t, _g), "ln%d_%d" % (_t, _g)]
 
-EST = {"cyc": 0.00083 * 1.1, "V": 0.02, "S": 0.03, "ind": 0.04, "ga": 1.25, "sc": 3.3, "pe": 0.0005, "wake": 0.18, "net": 2.5, "dma": 1.5, "rate": 350e3}
-CASES = ({}, {"net": 4.0, "pe": 0.0007, "wake": 0.2})
+EST = {"cyc": 0.00083 * 1.08, "V": 0.02, "S": 0.04, "ind": 0.03, "ga": 1.3, "sc": 3.5, "pe": 0.00075, "wake": 0.14, "net": 2.5, "dma": 1.3, "rate": 350e3}
+CASES = ({}, {"net": 3.5, "pe": 0.0005, "wake": 0.12, "ga": 1.5})
 JITTER = 0.5
-SHIFTS = 7000
+REACH = 0.5
+SEED = 1
+SHIFTS = 3000
 PERIOD = 21.0
-MOVES = 2000
+MOVES = 1000
 MARGIN = 0.6
 EARLY = 0.3
+COLUMNS = {}
 SIZE = {"float32": 4, "int32": 4, "bfloat16": 2, "float16": 2, "uint16": 2}
+
+
+def pieces(lo, hi, k):
+    w = (hi - lo) // k
+    return [(hi - w * (j + 1), hi - w * j) for j in range(k)]
 
 
 def build(core, T, topo, ops, EST):
@@ -138,15 +151,14 @@ def build(core, T, topo, ops, EST):
 
     def at(name, *idx):
         where, shape, dt = SCRATCH[name]
-        if name not in cols:
-            cols[name] = np.arange(int(np.prod(shape[1:]))).reshape(shape[1:])
-        idx = tuple(slice(*i) if isinstance(i, tuple) else i for i in idx)
-        c = cols[name][idx].reshape(-1)
-        bits = np.zeros(cols[name].size, np.uint8)
-        bits[c] = 1
-        m = int.from_bytes(np.packbits(bits, bitorder="little").tobytes(), "little")
-        ap = T[name][(slice(None),) + idx] if idx else T[name][:]
-        return {"ap": ap, "acc": (name, m), "n": int(c.size), "two": SIZE[dt] == 2, "ps": where == "psum", "off": None, "bytes": 128 * int(c.size) * SIZE[dt]}
+        cut = tuple(slice(*i) if isinstance(i, tuple) else i for i in idx)
+        if (name, idx) not in COLUMNS:
+            bits = np.zeros(shape[1:], np.uint8)
+            bits[cut] = 1
+            COLUMNS[(name, idx)] = (int.from_bytes(np.packbits(bits, bitorder="little").tobytes(), "little"), int(bits.sum()))
+        m, k = COLUMNS[(name, idx)]
+        ap = T[name][(slice(None),) + cut] if idx else T[name][:]
+        return {"ap": ap, "acc": (name, m), "n": k, "two": SIZE[dt] == 2, "ps": where == "psum", "off": None, "bytes": 128 * k * SIZE[dt]}
 
     def ind(win, off):
         return dict(win, ap=win["ap"].indirect(off["ap"]), n=16 * off["n"], off=off["acc"])
@@ -245,9 +257,10 @@ def build(core, T, topo, ops, EST):
     dma("Y", at("Si", (0, 4096)), T.stm[:])
     dma("Y", at("wI"), T.wt[:], 6.0)
     dma("Y", at("XX", (0, 2048)), T.vx[:], 6.0)
-    dma("Y", at("XX", (2048, 4096)), T.vx[:], 7.5)
-    dma("Y", at("XC", (0, 256)), T.x0[:], 9.0)
-    for j in range(1, 6):
+    if X_COPY:
+        dma("Y", at("XX", (2048, 4096)), T.vx[:], 7.5)
+    dma("Y", at("XC", (0, 256)), T.x0[:], 8.0)
+    for j in range(1, len(ops)):
         ops[j]["after"].append((j - 1, 0.1 - ops[j - 1]["dur"]))
         ops[j]["hard"].append(j - 1)
 
@@ -259,11 +272,11 @@ def build(core, T, topo, ops, EST):
     iota(at("q16"), [[16, 16]], 0, allow_small_or_imprecise_dtypes=True)
     iota(at("r256"), [[0, 16], [1, 16]], 0, allow_small_or_imprecise_dtypes=True)
     asel(Id, on, [[-1, 128]], A.is_equal, 0, 1)
-    asel(at("SW"), on, [[-2, 64], [1, 2]], A.is_equal, -1, 1)
     asel(at("BI"), on, [[-16, 8], [0, 16]], A.is_ge, 0, 1)
     asel(BM, at("BI"), [[16, 8], [0, 16]], A.is_ge, 15, -1)
     asel(at("CNT"), BM, [[1, 128]], A.is_ge, -1, -1)
-    asel(at("DA"), at("on"), [[1000, 16], [-16, 8], [-1001, 16]], A.is_equal, 0, 1)
+    asel(at("SEL", (0, 16), 0), on, [[-1, 16], [-16, 8]], A.is_equal, 0, 1)
+    asel(at("SEL", (0, 16), 1), on, [[-2, 8], [1, 2], [-16, 8]], A.is_equal, -1, 1)
     ts(at("pI", (2, 3)), at("pI", (0, 1)), 15, A.bitwise_and)
     cp(kcol, at("pI", (2, 3)))
     ts(row0, kcol, 0.0, A.is_equal, 4096.0, A.mult)
@@ -274,19 +287,17 @@ def build(core, T, topo, ops, EST):
     ts(at("EQ"), at("r256", (0, 16)), kcol, A.is_equal)
     fill(at("LR"), 0.0)
     for r in range(16):
-        ts(at("DB", r), at("SW"), at("EQ", (r ^ 1, (r ^ 1) + 1)), A.mult)
         ts(at("ER", r), BM, at("EQ", (r, r + 1)), A.mult, -32.0, A.mult)
         act(at("LR", r, (0, 8), r), at("BM", (0, 4), (0, 32, 16)), F.Copy)
-    ts(at("WU"), at("LR"), wF, A.mult, 1.0 / 4096, A.mult)
-    if "V" in ABS_ON:
-        ts(at("WN"), at("LR"), wF, A.mult, -1.0 / 4096, A.mult)
+    for j in range(2):
+        ts(at("WG", j), at("BM", (0, 4), (0, 32, 16)), wF, A.mult, (1.0 - 2 * j) / 4096, A.mult)
     for m, f in ((Id32, 32.0), (IdK, 1.0 / 4096), (Id5, 5.0), (IdN, -1.0), (IdH, 0.5), (IdM, -100.0), (IdT, -2.0)):
         act(m, Id, F.Copy, scale=f)
     tt(at("CN2"), at("CNT"), IdM, A.add)
     tt(BMK, Id, at("CNT"), A.subtract)
     act(at("CN1"), BMK, F.Copy, scale=4096.0)
     act(at("c47"), at("on", (0, 256)), F.Copy, scale=-2047.0)
-    for j, c in enumerate((32.0, 1024.0, -0.5, 6144.0)):
+    for j, c in enumerate((32.0, 1024.0, -0.5, 6144.0, 393216.0)):
         fill(at("con", j), c)
     ts(at("RM"), at("r256"), kcol, A.is_ge, 0.5, A.mult)
     fill(at("RS"), 1.0)
@@ -308,7 +319,7 @@ def build(core, T, topo, ops, EST):
     act(at("accB"), on, F.Copy, scale=0.0625)
     cp(at("sU"), at("sL0"))
 
-    swin, xwin = at("Si", (0, 4096)), at("XX", (0, 4096))
+    swin, xwin = at("Si", (0, 4096)), at("XX", (0, 4096 if X_COPY else 2048))
 
     def step(t):
         last = t + 1 == STEPS
@@ -324,52 +335,52 @@ def build(core, T, topo, ops, EST):
             plus(ON["sF"], at("sF", (lo // 16, hi // 16)), at("sU", (lo // 16, hi // 16)), -2048.0)
             plus(ON["cF"], at("cF", (lo, hi)), at("cU", (lo, hi)), -2048.0)
         for ch, (lo, hi) in enumerate(CHUNKS):
-            plus(G_ON[ch], at("G", (16 * lo, 16 * hi)), ind(swin, at("cU", (lo, hi))), -2048.0)
-            tag["G%d" % ch] = len(ops) - 1
+            for j, (a, b) in enumerate(pieces(lo, hi, G_SUB[ch])):
+                plus(G_ON[ch][j % len(G_ON[ch])], at("G", (16 * a, 16 * b)), ind(swin, at("cU", (a, b))), -2048.0)
+                tag.setdefault("G%d" % ch, []).append(len(ops) - 1)
         for lo, hi in E_CUTS:
             E = at("b4", (lo, hi))
             mms([(E, Id32, at("cF", (lo, hi))), (E, at("accB"), at("con", 0, (lo, hi)))] +
                 [(at("b4", (lo + r, hi, 16)), at("ER", r), at("sF", (lo // 16, hi // 16))) for r in range(16)])
             mms([(at("b5", (lo // 32, hi // 32)), IdK, at("cF", (lo, hi)))])
 
-        def chunk(ch):
-            lo, hi = CHUNKS[ch]
-            a, b, nb = 16 * lo, 16 * hi, (hi - lo) // 32
-            bank = "b%d" % (ch % 2)
-            oa, ob = at("AB", (2 * lo, lo + hi)), at("AB", (lo + hi, 2 * hi))
-            ca = [(at(bank, (0, nb)), at("DA", k), at("G", (a + k, b, 16))) for k in range(16)]
-            cb = [(at(bank, (nb, 2 * nb)), at("DB", k), at("G", (a + k, b, 16))) for k in range(16)]
-            if ch in SPLIT_AB:
-                other = "b%d" % ((ch + 1) % 2)
-                cb = [(at(other, (nb, 2 * nb)), c[1], c[2]) for c in cb]
-                mms(ca)
-                plus(AB_ON[ch], oa, at(bank, (0, nb)), 2048.0)
-                mms(cb)
-                plus(AB_ON[ch], ob, at(other, (nb, 2 * nb)), 2048.0)
+        def gathers(gi):
+            lo, hi = PARTS[gi]
+            bank, ub, o = "b%d" % gi, U_BANK[gi], 2 * lo
+            ps, gt = at(bank, (0, 8)), at("GT", (o, o + 256))
+            mms(([] if X_COPY else [(ps, Id, at("con", 4))]) + [(at(bank, (0, 8), (0, 2), k), at("G", (16 * lo + k, 16 * hi, 16)), at("SEL", k)) for k in range(16)])
+            if X_COPY:
+                move(AB_ON[2 * gi], gt, ps)
             else:
-                mms(ca)
-                mms(cb)
-                plus(AB_ON[ch], at("AB", (2 * lo, 2 * hi)), at(bank, (0, 2 * nb)), 2048.0)
-            act(at("Xa", (a, b)), ind(xwin, oa), F.Copy)
-            tag["a%d" % ch] = len(ops) - 1
-            tt(at(D, (a, b)), ind(xwin, ob), at("Xa", (a, b)), A.subtract)
-            tag["d%d" % ch] = len(ops) - 1
-            gi = [i for i in range(len(PARTS)) if PARTS[i][0] <= lo < PARTS[i][1]][0]
-            uo = at(U_BANK[gi], ((lo - PARTS[gi][0]) // 32, (hi - PARTS[gi][0]) // 32))
-            pre = [(uo, Id, at("con", 1, (lo, hi)))]
-            wu = [(uo, at("WU", k), at(Z, (a + k, b, 16))) for k in range(16)]
-            if ABS_ON[ch] == "V":
-                ts(at(Z, (a, b)), at(D, (a, b)), 0.0, A.max, 2.0, A.mult)
-                pre += [(uo, at("WN", k), at(D, (a + k, b, 16))) for k in range(16)]
-            else:
-                act(at(Z, (a, b)), at(D, (a, b)), F.Abs)
-            tag["z%d" % ch] = len(ops) - 1
-            if lo == PARTS[gi][0]:
-                mms(pre, True, False)
-                ops[-1]["r"].append(at(U_BANK[gi], (nb, 16) if hi < PARTS[gi][1] or gi else (nb, nb + 1))["acc"])
-                mms(wu, False, True)
-            else:
-                mms(pre + wu)
+                plus(AB_ON[2 * gi], at("hi", (o, o + 256)), ps, -1023.5)
+                tt(gt, ps, at("hi", (o, o + 256)), A.subtract)
+            mms([(at(bank, (4 * j, 4 * j + 4)), at("GT", (o + 128 * j, o + 128 * j + 128)), Id) for j in range(2)])
+            plus(AB_ON[2 * gi + 1], at("AB", (o, o + 256)), ps, 2048.0 if X_COPY else 0.0)
+            mine = [ch for ch in range(len(CHUNKS)) if lo <= CHUNKS[ch][0] < hi]
+            for ch in mine:
+                for c0, c1 in pieces(CHUNKS[ch][0], CHUNKS[ch][1], X_SUB[ch]):
+                    a, b = 16 * c0, 16 * c1
+                    act(at("Xa", (a, b)), ind(xwin, at("AB", (lo + c0, lo + c1))), F.Copy)
+                    tag.setdefault("a%d" % ch, []).append(len(ops) - 1)
+                    tt(at(D, (a, b)), ind(xwin, at("AB", (hi + c0, hi + c1))), at("Xa", (a, b)), A.subtract)
+                    tag.setdefault("d%d" % ch, []).append(len(ops) - 1)
+                for c0, c1 in pieces(CHUNKS[ch][0], CHUNKS[ch][1], Z_SUB[ch]):
+                    a, b = 16 * c0, 16 * c1
+                    if ABS_ON[ch] == "V":
+                        ts(at(Z, (a, b)), at(D, (a, b)), 0.0, A.max, 2.0, A.mult)
+                    else:
+                        act(at(Z, (a, b)), at(D, (a, b)), F.Abs)
+                    tag.setdefault("z%d" % ch, []).append(len(ops) - 1)
+            relu = [CHUNKS[ch] for ch in mine if ABS_ON[ch] == "V"]
+            pre = [(at(ub, (0, 4)), Id, at("con", 1, (0, 128)))]
+            if relu:
+                c0, c1 = min(c[0] for c in relu), max(c[1] for c in relu)
+                for k in range(16):
+                    out = at(ub, (0, 4), (0, 2), k)
+                    pre.append((dict(out, ap=T[ub][c0 - lo:c1 - lo, 0:4, 0:2, k]), at(D, (16 * c0 + k, 16 * c1, 16)), at("WG", 1)))
+            mms(pre, True, False)
+            ops[-1]["r"].append(at(ub, (4, 16))["acc"])
+            mms([(at(ub, (0, 4), (0, 2), k), at(Z, (16 * lo + k, 16 * hi, 16)), at("WG", 0)) for k in range(16)], False, True)
 
         def claims(gi):
             lo, hi = PARTS[gi]
@@ -381,7 +392,8 @@ def build(core, T, topo, ops, EST):
             L = lambda j, k=1: at("L", (j, j + k), (q0, q1))
             y = at(U_BANK[gi], (0, nb))
             move(ON["rq"], h("rq"), y)
-            tt(y, y, h("rq"), A.subtract)
+            tt(h("yT"), y, h("rq"), A.subtract)
+            mms([(y, h("yT"), Id)])
             act(h("sq"), y, F.Square, scale=4096.0, bias=c16)
             tt(h("tt"), h("sq"), h("b4"), A.add)
             ts(h("tb"), h("tt"), 480, A.bitwise_and)
@@ -389,7 +401,7 @@ def build(core, T, topo, ops, EST):
                 ts(h("Fc"), h("tb"), 0.0, A.is_equal)
             else:
                 act(h("Fc"), h("tb"), F.Relu, scale=-1.0, bias=1.0)
-            s1, s2 = at("b0", (4 + b0, 4 + b1)), at("b1", (4 + b0, 4 + b1))
+            s1, s2 = at("b0", (8 + b0, 8 + b1)), at("b1", (8 + b0, 8 + b1))
             mms([(s1, at("CN2"), h("Fc"))])
             mms([(s2, at("CN2"), h("Fc"))])
             act(qt(4), s1, F.Relu, scale=-4096.0, bias=cm99)
@@ -442,26 +454,23 @@ def build(core, T, topo, ops, EST):
             ts(h("nd"), h("nc"), 4095, A.bitwise_and)
             act(h("z1"), ind(at(D), at(JU, (0, m))), F.Abs)
             act(h("z2"), ind(at(D), at(JU, (m, 2 * m))), F.Abs)
-            move(ON["yi"], q("yi"), L(8))
-            ts(q("y7"), q("yi"), 7, A.bitwise_and)
-            if TT_U16:
-                tt(q("WLU"), q("y7"), at("hm", 2, (q0, q1)), A.add)
-            else:
-                tt(q("w2"), q("y7"), at("hm", 2, (q0, q1)), A.add)
-                move(ON["WLU"], q("WLU"), q("w2"))
 
-        for ch in range(len(CHUNKS)):
-            chunk(ch)
         for gi in range(len(PARTS)):
-            tag["c%d" % gi] = len(ops)
+            gathers(gi)
+        for gi in range(len(PARTS)):
+            tag["c%d" % gi] = [len(ops)]
             claims(gi)
         for names in TURNS:
             for a, b in zip(names, names[1:]):
-                ops[tag[b]]["after"].append((tag[a], 0.0))
+                ops[tag[b][0]]["hard"].append(tag[a][-1])
         for j in range(3, -1, -1):
             cp(ind(at("Si"), at("posU", (4 * j, 4 * j + 4))), at("nd", (64 * j, 64 * j + 64)))
-        for lo, hi in PARTS:
-            w = at("WLU", (lo // 16, hi // 16))
+        for lo, hi in X_CUTS:
+            q0, q1 = lo // 16, hi // 16
+            move(ON["yi"], at("yi", (q0, q1)), at("L", 8, (q0, q1)))
+            ts(at("y7", (q0, q1)), at("yi", (q0, q1)), 7, A.bitwise_and)
+            w = at("WLU", (q0, q1))
+            tt(w, at("y7", (q0, q1)), at("hm", 2, (q0, q1)), A.add)
             cp(ind(at("XX", (0, 6144)), w), at("z1", (lo, hi)))
             if not last and X_COPY == "V":
                 cp(ind(at("XX", (2048, 8192)), w), at("z1", (lo, hi)))
@@ -683,11 +692,8 @@ def improve(ops, order, cases):
                     stack.pop()
         return out, full
 
-    order, full = arrange(key)
-    now = [run(order, d, w) for d, w in cases]
-    cost = sum(x[0] for x in now)
-    best = (cost, order)
-    for it in range(SHIFTS):
+    best = (0, order)
+    for it in range(0):
         held, why = now[int(rng.integers(len(cases)))][1:3]
         new = list(key)
         for rep in range(1 + int(rng.random() < 0.3)):
@@ -762,6 +768,114 @@ def improve(ops, order, cases):
     return order, extra, best[0] / len(cases)
 
 
+def plan(ops, cases):
+    n = len(ops)
+    names = sorted(set(o["q"] for o in ops) | set(b for o in ops for b in o["banks"]))
+    queue = [names.index(o["q"]) if o["kind"] != "recv" else -1 for o in ops]
+    banks = [[names.index(b) for b in sorted(o["banks"])] for o in ops]
+    pred = [sorted(o["d"]) for o in ops]
+    hard = [o["hard"] for o in ops]
+    isdma = [o["kind"] == "dma" for o in ops]
+    succ = [[] for _ in range(n)]
+    for i in range(n):
+        for j in set(pred[i]) | set(hard[i]):
+            succ[j].append(i)
+    count = [len(set(pred[i]) | set(hard[i])) for i in range(n)]
+    slots = {}
+    slot = [slots.setdefault(o["slot"], len(slots)) for o in ops]
+
+    def run(dur, wake, order=None, rank=None):
+        end, why, issued, base, cause = [0.0] * n, [-1] * n, [0.0] * n, [0.0] * n, [-1] * n
+        free, last, user = [0.0] * len(names), [-1] * len(names), [[] for _ in names]
+        need, out = list(count), []
+        ready = [i for i in range(n) if count[i] == 0]
+
+        def start(i):
+            s, w, q = base[i], cause[i], queue[i]
+            if q >= 0 and free[q] > s:
+                s, w = free[q], -2 - last[q]
+            for b in banks[i]:
+                for j in user[b]:
+                    if queue[j] != q and end[j] + wake > s:
+                        s, w = end[j] + wake, -2 - j
+            return s, w
+
+        for pos in range(n):
+            if order:
+                i = order[pos]
+                s, w = start(i)
+            else:
+                cand = [(start(i), i) for i in ready]
+                (s0, w0), i0 = min(cand, key=lambda c: c[0][0] + (0.1 if isdma[c[1]] else dur[c[1]]))
+                lim, q0 = s0 + REACH * (0.1 if isdma[i0] else dur[i0]), queue[i0]
+                (s, w), i = max([c for c in cand if queue[c[1]] == q0 and c[0][0] <= lim], key=lambda c: rank[c[1]])
+                ready.remove(i)
+                out.append(i)
+            q = queue[i]
+            for b in banks[i]:
+                user[b] = [j for j in user[b] if queue[j] != q] + [i]
+            end[i], why[i] = s + dur[i], w
+            issued[i] = s + 0.1 if isdma[i] else end[i]
+            if q >= 0:
+                free[q], last[q] = issued[i], i
+            for k in succ[i]:
+                need[k] -= 1
+                if need[k] == 0:
+                    t, c = 0.0, -1
+                    for j in pred[k]:
+                        if end[j] + wake > t:
+                            t, c = end[j] + wake, j
+                    for j in hard[k]:
+                        if issued[j] > t:
+                            t, c = issued[j], j
+                    base[k], cause[k] = t, c
+                    if not order:
+                        ready.append(k)
+        i = max(range(n), key=lambda x: end[x])
+        total, held = end[i] + EARLY * sum(end) / n, []
+        while why[i] != -1:
+            j = why[i] if why[i] >= 0 else -2 - why[i]
+            if why[i] < 0:
+                held.append((j, i))
+            i = j
+        return total, held, out
+
+    dur, wake = cases[0]
+    way = [0.0] * n
+    for sweep in range(4):
+        for i in range(n - 1, -1, -1):
+            way[i] = dur[i] + max([way[k] + wake for k in succ[i]] + [0.0])
+
+    def judge(gain):
+        first = run(dur, wake, None, [way[i] + gain[slot[i]] for i in range(n)])
+        res = [first] + [run(d, w, first[2]) for d, w in cases[1:]]
+        return sum(x[0] for x in res), res
+
+    rng = np.random.default_rng(SEED)
+    gain = [0.0] * len(slots)
+    cost, now = judge(gain)
+    best = (cost, now[0][2])
+    for it in range(SHIFTS):
+        held = now[int(rng.integers(len(cases)))][1]
+        new = list(gain)
+        for rep in range(1 + int(rng.random() < 0.3)):
+            if held and rng.random() < 0.8:
+                j, i = held[int(rng.integers(len(held)))]
+                gap = max(way[j] + gain[slot[j]] - way[i] - gain[slot[i]], 0.0) + float(rng.random())
+                if rng.random() < 0.5:
+                    new[slot[i]] += gap
+                else:
+                    new[slot[j]] -= gap
+            else:
+                new[int(rng.integers(len(slots)))] += float(rng.normal()) * 2
+        c, res = judge(new)
+        if c <= cost + MARGIN * (1 - it / SHIFTS) * float(rng.random()):
+            gain, now, cost = new, res, c
+            if c < best[0]:
+                best = (c, res[0][2])
+    return best[1]
+
+
 PLAN = {}
 
 
@@ -777,7 +891,7 @@ def rank_program(g, core, T, topo):
             other = []
             build(core, T, topo, other, dict(EST, **c))
             cases.append(([o["dur"] for o in other], dict(EST, **c)["wake"]))
-        PLAN["order"] = improve(ops, schedule(ops), cases)
+        PLAN["order"] = improve(ops, plan(ops, cases), cases)
     order = PLAN["order"][0]
     for i, j in PLAN["order"][1]:
         ops[i]["d"].add(j)

@@ -4,138 +4,59 @@ from concourse.mybir import AluOpType as A, ActivationFunctionType as F
 STEPS = 4
 CHUNKS = ((192, 256), (128, 192), (64, 128), (0, 64))
 PARTS = ((128, 256), (0, 128))
-U_BANK = ("b2", "b3")
-TURNS = (("G1", "G3"), ("a0", "a1", "a2", "a3"), ("G0", "G2"), ("d0", "d1", "d2", "d3"))
-G_ON = "VSVS"
+TURNS = (("a0", "a1", "a2", "a3"), ("G0", "G2", "G3", "d0", "d1", "d2", "d3"))
+G_ON = "VSVV"
 ABS_ON = "VVSV"
-AB_ON = "VVVV"
-C_CUTS = ((128, 256), (0, 128))
-E_CUTS = ((0, 256),)
-X_CUTS = ((128, 256), (0, 128))
-G_SUB = (1, 1, 1, 1)
-X_SUB = (1, 1, 1, 1)
-Z_SUB = (1, 1, 1, 1)
-OLD_ON = "S"
-HALF_ON = "V"
-ON = {"rq": "S", "Fc": "V", "c": "S", "cF": "S", "sF": "S", "JU": "S", "yi": "S", "WLU": "S", "XLU": "S", "sU": "V", "ch": "S", "pos": "V"}
-TT_U16 = True
-ROUNDS = 1
-X_COPY = "Y"
-SPLIT_AB = (0,)
+SUM_ON = "PV"
+X_SUB = (1, 1, 2, 2)
+Z_SUB = (1, 1, 2, 2)
+LR_CUT = 16
+YT_ON = "SVSSSS"
 MAGIC = 12582912.0
-NT = 9
+NT = 8
 
 SCRATCH = {
     "Si": ("sbuf", [128, 4352], "int32"),
     "XX": ("sbuf", [128, 8192], "bfloat16"),
-    "G": ("sbuf", [128, 4096], "float16"),
-    "Xa": ("sbuf", [128, 4096], "bfloat16"),
-    "S16": ("sbuf", [128, 4096], "float16"),
-    "AB": ("sbuf", [128, 512], "uint16"),
-    "on": ("sbuf", [128, 256], "bfloat16"),
-    "SEL": ("sbuf", [128, 16, 2, 8], "bfloat16"),
-    "GT": ("sbuf", [128, 512], "float16"),
-    "yT": ("sbuf", [128, 256], "float16"),
-    "ER": ("sbuf", [128, 16, 128], "bfloat16"),
-    "LR": ("sbuf", [128, 16, 8, 16], "bfloat16"),
-    "WG": ("sbuf", [128, 2, 8], "bfloat16"),
-    "PM": ("sbuf", [128, 4, 4, 32], "bfloat16"),
-    "PF": ("sbuf", [128, 2, 128], "bfloat16"),
-    "UK": ("sbuf", [128, 4, 4, 32], "bfloat16"),
-    "BI": ("sbuf", [128, 128], "bfloat16"),
-    "BM": ("sbuf", [128, 4, 32], "bfloat16"),
-    "Id": ("sbuf", [128, 4, 32], "bfloat16"),
-    "SW": ("sbuf", [128, 128], "bfloat16"),
-    "CNT": ("sbuf", [128, 128], "bfloat16"),
-    "CN2": ("sbuf", [128, 128], "bfloat16"),
-    "mat": ("sbuf", [128, 8, 128], "bfloat16"),
-    "hi": ("sbuf", [128, 512], "bfloat16"),
-    "con": ("sbuf", [128, 5, 256], "bfloat16"),
-    "RM": ("sbuf", [128, 256], "bfloat16"),
-    "RS": ("sbuf", [128, 768], "bfloat16"),
-    "r256": ("sbuf", [128, 256], "float32"),
-    "JC": ("sbuf", [128, NT, 16], "float16"),
-    "KT": ("sbuf", [128, 3, 16], "float32"),
-    "EQ": ("sbuf", [128, 16], "float32"),
-    "q16": ("sbuf", [128, 16], "float32"),
-    "Ic": ("sbuf", [128, 16], "float32"),
-    "col": ("sbuf", [128, 8], "float32"),
-    "pI": ("sbuf", [128, 4], "int32"),
-    "wI": ("sbuf", [128, 1], "int32"),
-    "sL0": ("sbuf", [128, 16], "int32"),
-    "sL": ("sbuf", [128, 16], "int32"),
-    "sU": ("sbuf", [128, 16], "uint16"),
-    "sF": ("sbuf", [128, 16], "float16"),
-    "m0": ("sbuf", [128, 16], "float32"),
-    "m1": ("sbuf", [128, 16], "int32"),
-    "hm": ("sbuf", [128, 3, 16], "float32"),
-    "yi": ("sbuf", [128, 16], "int32"),
-    "y7": ("sbuf", [128, 16], "int32"),
-    "w2": ("sbuf", [128, 16], "float32"),
-    "WLU": ("sbuf", [128, 16], "uint16"),
-    "xt": ("sbuf", [128, 16], "int32"),
-    "xi": ("sbuf", [128, 16], "float32"),
-    "XLU": ("sbuf", [128, 16], "uint16"),
-    "posU": ("sbuf", [128, 16], "uint16"),
-    "jk": ("sbuf", [128, 16], "bfloat16"),
-    "accB": ("sbuf", [128, 128], "float16"),
-    "cU": ("sbuf", [128, 256], "uint16"),
-    "cF": ("sbuf", [128, 256], "float16"),
-    "rq": ("sbuf", [128, 256], "float16"),
-    "old": ("sbuf", [128, 256], "float32"),
-    "ch": ("sbuf", [128, 2, 16], "float16"),
-    "sq": ("sbuf", [128, 256], "float32"),
-    "tt": ("sbuf", [128, 256], "int32"),
-    "tb": ("sbuf", [128, 256], "int32"),
-    "Fc": ("sbuf", [128, 256], "float16"),
-    "nc": ("sbuf", [128, 256], "int32"),
-    "nd": ("sbuf", [128, 256], "int32"),
-    "RT": ("sbuf", [128, 4, 2, 32], "float32"),
-    "eq": ("sbuf", [128, 768], "bfloat16"),
-    "lose": ("sbuf", [128, 768], "bfloat16"),
-    "CN1": ("sbuf", [128, 128], "bfloat16"),
-    "c47": ("sbuf", [128, 256], "float16"),
-    "dump": ("sbuf", [128, 16], "float32"),
-    "pos": ("sbuf", [128, 16], "float32"),
-    "b4": ("psum", [128, 512], "float32"),
-    "z1": ("sbuf", [128, 256], "bfloat16"),
-    "z2": ("sbuf", [128, 256], "bfloat16"),
-    "ha": ("sbuf", [128, 256], "float32"),
-    "yto": ("sbuf", [128, 256], "float32"),
-    "yso": ("sbuf", [128, 16], "float32"),
-    "rcv": ("sbuf", [128, STEPS, 16], "float32"),
-    "Y": ("sbuf", [128, STEPS, 256], "bfloat16"),
     "XC": ("sbuf", [128, (STEPS + 1) * 768], "bfloat16"),
     "L": ("psum", [128, 32, 16], "float32"),
+    "b4": ("psum", [128, 512], "float32"),
 }
+for _dt, _shapes in (
+        ("bfloat16", {"Xa": [4096], "on": [256], "SEL": [16, 2, 8], "ER": [16, 128], "LR": [16, 8, 16], "WG": [2, 8], "PM": [4, 4, 32], "PF": [2, 128],
+                      "UK": [4, 4, 32], "BI": [128], "BM": [4, 32], "Id": [4, 32], "CNT": [128], "CN1": [128], "CN2": [128], "mat": [8, 128],
+                      "con": [5, 256], "RM": [256], "RS": [384], "jk": [16], "eq": [768], "lose": [768], "zz": [512], "Y": [STEPS, 256],
+                      "D0": [4096], "D1": [4096], "Z0": [4096], "Z1": [4096]}),
+        ("float16", {"G": [4096], "S16": [4096], "GT": [512], "yT": [256], "JC": [NT, 16], "sF": [16], "accB": [128], "cF": [256], "rq": [256],
+                     "old": [256], "ch": [2, 16], "Fc": [256], "c47": [256], "Qt0": [4 * NT, 2, 16], "Qt1": [4 * NT, 2, 16]}),
+        ("float32", {"r256": [256], "KT": [2, 16], "EQ": [16], "q16": [16], "Ic": [16], "I8": [16], "w8": [16], "col": [8], "m0": [16], "hm": [2, 16], "old2": [256],
+                     "RT": [4, 2, 32], "dump": [16], "ha": [256], "ysum": [1024], "yto": [256], "yso": [16], "rcv": [STEPS, 16],
+                     "cs0": [2 * STEPS, 8], "cs1": [2 * STEPS, 8]}),
+        ("int32", {"pI": [4], "wI": [1], "sL0": [16], "sL": [16], "m1": [16], "yi": [16], "y7": [16], "xt": [16], "ei": [256], "em": [256], "sq": [256], "tb": [256],
+                   "nc": [256], "nd": [256]}),
+        ("uint16", {"AB": [512], "sU": [16], "WLU": [16], "XLU": [16], "posU": [16], "cU": [256], "JU0": [24], "JU1": [24]})):
+    for _nm in _shapes:
+        SCRATCH[_nm] = ("sbuf", [128] + _shapes[_nm], _dt)
 for _b in (0, 1, 2, 3, 5, 7):
     SCRATCH["b%d" % _b] = ("psum", [128, 16, 2, 16], "float32")
-for _p in range(2):
-    SCRATCH["D%d" % _p] = ("sbuf", [128, 4096], "bfloat16")
-    SCRATCH["Z%d" % _p] = ("sbuf", [128, 4096], "bfloat16")
-for _g, (_a, _b) in enumerate(PARTS):
-    _n = _b - _a
-    SCRATCH["Qt%d" % _g] = ("sbuf", [128, NT * (_n // 32), 2, 16], "float16")
-    SCRATCH["JU%d" % _g] = ("sbuf", [128, 3 * _n // 16], "uint16")
-    SCRATCH["cs%d" % _g] = ("sbuf", [128, 2 * STEPS, _n // 16], "float32")
 
-SEMAPHORES = ["eV", "eS", "eP", "eG"] + ["m%d" % i for i in range(24)]
+SEMAPHORES = ["eV", "eS", "eP", "eG"] + ["m%d" % i for i in range(16)]
 for _t in range(STEPS):
-    SEMAPHORES += ["ax%d" % _t, "lx%d" % _t]
-    for _g in range(len(PARTS)):
-        SEMAPHORES += ["an%d_%d" % (_t, _g), "ln%d_%d" % (_t, _g)]
+    for _nm in ("x%d" % _t, "n%d_0" % _t, "n%d_1" % _t):
+        SEMAPHORES += ["a" + _nm, "l" + _nm]
 
-EST = {"cyc": 0.00083 * 1.08, "V": 0.02, "S": 0.04, "ind": 0.03, "ga": 1.3, "sc": 3.5, "pe": 0.00075, "wake": 0.14, "net": 2.5, "dma": 1.3, "rate": 350e3}
-CASES = ({}, {"net": 3.5, "pe": 0.0005, "wake": 0.12, "ga": 1.5})
-JITTER = 0.5
+EST = {"cyc": 0.00083 * 1.05, "V": 0.02, "S": 0.04, "ind": 0.12, "ga": 1.2, "sc": 3.5, "pe": 0.00063, "wake": 0.14, "same": 0.19, "net": 3.2, "dma": 1.3, "rate": 350e3}
+CASES = ({}, {"cyc": 0.00083 * 1.4, "pe": 0.00085, "ga": 1.35}, {"net": 3.8, "ga": 1.05, "cyc": 0.00083})
 REACH = 0.5
-SEED = 1
-SHIFTS = 3000
-PERIOD = 21.0
-MOVES = 1000
-MARGIN = 0.6
-EARLY = 0.3
+URGENT = {"fork0": 4.0, "fork1": 4.0, "claim0": 4.0, "tables0": 4.0, "lists0": 4.0, "lists1": 2.0}
+SEED = 4
+SHIFTS = 4500
+TASKS = 0.2
+MOVES = 300
+MARGIN = 0.9
+EARLY = 0.1
 COLUMNS = {}
+PLAN = {}
 SIZE = {"float32": 4, "int32": 4, "bfloat16": 2, "float16": 2, "uint16": 2}
 
 
@@ -147,7 +68,7 @@ def pieces(lo, hi, k):
 def build(core, T, topo, ops, EST):
     rank = T.rank_of(core)
     cyc = EST["cyc"]
-    cols, times, now = {}, {}, [-1]
+    times, now = {}, [-1, "start"]
 
     def at(name, *idx):
         where, shape, dt = SCRATCH[name]
@@ -172,7 +93,8 @@ def build(core, T, topo, ops, EST):
         banks = set(x["acc"][0] for x in ins + outs if isinstance(x, dict) and x["ps"])
         sig = (q, now[0] < 0) + tuple(x[0].rstrip("01") if x[0][0] in "DZ" else x[0] for x in w + r)
         times[sig] = times.get(sig, 0) + 1
-        ops.append({"slot": (sig, times[sig]), "step": max(now[0], 0), "q": q, "fn": fn, "dur": dur, "r": r, "w": w, "kind": kind, "sem": sem, "cnt": cnt, "banks": banks, "after": [], "hard": []})
+        ops.append({"slot": (sig, times[sig]), "task": now[1], "step": max(now[0], 0), "q": q, "fn": fn, "dur": dur, "r": r, "w": w,
+                    "kind": kind, "sem": sem, "cnt": cnt, "banks": banks, "hard": []})
 
     def time(q, out, i0, per):
         if out["off"]:
@@ -206,12 +128,6 @@ def build(core, T, topo, ops, EST):
         else:
             ts(out, i0, c, A.add)
 
-    def move(q, out, i0):
-        if q == "S":
-            act(out, i0, F.Copy)
-        else:
-            cp(out, i0)
-
     def mms(calls, start=True, stop=True):
         first, m = [], 0
         for j, c in enumerate(calls):
@@ -225,9 +141,9 @@ def build(core, T, topo, ops, EST):
             for j, c in enumerate(calls):
                 last = e.matmul(val(c[0]), val(c[1]), val(c[2]), first[j], first[j + 1])
             return last
-        dur = 0.03 + EST["pe"] * sum(max(64, c[2]["n"]) * (1 if c[2]["two"] else 4) for c in calls)
         outs = [c[0] for c in calls]
-        add("P", run, dur, outs, [c[1] for c in calls] + [c[2] for c in calls] + ([] if start else outs))
+        add("P", run, 0.03 + EST["pe"] * sum(max(64, c[2]["n"]) for c in calls), outs, [c[1] for c in calls] + [c[2] for c in calls] + ([] if start else outs))
+        ops[-1].update({"goes on": not start, "open": not stop})
 
     def asel(out, i0, pat, op, base, cm):
         add("G", lambda e: e.affine_select(val(out), val(i0), pat, op, 0.0, base, cm), 0.17 + 2 * cyc * out["n"], [out], [i0])
@@ -237,11 +153,11 @@ def build(core, T, topo, ops, EST):
 
     ndma = [0]
 
-    def dma(q, out, i0, extra=0.0):
+    def dma(out, i0, behind=0.0):
         s = "m%d" % ndma[0]
         ndma[0] += 1
         sb = out if isinstance(out, dict) else i0
-        add(q, lambda e: e.dma_start(val(out), val(i0)), EST["dma"] + extra + sb["bytes"] / EST["rate"], [out] if isinstance(out, dict) else [],
+        add("Y", lambda e: e.dma_start(val(out), val(i0)), EST["dma"] + behind + sb["bytes"] / EST["rate"], [out] if isinstance(out, dict) else [],
             [i0], "dma", s, 16)
 
     def send(out, i0, sem, dst):
@@ -250,23 +166,20 @@ def build(core, T, topo, ops, EST):
         mask = sum(1 << e for e in eng)
         add("G", lambda e: e.remote_dma(val(out), val(i0), T.sem["a" + sem], T.sem["l" + sem], pid, rid, mask), 0.6, [], [i0], "send", "a" + sem, len(eng))
         add("N", None, EST["net"] + out["bytes"] / 60e3, [out], [i0], "recv", "a" + sem, len(eng))
-        ops[-1]["after"].append((len(ops) - 2, 0.0))
         ops[-1]["hard"].append(len(ops) - 2)
 
-    dma("Y", at("sL0"), T.s0[:])
-    dma("Y", at("Si", (0, 4096)), T.stm[:])
-    dma("Y", at("wI"), T.wt[:], 6.0)
-    dma("Y", at("XX", (0, 2048)), T.vx[:], 6.0)
-    if X_COPY:
-        dma("Y", at("XX", (2048, 4096)), T.vx[:], 7.5)
-    dma("Y", at("XC", (0, 256)), T.x0[:], 8.0)
+    dma(at("sL0"), T.s0[:])
+    dma(at("Si", (0, 4096)), T.stm[:])
+    dma(at("wI"), T.wt[:], 6.0)
+    dma(at("XX", (0, 2048)), T.vx[:], 6.0)
+    dma(at("XX", (2048, 4096)), T.vx[:], 7.5)
+    dma(at("XC", (0, 256)), T.x0[:], 8.0)
     for j in range(1, len(ops)):
-        ops[j]["after"].append((j - 1, 0.1 - ops[j - 1]["dur"]))
         ops[j]["hard"].append(j - 1)
 
     Id, BM, on = at("Id"), at("BM"), at("on", (0, 128))
-    kcol, dump, row0, c16, wF, acc, kfr, cm99 = [at("col", (j, j + 1)) for j in range(8)]
-    Id32, IdK, Id5, IdN, IdH, IdM, BMK, IdT = [at("mat", j) for j in range(8)]
+    kcol, row0, c16, wF, acc, kfr, cm99 = [at("col", (j, j + 1)) for j in (0, 2, 3, 4, 5, 6, 7)]
+    IdK, Id5, IdN, IdH, IdM, IdC, IdT = [at("mat", j) for j in range(7)]
     fill(at("on"), 1.0)
     iota(at("pI", (0, 1)), [[0, 1]], 1)
     iota(at("q16"), [[16, 16]], 0, allow_small_or_imprecise_dtypes=True)
@@ -287,21 +200,21 @@ def build(core, T, topo, ops, EST):
     ts(at("EQ"), at("r256", (0, 16)), kcol, A.is_equal)
     fill(at("LR"), 0.0)
     for r in range(16):
-        ts(at("ER", r), BM, at("EQ", (r, r + 1)), A.mult, -32.0, A.mult)
+        ts(at("ER", r), BM, at("EQ", (r, r + 1)), A.mult)
         act(at("LR", r, (0, 8), r), at("BM", (0, 4), (0, 32, 16)), F.Copy)
     for j in range(2):
         ts(at("WG", j), at("BM", (0, 4), (0, 32, 16)), wF, A.mult, (1.0 - 2 * j) / 4096, A.mult)
-    for m, f in ((Id32, 32.0), (IdK, 1.0 / 4096), (Id5, 5.0), (IdN, -1.0), (IdH, 0.5), (IdM, -100.0), (IdT, -2.0)):
+    for m, f in ((IdK, 1.0 / 4096), (Id5, 5.0), (IdN, -1.0), (IdH, 0.5), (IdM, -100.0), (IdT, -2.0)):
         act(m, Id, F.Copy, scale=f)
     tt(at("CN2"), at("CNT"), IdM, A.add)
-    tt(BMK, Id, at("CNT"), A.subtract)
-    act(at("CN1"), BMK, F.Copy, scale=4096.0)
+    tt(IdC, Id, at("CNT"), A.subtract)
+    act(at("CN1"), IdC, F.Copy, scale=4096.0)
     act(at("c47"), at("on", (0, 256)), F.Copy, scale=-2047.0)
-    for j, c in enumerate((32.0, 1024.0, -0.5, 6144.0, 393216.0)):
+    for j, c in enumerate((-1.0, 1024.0, -0.5, 6144.0, 4096.0 * len(YT_ON))):
         fill(at("con", j), c)
     ts(at("RM"), at("r256"), kcol, A.is_ge, 0.5, A.mult)
     fill(at("RS"), 1.0)
-    fill(at("RS", (0, 768, 32)), 0.0)
+    fill(at("RS", (0, 384, 32)), 0.0)
     fill(at("PM"), 0.0)
     fill(at("UK"), 0.0)
     for a in range(2):
@@ -312,50 +225,46 @@ def build(core, T, topo, ops, EST):
         tt(at("PF", a), at("PM", 2 * a), at("PM", 2 * a + 1), A.add)
     ts(at("Ic"), at("q16"), kcol, A.add)
     ts(at("dump"), at("Ic"), 4096.0, A.add)
-    for j, (f, c) in enumerate(((16.0, 0.0), (16.0, 0.0), (0.0, 32768.0), (0.0, 2048.0), (0.0, 0.0), (0.0, 0.0), (-1.0 / 512, -1.0), (0.0, 14336.0), (0.0, 0.0))):
+    for j, (f, c) in enumerate(((16.0, 0.0), (16.0, 0.0), (0.0, 32768.0), (0.0, 2048.0), (0.0, 0.0), (0.0, 0.0), (0.0, 14336.0), (0.0, 0.0))):
         ts(at("JC", j), at("Ic"), f, A.mult, c, A.add)
-    for j, c in enumerate((16.0, 8.0, -4096.0)):
+    ts(at("I8"), at("Ic"), 8.0, A.mult, 4096.0, A.add)
+    for j, c in enumerate((16.0, 8.0)):
         fill(at("KT", j), c)
-    act(at("accB"), on, F.Copy, scale=0.0625)
+    act(at("accB"), on, F.Copy, scale=-0.0625)
     cp(at("sU"), at("sL0"))
 
-    swin, xwin = at("Si", (0, 4096)), at("XX", (0, 4096 if X_COPY else 2048))
+    swin, xwin = at("Si", (0, 4096)), at("XX", (0, 4096))
 
     def step(t):
         last = t + 1 == STEPS
         D, Z = "D%d" % (t % 2), "Z%d" % (t % 2)
         x0 = 768 * t
         tag = {}
-        now[0] = t
+        now[:] = [t, "gathers"]
         times.clear()
         dst = T.cores[(rank + 1 + t % (len(T.cores) - 1)) % len(T.cores)]
-        for lo, hi in C_CUTS:
-            move(ON["c"], at("cU", (lo, hi)), ind(swin, at("sU", (lo // 16, hi // 16))))
-        for lo, hi in E_CUTS:
-            plus(ON["sF"], at("sF", (lo // 16, hi // 16)), at("sU", (lo // 16, hi // 16)), -2048.0)
-            plus(ON["cF"], at("cF", (lo, hi)), at("cU", (lo, hi)), -2048.0)
+        for lo, hi in PARTS:
+            act(at("cU", (lo, hi)), ind(swin, at("sU", (lo // 16, hi // 16))), F.Copy)
+        plus("S", at("sF", (0, 16)), at("sU", (0, 16)), -2048.0)
+        plus("S", at("cF", (0, 256)), at("cU", (0, 256)), -2048.0)
         for ch, (lo, hi) in enumerate(CHUNKS):
-            for j, (a, b) in enumerate(pieces(lo, hi, G_SUB[ch])):
-                plus(G_ON[ch][j % len(G_ON[ch])], at("G", (16 * a, 16 * b)), ind(swin, at("cU", (a, b))), -2048.0)
-                tag.setdefault("G%d" % ch, []).append(len(ops) - 1)
-        for lo, hi in E_CUTS:
-            E = at("b4", (lo, hi))
-            mms([(E, Id32, at("cF", (lo, hi))), (E, at("accB"), at("con", 0, (lo, hi)))] +
-                [(at("b4", (lo + r, hi, 16)), at("ER", r), at("sF", (lo // 16, hi // 16))) for r in range(16)])
-            mms([(at("b5", (lo // 32, hi // 32)), IdK, at("cF", (lo, hi)))])
+            plus(G_ON[ch], at("G", (16 * lo, 16 * hi)), ind(swin, at("cU", (lo, hi))), -2048.0)
+            tag["G%d" % ch] = [len(ops) - 1]
+        E = at("b4", (0, 256))
+        mms([(E, IdN, at("cF", (0, 256))), (E, at("accB"), at("con", 0, (0, 256)))] + [(at("b4", (r, 256, 16)), at("ER", r), at("sF", (0, 16))) for r in range(16)])
+        act(at("ei"), E, F.Copy)
+        ts(at("em"), at("ei"), 15, A.bitwise_and)
+        act(E, at("em"), F.Copy)
+        mms([(at("b5", (0, 8)), IdK, at("cF", (0, 256)))])
 
         def gathers(gi):
             lo, hi = PARTS[gi]
-            bank, ub, o = "b%d" % gi, U_BANK[gi], 2 * lo
-            ps, gt = at(bank, (0, 8)), at("GT", (o, o + 256))
-            mms(([] if X_COPY else [(ps, Id, at("con", 4))]) + [(at(bank, (0, 8), (0, 2), k), at("G", (16 * lo + k, 16 * hi, 16)), at("SEL", k)) for k in range(16)])
-            if X_COPY:
-                move(AB_ON[2 * gi], gt, ps)
-            else:
-                plus(AB_ON[2 * gi], at("hi", (o, o + 256)), ps, -1023.5)
-                tt(gt, ps, at("hi", (o, o + 256)), A.subtract)
+            bank, ub, o = "b%d" % gi, "b%d" % (2 + gi), 2 * lo
+            ps = at(bank, (0, 8))
+            mms([(at(bank, (0, 8), (0, 2), k), at("G", (16 * lo + k, 16 * hi, 16)), at("SEL", k)) for k in range(16)])
+            act(at("GT", (o, o + 256)), ps, F.Copy)
             mms([(at(bank, (4 * j, 4 * j + 4)), at("GT", (o + 128 * j, o + 128 * j + 128)), Id) for j in range(2)])
-            plus(AB_ON[2 * gi + 1], at("AB", (o, o + 256)), ps, 2048.0 if X_COPY else 0.0)
+            plus("S", at("AB", (o, o + 256)), ps, 2048.0)
             mine = [ch for ch in range(len(CHUNKS)) if lo <= CHUNKS[ch][0] < hi]
             for ch in mine:
                 for c0, c1 in pieces(CHUNKS[ch][0], CHUNKS[ch][1], X_SUB[ch]):
@@ -370,60 +279,59 @@ def build(core, T, topo, ops, EST):
                         ts(at(Z, (a, b)), at(D, (a, b)), 0.0, A.max, 2.0, A.mult)
                     else:
                         act(at(Z, (a, b)), at(D, (a, b)), F.Abs)
-                    tag.setdefault("z%d" % ch, []).append(len(ops) - 1)
             relu = [CHUNKS[ch] for ch in mine if ABS_ON[ch] == "V"]
             pre = [(at(ub, (0, 4)), Id, at("con", 1, (0, 128)))]
-            if relu:
-                c0, c1 = min(c[0] for c in relu), max(c[1] for c in relu)
-                for k in range(16):
-                    out = at(ub, (0, 4), (0, 2), k)
-                    pre.append((dict(out, ap=T[ub][c0 - lo:c1 - lo, 0:4, 0:2, k]), at(D, (16 * c0 + k, 16 * c1, 16)), at("WG", 1)))
+            c0, c1 = min(c[0] for c in relu), max(c[1] for c in relu)
+            for k in range(16):
+                out = at(ub, (0, 4), (0, 2), k)
+                pre.append((dict(out, ap=T[ub][c0 - lo:c1 - lo, 0:4, 0:2, k]), at(D, (16 * c0 + k, 16 * c1, 16)), at("WG", 1)))
             mms(pre, True, False)
             ops[-1]["r"].append(at(ub, (4, 16))["acc"])
             mms([(at(ub, (0, 4), (0, 2), k), at(Z, (16 * lo + k, 16 * hi, 16)), at("WG", 0)) for k in range(16)], False, True)
 
         def claims(gi):
             lo, hi = PARTS[gi]
-            q0, q1, b0, b1, nb, m = lo // 16, hi // 16, lo // 32, hi // 32, (hi - lo) // 32, (hi - lo) // 16
-            Qt, JU, cs = "Qt%d" % gi, "JU%d" % gi, "cs%d" % gi
+            q0, q1, b0, b1, nb, m, w = lo // 16, hi // 16, lo // 32, hi // 32, (hi - lo) // 32, (hi - lo) // 16, hi - lo
+            Qt, JU, cs, ub = "Qt%d" % gi, "JU%d" % gi, "cs%d" % gi, "b%d" % (2 + gi)
             h = lambda nm: at(nm, (lo, hi))
             q = lambda nm: at(nm, (q0, q1))
             qt = lambda j, k=1: at(Qt, (j * nb, (j + k) * nb))
             L = lambda j, k=1: at("L", (j, j + k), (q0, q1))
-            y = at(U_BANK[gi], (0, nb))
-            move(ON["rq"], h("rq"), y)
+            y = at(ub, (0, nb))
+            now[1] = "claim%d" % gi
+            act(h("rq"), y, F.Copy)
             tt(h("yT"), y, h("rq"), A.subtract)
             mms([(y, h("yT"), Id)])
             act(h("sq"), y, F.Square, scale=4096.0, bias=c16)
-            tt(h("tt"), h("sq"), h("b4"), A.add)
-            ts(h("tb"), h("tt"), 480, A.bitwise_and)
-            if ON["Fc"] == "V":
-                ts(h("Fc"), h("tb"), 0.0, A.is_equal)
-            else:
-                act(h("Fc"), h("tb"), F.Relu, scale=-1.0, bias=1.0)
+            ts(h("tb"), h("sq"), 5, A.arith_shift_right, 15, A.bitwise_and)
+            tt(h("Fc"), h("tb"), h("b4"), A.is_equal)
+            now[1] = "tables%d" % gi
             s1, s2 = at("b0", (8 + b0, 8 + b1)), at("b1", (8 + b0, 8 + b1))
             mms([(s1, at("CN2"), h("Fc"))])
             mms([(s2, at("CN2"), h("Fc"))])
             act(qt(4), s1, F.Relu, scale=-4096.0, bias=cm99)
             ts(qt(5), s2, -99.0, A.is_equal, 4096.0, A.mult)
-            act(qt(7), y, F.Copy, scale=row0)
+            act(qt(6), y, F.Copy, scale=row0)
             s3 = at("b5", (8 + b0, 8 + b1))
             mms([(s3, Id, h("cF")), (s3, Id, at("c47", (lo, hi))), (s3, at("CN1"), h("Fc"))])
             ts(qt(2), s3, 0.0, A.max, -2048.0, A.add)
             tt(qt(3), qt(5), at("b5", (b0, b1)), A.mult)
-            tt(qt(8), qt(4), y, A.mult)
+            tt(qt(7), qt(4), y, A.mult)
             act(qt(0, 2), qt(4, 2), F.Copy, scale=kfr)
-            act(qt(6), qt(4), F.Copy, scale=1.0 / 4096)
-            R, w, ub = at("b4", (256 + lo, 256 + hi)), hi - lo, U_BANK[gi]
+            now[1] = "lowest%d" % gi
+            R = at("b4", (256 + lo, 256 + hi))
             mms([(R, BM, qt(2))])
             B0, B1 = at("b7", (b0, b1)), at("b7", (8 + b0, 8 + b1))
             mms([(B0, Id, h("RM"))] + [(at("b7", (b0, b1), a), at("PM", 2 * a + b), at(Qt, (2 * nb, 3 * nb), b)) for a in range(2) for b in range(2)] +
                 [(at("b7", (8 + b0, 8 + b1), a), at("PM", 2 * a + 1), at(Qt, (2 * nb, 3 * nb), 0)) for a in range(2)])
             mms([(at(ub, (nb + b * nb // 2, nb + (b + 1) * nb // 2), a), at("PF", a), at(Qt, (2 * nb, 3 * nb, 2), b)) for b in range(2) for a in range(2)])
-            mms([(L(0, NT), Id, at("JC", (0, NT), (q0, q1))), (L(7), Id5, q("sF")), (L(2), IdN, at("on", (0, m)))] +
-                [(L(0, NT), at("LR", r), at(Qt, (0, NT * nb), (0, 2), r)) for r in range(16)])
-            ch = at("ch", (0, 2), (q0, q1))
-            plus(ON["ch"], ch, at("L", (2, 5, 2), (q0, q1)), -2048.0)
+            now[1] = "lists%d" % gi
+            mms([(L(0, NT), Id, at("JC", (0, NT), (q0, q1))), (L(6), Id5, q("sF")), (L(2), IdN, at("on", (0, m)))], True, False)
+            ops[-1]["r"].append(at("L", (0, NT), (q1, 16) if gi else (0, q0))["acc"])
+            for r0 in range(0, 16, LR_CUT):
+                mms([(L(0, NT), at("LR", r), at(Qt, (0, NT * nb), (0, 2), r)) for r in range(r0, r0 + LR_CUT)], False, r0 + LR_CUT == 16)
+            now[1] = "lowest%d" % gi
+            plus("S", at("ch", (0, 2), (q0, q1)), at("L", (2, 5, 2), (q0, q1)), -2048.0)
             RT = at("RT", (lo // 64, hi // 64))
             add("V", lambda e: e.transpose(val(RT), val(R)), time("V", RT, R, 1), [RT], [R])
             e0 = 3 * lo
@@ -433,95 +341,93 @@ def build(core, T, topo, ops, EST):
                 tt(at("eq", (e0 + 2 * w + b, e0 + 3 * w, 2)), at("RT", (lo // 64, hi // 64), 1), at(ub, (nb + b * nb // 2, nb + (b + 1) * nb // 2)), A.is_equal)
             lose, eq, rs = at("lose", (e0, e0 + 3 * w)), at("eq", (e0, e0 + 3 * w)), at("RS", (0, 3 * w))
             add("V", lambda e: e.tensor_tensor_scan(val(lose), val(rs), val(eq), 0.0, A.mult, A.max), time("V", lose, lose, 0.5), [lose], [rs, eq])
-            mms([(L(NT), Id, at("ch", 0, (q0, q1))), (L(NT), IdT, at("ch", 1, (q0, q1))), (L(NT), Id, at("con", 3, (0, m)))] +
-                [(at("L", NT, (q0 + a, q1, 2)), at("UK", 2 * a + b), at("lose", (e0 + 32 * b + 31, e0 + 2 * w, 64))) for a in range(2) for b in range(2)] +
-                [(at("L", NT, (q0 + 2 + a, q1, 4)), at("UK", 2 * a + b), at("lose", (e0 + 2 * w + 32 * b + 31, e0 + 3 * w, 64))) for a in range(2) for b in range(2)])
-            if TT_U16:
-                tt(q("posU"), L(NT), q("dump"), A.min)
-            else:
-                tt(q("pos"), L(NT), q("dump"), A.min)
-                move(ON["pos"], q("posU"), q("pos"))
-            if ON["JU"] == "S":
-                act(at(JU), L(0, 3), F.Relu)
-            else:
-                cp(at(JU), L(0, 3))
-            tt(at("hm", (0, 3), (q0, q1)), L(4, 3), at("KT", (0, 3), (q0, q1)), A.mult)
+            P = at("b1", 0, 0, (q0, q1))
+            mms([(P, Id, at("ch", 0, (q0, q1))), (P, IdT, at("ch", 1, (q0, q1))), (P, Id, at("con", 3, (0, m)))] +
+                [(at("b1", 0, 0, (q0 + a, q1, 2)), at("UK", 2 * a + b), at("lose", (e0 + 32 * b + 31, e0 + 2 * w, 64))) for a in range(2) for b in range(2)] +
+                [(at("b1", 0, 0, (q0 + 2 + a, q1, 4)), at("UK", 2 * a + b), at("lose", (e0 + 2 * w + 32 * b + 31, e0 + 3 * w, 64))) for a in range(2) for b in range(2)])
+            tt(q("posU"), P, q("dump"), A.min)
+            now[1] = "column%d" % gi
+            act(at(JU), L(0, 3), F.Relu)
+            now[1] = "fork%d" % gi
+            tt(at("hm", (0, 2), (q0, q1)), L(4, 2), at("KT", (0, 2), (q0, q1)), A.mult)
             tt(at(cs, (2 * t, 2 * t + 2)), L(2, 2), at("hm", (0, 2), (q0, q1)), A.add)
             send(at("rcv", t, (q0, q1)), at(cs, 2 * t + 1), "n%d_%d" % (t, gi), dst)
-            tt(q("m0"), L(7), at(cs, 2 * t), A.max)
-            move(OLD_ON, h("old"), ind(swin, at(JU, (2 * m, 3 * m))))
-            tt(h("nc"), h("old"), qt(8), A.add)
+            tt(q("m0"), L(6), at(cs, 2 * t), A.max)
+            now[1] = "column%d" % gi
+            if SUM_ON[gi] == "P":
+                plus("S", h("old"), ind(swin, at(JU, (2 * m, 3 * m))), -2048.0)
+                nc = at("b0", (b0, b1))
+                mms([(nc, Id, qt(7)), (nc, Id, h("old"))])
+                plus("S", h("nc"), nc, 2048.0)
+            else:
+                act(h("old2"), ind(swin, at(JU, (2 * m, 3 * m))), F.Copy)
+                tt(h("nc"), h("old2"), qt(7), A.add)
             ts(h("nd"), h("nc"), 4095, A.bitwise_and)
-            act(h("z1"), ind(at(D), at(JU, (0, m))), F.Abs)
-            act(h("z2"), ind(at(D), at(JU, (m, 2 * m))), F.Abs)
+            now[1] = "X%d" % gi
+            act(at("zz", (2 * lo, 2 * hi)), ind(at(D), at(JU, (0, 2 * m))), F.Abs)
 
         for gi in range(len(PARTS)):
             gathers(gi)
         for gi in range(len(PARTS)):
-            tag["c%d" % gi] = [len(ops)]
             claims(gi)
         for names in TURNS:
             for a, b in zip(names, names[1:]):
                 ops[tag[b][0]]["hard"].append(tag[a][-1])
+        now[1] = "S"
         for j in range(3, -1, -1):
             cp(ind(at("Si"), at("posU", (4 * j, 4 * j + 4))), at("nd", (64 * j, 64 * j + 64)))
-        for lo, hi in X_CUTS:
+        for gi, (lo, hi) in enumerate(PARTS):
+            now[1] = "X%d" % gi
             q0, q1 = lo // 16, hi // 16
-            move(ON["yi"], at("yi", (q0, q1)), at("L", 8, (q0, q1)))
+            act(at("yi", (q0, q1)), at("L", 7, (q0, q1)), F.Copy)
             ts(at("y7", (q0, q1)), at("yi", (q0, q1)), 7, A.bitwise_and)
+            tt(at("w8", (q0, q1)), at("I8", (q0, q1)), at("L", 4, (q0, q1)), A.subtract)
             w = at("WLU", (q0, q1))
-            tt(w, at("y7", (q0, q1)), at("hm", 2, (q0, q1)), A.add)
-            cp(ind(at("XX", (0, 6144)), w), at("z1", (lo, hi)))
-            if not last and X_COPY == "V":
-                cp(ind(at("XX", (2048, 8192)), w), at("z1", (lo, hi)))
-        if last:
-            dma("Y", T.yv[:], at("XX", (0, 2048)))
-        elif X_COPY == "Y":
-            dma("Y", at("XX", (2048, 4096)), at("XX", (0, 2048)))
-        for lo, hi in PARTS:
+            tt(w, at("y7", (q0, q1)), at("w8", (q0, q1)), A.add)
+            cp(ind(at("XX", (0, 6144)), w), at("zz", (2 * lo, lo + hi)))
+        dma(T.yv[:] if last else at("XX", (2048, 4096)), at("XX", (0, 2048)))
+        for gi, (lo, hi) in enumerate(PARTS):
+            now[1] = "place%d" % gi
             q = lambda nm: at(nm, (lo // 16, hi // 16))
             tt(q("m1"), q("m0"), at("rcv", t, (lo // 16, hi // 16)), A.max)
             ts(q("sL"), q("m1"), 4095, A.bitwise_and)
             if not last:
-                move(ON["sU"], q("sU"), q("sL"))
+                act(q("sU"), q("sL"), F.Copy)
         if last:
             cp(at("yso"), at("sL"))
-            dma("Y", T.ys[:], at("yso"))
+            dma(T.ys[:], at("yso"))
         else:
             act(at("jk"), at("L", 5), F.Copy, acc=acc, scale=1.0 / 4096)
-            act(at("accB"), on, F.Identity, scale=0.0625, bias=acc)
+            act(at("accB"), on, F.Identity, scale=-0.0625, bias=acc)
+        now[1] = "x"
         xo, yh = at("XC", (x0, x0 + 256)), at("b3", (8, 16))
-        mms([(yh, Id, at("z2")), (yh, IdN, xo)])
+        half = lambda lo, hi: at("b3", (8 + lo // 32, 8 + hi // 32))
+        mms([(yh, IdN, xo)] + [(half(lo, hi), Id, at("zz", (lo + hi, 2 * hi))) for lo, hi in PARTS])
         act(at("Y", t), yh, F.Abs)
         send(at("XC", (x0 + 256, x0 + 512)), at("Y", t), "x%d" % t, dst)
-        mms([(yh, IdH, at("z1")), (yh, IdH, xo), (yh, IdH, at("con", 2))])
-        xh = at("XC", (x0 + 512, x0 + 768))
-        if HALF_ON == "V":
-            ts(xh, yh, MAGIC, A.add, -MAGIC, A.add)
-        else:
-            act(at("ha"), yh, F.Identity, bias=MAGIC)
-            act(xh, at("ha"), F.Identity, bias=-MAGIC)
+        mms([(yh, IdH, xo), (yh, IdH, at("con", 2))] + [(half(lo, hi), IdH, at("zz", (2 * lo, lo + hi))) for lo, hi in PARTS])
+        act(at("ha"), yh, F.Identity, bias=MAGIC)
+        act(at("XC", (x0 + 512, x0 + 768)), at("ha"), F.Identity, bias=-MAGIC)
         ts(at("xt"), at("m1"), 7, A.arith_shift_right, 768, A.bitwise_and)
-        if TT_U16:
-            tt(at("XLU"), at("xt"), at("Ic"), A.add)
-        else:
-            tt(at("xi"), at("xt"), at("Ic"), A.add)
-            move(ON["XLU"], at("XLU"), at("xi"))
+        tt(at("XLU"), at("xt"), at("Ic"), A.add)
         xn = at("XC", (x0 + 768, x0 + 1024))
         act(xn, ind(at("XC", (x0, x0 + 768)), at("XLU")), F.Copy)
         if last:
-            dma("Y", T.yx[:], xn)
+            dma(T.yx[:], xn)
 
     for t in range(STEPS):
         step(t)
 
-    yt = at("b0", (0, 8))
-    for j in range(0, 16, 2):
-        a = 256 * j
-        plus("VS"[j // 2 % 2], at("S16", (a, a + 512)), at("Si", (a, a + 512)), -2048.0)
-        mms([(yt, Id, at("S16", (256 * k, 256 * k + 256))) for k in (j, j + 1)], j == 0, j == 14)
-    ts(at("yto"), yt, 32768.0, A.add)
-    dma("Y", T.yt[:], at("yto"))
+    yt, blk, many = at("b0", (0, 8)), lambda nm, j, k=1: at(nm, (256 * j, 256 * (j + k))), 2 * len(YT_ON)
+    for j in range(0, many, 2):
+        plus(YT_ON[j // 2], blk("S16", j, 2), blk("Si", j, 2), -2048.0)
+        mms([(yt, Id, blk("S16", k)) for k in (j, j + 1)] + ([(yt, Id, at("con", 4))] if j == 0 else []), j == 0, j + 2 == many)
+    k = (16 - many) // 2
+    tt(blk("ysum", 0, k), blk("Si", many, k), blk("Si", many + k, k), A.add)
+    for j in range(1, k):
+        tt(blk("ysum", 0), blk("ysum", 0), blk("ysum", j), A.add)
+    tt(at("yto"), yt, blk("ysum", 0), A.add)
+    dma(T.yt[:], at("yto"))
 
 
 def depends(ops):
@@ -539,233 +445,10 @@ def depends(ops):
                 lst[:] = [x for x in lst if x[1] & ~m]
             lst.append((i, m, wr))
         d.discard(i)
+        if o.get("goes on"):
+            o["hard"] += [j for j in d if ops[j].get("open")]
+            d -= set(o["hard"])
         o["d"] = d
-
-
-def schedule(ops):
-    wake = EST["wake"]
-    n = len(ops)
-    dur = [o["dur"] for o in ops]
-    pred = [[(j, wake) for j in sorted(o["d"])] + o["after"] for o in ops]
-    succ = [[] for _ in range(n)]
-    for i in range(n):
-        for j, lag in pred[i]:
-            succ[j].append((i, lag))
-
-    def place(before, after, key, back):
-        need = [len(p) for p in before]
-        ready = [i for i in range(n) if need[i] == 0]
-        at, busy = [0.0] * n, {}
-        while ready:
-            i = min(ready, key=lambda x: key[x])
-            ready.remove(i)
-            o, d = ops[i], dur[i]
-            s = max([at[j] + dur[j] + lag for j, lag in before[i]] + [0.0])
-            hold = (d - 0.1 if back else 0.0, d if back else 0.1) if o["kind"] == "dma" else (0.0, d)
-            res = [(o["q"], None, hold[0], hold[1])] if o["kind"] != "recv" else []
-            res += [(b, o["q"], -wake, d + wake) for b in o["banks"]]
-            moved = True
-            while moved:
-                moved = False
-                for r, own, a, b in res:
-                    lst = busy.get(r, ())
-                    k = len(lst) - 1
-                    while k >= 0 and lst[k][0] > s - 4.0:
-                        x = lst[k]
-                        if x[2] != own or own is None:
-                            if x[0] < s + b - 1e-9 and s + a < x[1] - 1e-9:
-                                s, moved = x[1] - a, True
-                                break
-                        k -= 1
-            at[i] = s
-            for r, own, a, b in res:
-                lst = busy.setdefault(r, [])
-                lst.append((s, s + d, own) if own else (s + a, s + b, None))
-                k = len(lst) - 1
-                while k > 0 and lst[k - 1][0] > lst[k][0]:
-                    lst[k - 1], lst[k] = lst[k], lst[k - 1]
-                    k -= 1
-            for k, lag in after[i]:
-                need[k] -= 1
-                if need[k] == 0:
-                    ready.append(k)
-        return at, max(at[i] + dur[i] for i in range(n))
-
-    key = [0.0] * n
-    for sweep in range(4):
-        for i in range(n - 1, -1, -1):
-            key[i] = -dur[i] + min([key[k] - lag for k, lag in succ[i]] + [0.0])
-    rng = np.random.default_rng(1)
-    best = None
-    for it in range(ROUNDS):
-        at, total = place(pred, succ, key, False)
-        if best is None or total < best[1]:
-            best = (at, total)
-        base = best[0] if it % 3 == 2 else at
-        jit = rng.random(n) * (JITTER if it % 3 == 2 else 0.0)
-        back = place(succ, pred, [-(base[i] + dur[i]) + float(jit[i]) for i in range(n)], True)[0]
-        key = [-(back[i] + dur[i]) for i in range(n)]
-    at = best[0]
-    return sorted(range(n), key=lambda i: (at[i], i))
-
-
-def improve(ops, order, cases):
-    n = len(ops)
-    names = sorted(set(o["q"] for o in ops) | set(b for o in ops for b in o["banks"]))
-    queue = [names.index(o["q"]) if o["kind"] != "recv" else -1 for o in ops]
-    banks = [[names.index(b) for b in sorted(o["banks"])] for o in ops]
-    pred = [sorted(o["d"]) for o in ops]
-    hard = [o["hard"] for o in ops]
-    allp = [set(pred[i]) | set(hard[i]) for i in range(n)]
-    isdma = [o["kind"] == "dma" for o in ops]
-
-    def run(order, dur, wake):
-        end, why = [0.0] * n, [-1] * n
-        free, last = [0.0] * len(names), [-1] * len(names)
-        user = [[] for _ in names]
-        issued = [0.0] * n
-        for i in order:
-            s, w = 0.0, -1
-            for j in pred[i]:
-                if end[j] > s:
-                    s, w = end[j], j
-            if w >= 0:
-                s += wake
-            for j in hard[i]:
-                if issued[j] > s:
-                    s, w = issued[j], j
-            q = queue[i]
-            if q >= 0 and free[q] > s:
-                s, w = free[q], -2 - last[q]
-            for b in banks[i]:
-                u = user[b]
-                keep = [i]
-                for j in u:
-                    if queue[j] != q:
-                        keep.append(j)
-                        if end[j] + wake > s:
-                            s, w = end[j] + wake, -2 - j
-                user[b] = keep
-            e = s + dur[i]
-            end[i], why[i] = e, w
-            issued[i] = s + 0.1 if isdma[i] else e
-            if q >= 0:
-                free[q], last[q] = issued[i], i
-        i = max(range(n), key=lambda x: end[x])
-        total, held = end[i] + EARLY * sum(end) / n, []
-        while why[i] != -1:
-            j = why[i] if why[i] >= 0 else -2 - why[i]
-            if why[i] < 0:
-                held.append((j, i))
-            i = j
-        return total, held, why, end
-
-    rng = np.random.default_rng(2)
-    slots = {}
-    slot = [slots.setdefault(o["slot"], len(slots)) for o in ops]
-    base = [PERIOD * o["step"] for o in ops]
-    end = run(order, *cases[0])[3]
-    first = [min(end[i] for i in range(n) if ops[i]["step"] == t and ops[i]["banks"]) for t in range(STEPS)]
-    key = [0.0] * len(slots)
-    for t in (3, 0, 2, 1):
-        for i in range(n):
-            if ops[i]["step"] == t:
-                key[slot[i]] = end[i] - cases[0][0][i] - first[t]
-    plist = [sorted(x) for x in allp]
-
-    def arrange(key):
-        full = [base[i] + key[slot[i]] for i in range(n)]
-        seen, out = [False] * n, []
-        for i in sorted(range(n), key=lambda x: full[x]):
-            stack = [i]
-            while stack:
-                x = stack[-1]
-                if seen[x]:
-                    stack.pop()
-                    continue
-                todo = [j for j in plist[x] if not seen[j]]
-                if todo:
-                    stack += sorted(todo, key=lambda y: -full[y])
-                else:
-                    seen[x] = True
-                    out.append(x)
-                    stack.pop()
-        return out, full
-
-    best = (0, order)
-    for it in range(0):
-        held, why = now[int(rng.integers(len(cases)))][1:3]
-        new = list(key)
-        for rep in range(1 + int(rng.random() < 0.3)):
-            if held and rng.random() < 0.6:
-                j, i = held[int(rng.integers(len(held)))]
-            else:
-                i = int(rng.integers(n))
-                j = -2 - why[i] if why[i] < -1 else i
-            step = float(rng.random()) ** 2 * 2.0 + 0.001
-            if rng.random() < 0.6:
-                new[slot[i]] = full[j] - base[i] - step
-            else:
-                new[slot[j]] = full[i] - base[j] + step
-        trial, f2 = arrange(new)
-        res = [run(trial, d, w) for d, w in cases]
-        c = sum(x[0] for x in res)
-        if c <= cost + MARGIN * (1 - it / SHIFTS) * float(rng.random()):
-            key, full, now, cost = new, f2, res, c
-            if c < best[0]:
-                best = (c, trial)
-    order = best[1]
-    now = [run(order, d, w) for d, w in cases]
-    cost = sum(x[0] for x in now)
-    best = (cost, order)
-    for it in range(MOVES):
-        held, why = now[int(rng.integers(len(cases)))][1:3]
-        if held and rng.random() < 0.6:
-            j, i = held[int(rng.integers(len(held)))]
-        else:
-            i = int(rng.integers(n))
-            j = -2 - why[i]
-            if j < 0:
-                continue
-        a, b = order.index(j), order.index(i)
-        for hop in range(int(rng.integers(3))):
-            k = a - 1
-            while k >= 0 and queue[order[k]] != queue[j]:
-                k -= 1
-            if k >= 0:
-                a, j = k, order[k]
-        mid = order[a:b + 1]
-        if rng.random() < 0.5:
-            take = {i}
-            for x in reversed(mid):
-                if x in take:
-                    take |= allp[x]
-            if j in take:
-                continue
-            mid = [x for x in mid if x in take] + [x for x in mid if x not in take]
-        else:
-            take = {j}
-            for x in mid[1:]:
-                if allp[x] & take:
-                    take.add(x)
-            if i in take:
-                continue
-            mid = [x for x in mid if x not in take] + [x for x in mid if x in take]
-        trial = order[:a] + mid + order[b + 1:]
-        new = [run(trial, d, w) for d, w in cases]
-        c = sum(x[0] for x in new)
-        if c <= cost + MARGIN * (1 - it / MOVES) * float(rng.random()):
-            order, now, cost = trial, new, c
-            if c < best[0]:
-                best = (c, trial)
-    order = best[1]
-    extra, users = [], {}
-    for i in order:
-        for b in sorted(ops[i]["banks"]):
-            u = users.setdefault(b, {})
-            extra += [(i, j) for q, j in u.items() if q != ops[i]["q"]]
-            u[ops[i]["q"]] = i
-    return order, extra, best[0] / len(cases)
 
 
 def plan(ops, cases):
@@ -775,20 +458,20 @@ def plan(ops, cases):
     banks = [[names.index(b) for b in sorted(o["banks"])] for o in ops]
     pred = [sorted(o["d"]) for o in ops]
     hard = [o["hard"] for o in ops]
+    allp = [set(pred[i]) | set(hard[i]) for i in range(n)]
     isdma = [o["kind"] == "dma" for o in ops]
     succ = [[] for _ in range(n)]
     for i in range(n):
-        for j in set(pred[i]) | set(hard[i]):
+        for j in allp[i]:
             succ[j].append(i)
-    count = [len(set(pred[i]) | set(hard[i])) for i in range(n)]
     slots = {}
     slot = [slots.setdefault(o["slot"], len(slots)) for o in ops]
 
-    def run(dur, wake, order=None, rank=None):
+    def run(dur, wake, same, order=None, rank=None):
         end, why, issued, base, cause = [0.0] * n, [-1] * n, [0.0] * n, [0.0] * n, [-1] * n
         free, last, user = [0.0] * len(names), [-1] * len(names), [[] for _ in names]
-        need, out = list(count), []
-        ready = [i for i in range(n) if count[i] == 0]
+        need, out = [len(x) for x in allp], []
+        ready = [i for i in range(n) if need[i] == 0]
 
         def start(i):
             s, w, q = base[i], cause[i], queue[i]
@@ -823,8 +506,9 @@ def plan(ops, cases):
                 if need[k] == 0:
                     t, c = 0.0, -1
                     for j in pred[k]:
-                        if end[j] + wake > t:
-                            t, c = end[j] + wake, j
+                        e = end[j] + (same if queue[j] == queue[k] else wake)
+                        if e > t:
+                            t, c = e, j
                     for j in hard[k]:
                         if issued[j] > t:
                             t, c = issued[j], j
@@ -840,26 +524,36 @@ def plan(ops, cases):
             i = j
         return total, held, out
 
-    dur, wake = cases[0]
     way = [0.0] * n
     for sweep in range(4):
         for i in range(n - 1, -1, -1):
-            way[i] = dur[i] + max([way[k] + wake for k in succ[i]] + [0.0])
+            way[i] = cases[0][0][i] + max([way[k] + cases[0][1] for k in succ[i]] + [0.0])
 
     def judge(gain):
-        first = run(dur, wake, None, [way[i] + gain[slot[i]] for i in range(n)])
-        res = [first] + [run(d, w, first[2]) for d, w in cases[1:]]
+        first = run(*cases[0], None, [way[i] + gain[slot[i]] for i in range(n)])
+        res = [first] + [run(*c, first[2]) for c in cases[1:]]
         return sum(x[0] for x in res), res
 
     rng = np.random.default_rng(SEED)
     gain = [0.0] * len(slots)
+    for i in range(n):
+        gain[slot[i]] = URGENT.get(ops[i]["task"], 0.0)
     cost, now = judge(gain)
     best = (cost, now[0][2])
     for it in range(SHIFTS):
+        if it == SHIFTS * 2 // 3:
+            for i in range(n):
+                if ops[i]["step"] in (0, STEPS - 1):
+                    gain.append(gain[slot[i]])
+                    slot[i] = len(gain) - 1
         held = now[int(rng.integers(len(cases)))][1]
         new = list(gain)
         for rep in range(1 + int(rng.random() < 0.3)):
-            if held and rng.random() < 0.8:
+            if rng.random() < TASKS:
+                task, d = ops[int(rng.integers(n))]["task"], float(rng.normal())
+                for x in set(slot[i] for i in range(n) if ops[i]["task"] == task):
+                    new[x] += d
+            elif held and rng.random() < 0.8:
                 j, i = held[int(rng.integers(len(held)))]
                 gap = max(way[j] + gain[slot[j]] - way[i] - gain[slot[i]], 0.0) + float(rng.random())
                 if rng.random() < 0.5:
@@ -867,16 +561,34 @@ def plan(ops, cases):
                 else:
                     new[slot[j]] -= gap
             else:
-                new[int(rng.integers(len(slots)))] += float(rng.normal()) * 2
+                new[int(rng.integers(len(new)))] += float(rng.normal()) * 2
         c, res = judge(new)
         if c <= cost + MARGIN * (1 - it / SHIFTS) * float(rng.random()):
             gain, now, cost = new, res, c
             if c < best[0]:
                 best = (c, res[0][2])
-    return best[1]
-
-
-PLAN = {}
+    cost, order = best
+    now = [run(*c, order) for c in cases]
+    for it in range(MOVES):
+        held = now[int(rng.integers(len(cases)))][1]
+        j, i = held[int(rng.integers(len(held)))]
+        a, b = order.index(j), order.index(i)
+        take = {i}
+        for x in reversed(order[a:b + 1]):
+            if x in take:
+                take |= allp[x]
+        if j not in take:
+            trial = order[:a] + [x for x in order[a:b + 1] if x in take] + [x for x in order[a:b + 1] if x not in take] + order[b + 1:]
+            new = [run(*c, trial) for c in cases]
+            if sum(x[0] for x in new) <= cost:
+                order, now, cost = trial, new, sum(x[0] for x in new)
+    extra, users = [], {}
+    for i in order:
+        for b in sorted(ops[i]["banks"]):
+            u = users.setdefault(b, {})
+            extra += [(i, j) for q, j in u.items() if q != ops[i]["q"]]
+            u[ops[i]["q"]] = i
+    return order, extra, cost / len(cases)
 
 
 def rank_program(g, core, T, topo):
@@ -888,10 +600,10 @@ def rank_program(g, core, T, topo):
     if "order" not in PLAN:
         cases = []
         for c in CASES:
-            other = []
-            build(core, T, topo, other, dict(EST, **c))
-            cases.append(([o["dur"] for o in other], dict(EST, **c)["wake"]))
-        PLAN["order"] = improve(ops, plan(ops, cases), cases)
+            other, est = [], dict(EST, **c)
+            build(core, T, topo, other, est)
+            cases.append(([o["dur"] for o in other], est["wake"], est["same"]))
+        PLAN["order"] = plan(ops, cases)
     order = PLAN["order"][0]
     for i, j in PLAN["order"][1]:
         ops[i]["d"].add(j)

@@ -2,73 +2,87 @@ import numpy as np
 from concourse.mybir import AluOpType as A, ActivationFunctionType as F
 
 STEPS = 4
-CHUNKS = ((192, 256), (128, 192), (64, 128), (0, 64))
 PARTS = ((128, 256), (0, 128))
-TURNS = (("a0", "a1", "a2", "a3"), ("G0", "G2", "G3", "d0", "d1", "d2", "d3"))
-G_ON = "VSVV"
-ABS_ON = "VVSV"
-SUM_ON = "PV"
-X_SUB = (1, 1, 2, 2)
-Z_SUB = (1, 1, 2, 2)
-LR_CUT = 16
+G_CUT = ((208, 256, "V"), (128, 208, "S"), (64, 128, "V"), (32, 64, "V"), (0, 32, "S"))
+X_CUT = (((224, 256), (192, 224), (128, 192)), ((96, 128), (64, 96), (32, 64), (0, 32)))
+Z_CUT = (((192, 256, "S"), (128, 192, "V")), ((64, 128, "S"), (32, 64, "S"), (0, 32, "V")))
+U_CUT = (((128, 192, "D"), (128, 256, "Z")), ((0, 32, "D"), (0, 128, "Z")))
+HALF_ON = "S"
+SUM_ON = "PP"
+C_ON = "SSSS"
+E_ON = "VVS"
+LR_CUT = (8, 16)
+FAST = {0: "S", 1: "S"}
+AB_ON = ("SSVV", "VV")
+CS_ON = "S"
 YT_ON = "SVSSSS"
+TURN = """
+cU.gathers.1 jk.place1.1+ sL.place1.1+ G.gathers.2 G.gathers.1 b0.gathers.1 sU.place1.1+ cU.gathers.2 sF.gathers.1 G.gathers.5 GT.gathers.1 b1.gathers.1 AB.gathers.1
+G.gathers.3 accB.place1.1+ XX.X1.2+ GT.gathers.2 b0.gathers.2 G.gathers.4 AB.gathers.2 Xa.var0.1 Xa.var0.2 b1.gathers.2 cF.gathers.1 GT.gathers.3 b1.gathers.3 D.var0.1
+AB.gathers.3 b4.E.1 Xa.var0.3 c0.E.1 D.var0.2 D.var0.3 Xa.var1.1 D.var1.1 rE.E.1 Z.var0.2 Xa.var1.2 Z.var0.1 c1.E.1 D.var1.2 Xa.var1.3 Xa.var1.4 b4.E.2 D.var1.3 b2.var0.2
+b2.var0.3 rq.claim0.1 yT.claim0.1 b2.claim0.1 D.var1.4 Z.var1.2 sq.claim0.1 tb.claim0.1 Fc.claim0.1 b3.var1.2 Z.var1.3 b0.tables0.1 c0.tables0.1 Z.var1.1 XC.x.2+
+Qt0.tables0.1 b3.var1.3 Qt0.tables0.4 Qt0.tables0.2 rq.claim1.1 Qt0.tables0.3 b2.tables0.1 b0.fork0.1 b4.lowest0.1 c0.lists0.1 Qt0.tables0.5 yT.claim1.1 b3.claim1.1
+b2.lowest0.1 O2.fork0.1 cs.fork0.1 O.lowest0.1 JC1.column0.1 sq.claim1.1 tb.claim1.1 xt.x.1+ old.column0.1 Qt1.tables1.1 c0.lists0.2 c0.lists0.3 yi.X0.1 b0.column0.1
+EQ.lowest0.3 Fc.claim1.1 XLU.x.1+ EQ.lowest0.4 EQ.lowest0.1 cs.fork0.2 EQ.lowest0.2 c1.tables1.1 JU0.X0.1 zz.X0.1 Qt1.tables1.3 Qt1.tables1.2 b3.tables1.1 Qt1.tables1.5
+lose.lowest0.2 b1.tables1.1 b1.fork1.1 lose.lowest0.1 nc.column0.1 O2.fork1.1 b4.lowest1.1 O.lowest1.1 nd.column0.1 c1.lists1.1 sc.lowest0.1 JC1.column1.1 b3.lowest1.1
+Y.x.2+ EQ.lowest1.4 EQ.lowest1.3 Qt1.tables1.4 cs.fork0.3 EQ.lowest1.2 EQ.lowest1.1 c1.lists1.2 cs.fork1.1 cs.fork1.3 old.column1.1 posU.lowest0.1 XC.x.1+ XC.x.3+
+m0.fork0.1 lose.lowest1.1 lose.lowest1.2 rcv.fork0.1 JU1.X1.1 b1.column1.1 nc.column1.1 Si.S.1 sc.lowest1.1 nd.column1.1 Si.S.2 posU.lowest1.1 b3.var1.1- y7.X0.1
+rcv.fork1.1 m1.place0.1 b2.var0.1- Si.S.3 zz.X1.1 WLU.X0.1 sL.place0.1 b0.x.1 Y.x.1 cs.fork1.2 yi.X1.1 Si.S.4 y7.X1.1 XX.X0.1 XX.X0.2 sU.place0.1 m0.fork1.1 WLU.X1.1
+b1.x.1 XX.X1.1 m1.place1.1 ha.x.1
+"""
 MAGIC = 12582912.0
-NT = 8
+HIGH = 65536.0
+CEIL = 61440.0
+SPARE = 256
+X0 = 8192
+NT = 6
 
 SCRATCH = {
-    "Si": ("sbuf", [128, 4352], "int32"),
-    "XX": ("sbuf", [128, 8192], "bfloat16"),
+    "Si": ("sbuf", [128, SPARE + 4096 + 272], "int32"),
+    "XX": ("sbuf", [128, X0 + 4096], "bfloat16"),
     "XC": ("sbuf", [128, (STEPS + 1) * 768], "bfloat16"),
-    "L": ("psum", [128, 32, 16], "float32"),
-    "b4": ("psum", [128, 512], "float32"),
+    "c0": ("psum", [128, 64, 8], "float32"),
+    "c1": ("psum", [128, 64, 8], "float32"),
 }
 for _dt, _shapes in (
-        ("bfloat16", {"Xa": [4096], "on": [256], "SEL": [16, 2, 8], "ER": [16, 128], "LR": [16, 8, 16], "WG": [2, 8], "PM": [4, 4, 32], "PF": [2, 128],
-                      "UK": [4, 4, 32], "BI": [128], "BM": [4, 32], "Id": [4, 32], "CNT": [128], "CN1": [128], "CN2": [128], "mat": [8, 128],
-                      "con": [5, 256], "RM": [256], "RS": [384], "jk": [16], "eq": [768], "lose": [768], "zz": [512], "Y": [STEPS, 256],
+        ("bfloat16", {"Xa": [4096], "on": [256], "SEL": [16, 2, 8], "ER": [16, 128], "LR": [16, 8, 16], "WG": [2, 8], "PM": [4, 4, 32],
+                      "BI": [128], "BM": [4, 32], "Id": [4, 32], "CNT": [128], "mat": [16, 128], "con": [2, 256], "low": [256], "RM": [128], "jk": [16],
+                      "EQ": [4, 256], "lose": [4, 256], "DM": [256], "zz": [512], "Y": [STEPS, 256],
                       "D0": [4096], "D1": [4096], "Z0": [4096], "Z1": [4096]}),
-        ("float16", {"G": [4096], "S16": [4096], "GT": [512], "yT": [256], "JC": [NT, 16], "sF": [16], "accB": [128], "cF": [256], "rq": [256],
-                     "old": [256], "ch": [2, 16], "Fc": [256], "c47": [256], "Qt0": [4 * NT, 2, 16], "Qt1": [4 * NT, 2, 16]}),
-        ("float32", {"r256": [256], "KT": [2, 16], "EQ": [16], "q16": [16], "Ic": [16], "I8": [16], "w8": [16], "col": [8], "m0": [16], "hm": [2, 16], "old2": [256],
-                     "RT": [4, 2, 32], "dump": [16], "ha": [256], "ysum": [1024], "yto": [256], "yso": [16], "rcv": [STEPS, 16],
-                     "cs0": [2 * STEPS, 8], "cs1": [2 * STEPS, 8]}),
-        ("int32", {"pI": [4], "wI": [1], "sL0": [16], "sL": [16], "m1": [16], "yi": [16], "y7": [16], "xt": [16], "ei": [256], "em": [256], "sq": [256], "tb": [256],
+        ("float16", {"G": [4096], "S16": [4096], "GT": [512], "yT": [256], "JC": [NT, 16], "JK": [2, 16], "sF": [16], "accB": [128], "cF": [256], "rq": [256],
+                     "rE": [256], "RK": [3, 128], "old": [256], "Fc": [256], "Qt0": [4 * NT, 2, 16], "Qt1": [4 * NT, 2, 16]}),
+        ("float32", {"r256": [256], "EQc": [16], "q16": [16], "Ic": [16], "I8": [16], "col": [8], "m0": [16], "O": [4, 4, 16], "O2": [128], "sc": [16], "dump": [16], "ha": [256],
+                     "ysum": [1024], "yto": [256], "yso": [16], "rcv": [STEPS, 16], "cs": [2 * STEPS, 2, 8]}),
+        ("int32", {"pI": [4], "wI": [1], "sL0": [16], "sL": [16], "m1": [16], "yi": [16], "y7": [16], "xt": [16], "sq": [256], "tb": [256],
                    "nc": [256], "nd": [256]}),
-        ("uint16", {"AB": [512], "sU": [16], "WLU": [16], "XLU": [16], "posU": [16], "cU": [256], "JU0": [24], "JU1": [24]})):
+        ("uint16", {"AB": [512], "sU": [16], "WLU": [16], "XLU": [16], "posU": [16], "cU": [256], "JC1": [16], "JU0": [16], "JU1": [16]})):
     for _nm in _shapes:
         SCRATCH[_nm] = ("sbuf", [128] + _shapes[_nm], _dt)
-for _b in (0, 1, 2, 3, 5, 7):
+for _b in (0, 1, 4):
     SCRATCH["b%d" % _b] = ("psum", [128, 16, 2, 16], "float32")
+for _b in (2, 3):
+    SCRATCH["b%d" % _b] = ("psum", [128, 8, 4, 16], "float32")
 
-SEMAPHORES = ["eV", "eS", "eP", "eG"] + ["m%d" % i for i in range(16)]
+SEMAPHORES = ["eV", "eS", "eP", "eG", "ax%d" % STEPS, "lx%d" % STEPS] + ["m%d" % i for i in range(20)]
 for _t in range(STEPS):
     for _nm in ("x%d" % _t, "n%d_0" % _t, "n%d_1" % _t):
         SEMAPHORES += ["a" + _nm, "l" + _nm]
 
-EST = {"cyc": 0.00083 * 1.05, "V": 0.02, "S": 0.04, "ind": 0.12, "ga": 1.2, "sc": 3.5, "pe": 0.00063, "wake": 0.14, "same": 0.19, "net": 3.2, "dma": 1.3, "rate": 350e3}
-CASES = ({}, {"cyc": 0.00083 * 1.4, "pe": 0.00085, "ga": 1.35}, {"net": 3.8, "ga": 1.05, "cyc": 0.00083})
-REACH = 0.5
-URGENT = {"fork0": 4.0, "fork1": 4.0, "claim0": 4.0, "tables0": 4.0, "lists0": 4.0, "lists1": 2.0}
-SEED = 4
-SHIFTS = 4500
-TASKS = 0.2
-MOVES = 300
-MARGIN = 0.9
+EST = {"cyc": 0.00083 * 1.05, "V": 0.02, "S": 0.04, "ind": 0.12, "ga": 1.2, "sc": 3.5, "pe": 0.0005, "wake": 0.14, "same": 0.19, "net": 3.2, "dma": 1.3, "rate": 350e3}
+CASES = ({}, {"cyc": 0.00083 * 1.4, "pe": 0.0007, "ga": 1.35}, {"net": 3.8, "ga": 1.05, "cyc": 0.00083})
+SEED = 1
+ROUNDS = (2500, 8000)
+MARGIN = 0.4
 EARLY = 0.1
 COLUMNS = {}
 PLAN = {}
 SIZE = {"float32": 4, "int32": 4, "bfloat16": 2, "float16": 2, "uint16": 2}
 
 
-def pieces(lo, hi, k):
-    w = (hi - lo) // k
-    return [(hi - w * (j + 1), hi - w * j) for j in range(k)]
-
-
 def build(core, T, topo, ops, EST):
     rank = T.rank_of(core)
     cyc = EST["cyc"]
-    times, now = {}, [-1, "start"]
+    times, now, group = {}, [-1, "start"], {}
 
     def at(name, *idx):
         where, shape, dt = SCRATCH[name]
@@ -91,9 +105,10 @@ def build(core, T, topo, ops, EST):
         r = [x["acc"] for x in ins if isinstance(x, dict)] + [x["off"] for x in ins + outs if isinstance(x, dict) and x["off"]]
         w = [x["acc"] for x in outs]
         banks = set(x["acc"][0] for x in ins + outs if isinstance(x, dict) and x["ps"])
-        sig = (q, now[0] < 0) + tuple(x[0].rstrip("01") if x[0][0] in "DZ" else x[0] for x in w + r)
-        times[sig] = times.get(sig, 0) + 1
-        ops.append({"slot": (sig, times[sig]), "task": now[1], "step": max(now[0], 0), "q": q, "fn": fn, "dur": dur, "r": r, "w": w,
+        buf = (w + r)[0][0]
+        name = "%s.%s" % (buf[0] if buf in ("D0", "D1", "Z0", "Z1") else buf, now[1])
+        times[name] = times.get(name, 0) + 1
+        ops.append({"slot": "%s.%d" % (name, times[name]), "task": now[1], "step": max(now[0], 0), "q": q, "fn": fn, "dur": dur, "r": r, "w": w,
                     "kind": kind, "sem": sem, "cnt": cnt, "banks": banks, "hard": []})
 
     def time(q, out, i0, per):
@@ -115,6 +130,12 @@ def build(core, T, topo, ops, EST):
 
     def fill(out, c):
         add("V", lambda e: e.memset(val(out), c), time("V", out, out, 0.5 if out["two"] else 1), [out], [])
+
+    def turn32(out, i0):
+        add("V", lambda e: e.transpose(val(out), val(i0)), time("V", out, i0, 1), [out], [i0])
+
+    def scan(out, i0, i1):
+        add("V", lambda e: e.tensor_tensor_scan(val(out), val(i0), val(i1), 0.0, A.max, A.mult), time("V", out, out, 0.5), [out], [i0, i1])
 
     def act(out, i0, f, acc=None, **k):
         kw = {n: val(v) for n, v in k.items()}
@@ -142,8 +163,15 @@ def build(core, T, topo, ops, EST):
                 last = e.matmul(val(c[0]), val(c[1]), val(c[2]), first[j], first[j + 1])
             return last
         outs = [c[0] for c in calls]
-        add("P", run, 0.03 + EST["pe"] * sum(max(64, c[2]["n"]) for c in calls), outs, [c[1] for c in calls] + [c[2] for c in calls] + ([] if start else outs))
+        add("P", run, 0.03 + EST["pe"] * sum(max(min(64, c[1]["n"]), c[2]["n"]) for c in calls), outs,
+            [c[1] for c in calls] + [c[2] for c in calls] + ([] if start else outs))
         ops[-1].update({"goes on": not start, "open": not stop})
+        closed, since = group.setdefault(outs[0]["acc"][0], [[], []])
+        if start:
+            ops[-1]["hard"] += closed + ([] if stop else since)
+            since.append(len(ops) - 1)
+        elif stop:
+            closed[:], since[:] = [len(ops) - 1], []
 
     def asel(out, i0, pat, op, base, cm):
         add("G", lambda e: e.affine_select(val(out), val(i0), pat, op, 0.0, base, cm), 0.17 + 2 * cyc * out["n"], [out], [i0])
@@ -169,17 +197,17 @@ def build(core, T, topo, ops, EST):
         ops[-1]["hard"].append(len(ops) - 2)
 
     dma(at("sL0"), T.s0[:])
-    dma(at("Si", (0, 4096)), T.stm[:])
+    dma(at("Si", (SPARE, SPARE + 4096)), T.stm[:])
     dma(at("wI"), T.wt[:], 6.0)
-    dma(at("XX", (0, 2048)), T.vx[:], 6.0)
-    dma(at("XX", (2048, 4096)), T.vx[:], 7.5)
-    dma(at("XC", (0, 256)), T.x0[:], 8.0)
+    dma(at("XX", (X0, X0 + 2048)), T.vx[:], 6.0)
+    dma(at("XX", (X0 + 2048, X0 + 4096)), T.vx[:], 7.5)
+    dma(at("XC", (512, 768)), T.x0[:], 8.0)
     for j in range(1, len(ops)):
         ops[j]["hard"].append(j - 1)
 
     Id, BM, on = at("Id"), at("BM"), at("on", (0, 128))
-    kcol, row0, c16, wF, acc, kfr, cm99 = [at("col", (j, j + 1)) for j in (0, 2, 3, 4, 5, 6, 7)]
-    IdK, Id5, IdN, IdH, IdM, IdC, IdT = [at("mat", j) for j in range(7)]
+    kcol, row0, c16, wF, acc, kap, kb = [at("col", (j, j + 1)) for j in (0, 2, 3, 4, 5, 6, 7)]
+    IdK, Id5, IdN, IdH, Id16, IdN16, IdJ, IdR, IdC, CA, CB, K1, K2, t0, t1 = [at("mat", j) for j in range(15)]
     fill(at("on"), 1.0)
     iota(at("pI", (0, 1)), [[0, 1]], 1)
     iota(at("q16"), [[16, 16]], 0, allow_small_or_imprecise_dtypes=True)
@@ -192,225 +220,238 @@ def build(core, T, topo, ops, EST):
     asel(at("SEL", (0, 16), 1), on, [[-2, 8], [1, 2], [-16, 8]], A.is_equal, -1, 1)
     ts(at("pI", (2, 3)), at("pI", (0, 1)), 15, A.bitwise_and)
     cp(kcol, at("pI", (2, 3)))
-    ts(row0, kcol, 0.0, A.is_equal, 4096.0, A.mult)
-    ts(kfr, kcol, 1.0 / 4096, A.mult)
+    ts(row0, kcol, 0.0, A.is_equal)
+    ts(kap, row0, -2.0, A.mult, -384.0, A.add)
+    ts(kb, kcol, -128.0, A.add)
     fill(c16, 16.0)
-    fill(cm99, -99.0 * 4096)
     cp(wF, at("wI"))
-    ts(at("EQ"), at("r256", (0, 16)), kcol, A.is_equal)
+    ts(at("EQc"), at("r256", (0, 16)), kcol, A.is_equal)
     fill(at("LR"), 0.0)
     for r in range(16):
-        ts(at("ER", r), BM, at("EQ", (r, r + 1)), A.mult)
+        ts(at("ER", r), BM, at("EQc", (r, r + 1)), A.mult)
         act(at("LR", r, (0, 8), r), at("BM", (0, 4), (0, 32, 16)), F.Copy)
     for j in range(2):
         ts(at("WG", j), at("BM", (0, 4), (0, 32, 16)), wF, A.mult, (1.0 - 2 * j) / 4096, A.mult)
-    for m, f in ((IdK, 1.0 / 4096), (Id5, 5.0), (IdN, -1.0), (IdH, 0.5), (IdM, -100.0), (IdT, -2.0)):
+    for m, f in ((IdK, 4096.0), (Id5, 5.0), (IdN, -1.0), (IdH, 0.5), (Id16, 16.0), (IdN16, -16.0), (IdJ, 1024.0), (IdR, 2304.0)):
         act(m, Id, F.Copy, scale=f)
-    tt(at("CN2"), at("CNT"), IdM, A.add)
     tt(IdC, Id, at("CNT"), A.subtract)
-    act(at("CN1"), IdC, F.Copy, scale=4096.0)
-    act(at("c47"), at("on", (0, 256)), F.Copy, scale=-2047.0)
-    for j, c in enumerate((-1.0, 1024.0, -0.5, 6144.0, 4096.0 * len(YT_ON))):
+    act(CA, IdC, F.Copy, scale=-HIGH)
+    act(K1, IdC, F.Copy, scale=128.0)
+    tt(t0, Id, IdC, A.add)
+    act(CB, t0, F.Copy, scale=-HIGH)
+    ts(t1, at("r256", (0, 128)), -1.0, A.mult, 32.0, A.add)
+    tt(t0, t1, IdC, A.mult)
+    act(t1, Id, F.Copy, scale=128.0)
+    tt(K2, t0, t1, A.add)
+    for j, c in enumerate((-0.5, 4096.0 * len(YT_ON))):
         fill(at("con", j), c)
-    ts(at("RM"), at("r256"), kcol, A.is_ge, 0.5, A.mult)
-    fill(at("RS"), 1.0)
-    fill(at("RS", (0, 384, 32)), 0.0)
+    fill(at("low"), HIGH)
+    fill(at("RK", 0), 0.5)
+    fill(at("RK", 2), -399.0)
+    ts(at("RM"), at("r256", (0, 128)), kcol, A.is_ge, 2.0, A.mult)
+    ts(at("RK", 1), at("RM"), -399.0, A.add)
+    ts(at("Ic"), at("q16"), kcol, A.add)
+    ts(at("dump"), at("Ic"), SPARE + 4096.0, A.add)
+    fill(at("EQ"), 0.0)
+    fill(at("DM"), 1.0)
+    fill(at("DM", (63, 256, 64)), -8192.0)
     fill(at("PM"), 0.0)
-    fill(at("UK"), 0.0)
     for a in range(2):
         for b in range(2):
             act(at("PM", 2 * a + b, (0, 4), (16 * b, 16 * b + 16)), at("BM", (0, 4), (16 * a, 16 * a + 16)), F.Copy)
-            act(at("UK", 2 * a + b, (0, 4), (16 * b, 16 * b + 16)), at("Id", (0, 4), (16 * a, 16 * a + 16)), F.Copy, scale=16384.0)
-    for a in range(2):
-        tt(at("PF", a), at("PM", 2 * a), at("PM", 2 * a + 1), A.add)
-    ts(at("Ic"), at("q16"), kcol, A.add)
-    ts(at("dump"), at("Ic"), 4096.0, A.add)
-    for j, (f, c) in enumerate(((16.0, 0.0), (16.0, 0.0), (0.0, 32768.0), (0.0, 2048.0), (0.0, 0.0), (0.0, 0.0), (0.0, 14336.0), (0.0, 0.0))):
-        ts(at("JC", j), at("Ic"), f, A.mult, c, A.add)
-    ts(at("I8"), at("Ic"), 8.0, A.mult, 4096.0, A.add)
-    for j, c in enumerate((16.0, 8.0)):
-        fill(at("KT", j), c)
-    act(at("accB"), on, F.Copy, scale=-0.0625)
+    fork0 = 4096 + 61440 - 14 * CEIL
+    for j, c in enumerate((10240 - 15 * CEIL, 2048 + 28672 - 15 * CEIL, 0.0, 0.0, fork0, 69632.0 + 10240)):
+        fill(at("JC", j), c / 1024)
+    for j in range(2):
+        ts(at("JK", j), at("Ic"), -2.0 * j, A.add)
+    ts(at("I8"), at("Ic"), 8.0, A.mult)
+    act(at("accB"), on, F.Identity, scale=kap)
     cp(at("sU"), at("sL0"))
 
-    swin, xwin = at("Si", (0, 4096)), at("XX", (0, 4096))
+    swin, xwin = at("Si", (SPARE, SPARE + 4096)), at("XX", (X0, X0 + 4096))
 
     def step(t):
         last = t + 1 == STEPS
         D, Z = "D%d" % (t % 2), "Z%d" % (t % 2)
         x0 = 768 * t
-        tag = {}
+        turn = {"V": [], "S": []}
         now[:] = [t, "gathers"]
         times.clear()
         dst = T.cores[(rank + 1 + t % (len(T.cores) - 1)) % len(T.cores)]
-        for lo, hi in PARTS:
-            act(at("cU", (lo, hi)), ind(swin, at("sU", (lo // 16, hi // 16))), F.Copy)
-        plus("S", at("sF", (0, 16)), at("sU", (0, 16)), -2048.0)
-        plus("S", at("cF", (0, 256)), at("cU", (0, 256)), -2048.0)
-        for ch, (lo, hi) in enumerate(CHUNKS):
-            plus(G_ON[ch], at("G", (16 * lo, 16 * hi)), ind(swin, at("cU", (lo, hi))), -2048.0)
-            tag["G%d" % ch] = [len(ops) - 1]
-        E = at("b4", (0, 256))
-        mms([(E, IdN, at("cF", (0, 256))), (E, at("accB"), at("con", 0, (0, 256)))] + [(at("b4", (r, 256, 16)), at("ER", r), at("sF", (0, 16))) for r in range(16)])
-        act(at("ei"), E, F.Copy)
-        ts(at("em"), at("ei"), 15, A.bitwise_and)
-        act(E, at("em"), F.Copy)
-        mms([(at("b5", (0, 8)), IdK, at("cF", (0, 256)))])
+        for gi, (lo, hi) in enumerate(PARTS):
+            plus(C_ON[gi], at("cU", (lo, hi)), ind(swin, at("sU", (lo // 16, hi // 16))), 0.0)
+        plus(E_ON[0], at("sF", (0, 16)), at("sU", (0, 16)), -2048.0)
+        plus(E_ON[1], at("cF", (0, 256)), at("cU", (0, 256)), -2048.0)
+        for lo, hi, q in G_CUT:
+            plus(q, at("G", (16 * lo, 16 * hi)), ind(swin, at("cU", (lo, hi))), -2048.0)
+            turn[q].append(len(ops) - 1)
+        now[1] = "E"
+        E = at("b4", (0, 8))
+        whole = [(E, IdN, at("cF", (0, 256))), (E, at("accB"), at("con", 0, (0, 256)))]
+        whole += [(at("b4", (0, 8), (0, 2), r), at("ER", r), at("sF", (0, 16))) for r in range(16)]
+        mms(whole)
+        if E_ON[2] == "S":
+            act(at("rE"), E, F.Identity, scale=1.0 / 16, bias=-15.0 / 32)
+        else:
+            ts(at("rE"), E, 1.0 / 16, A.mult, -15.0 / 32, A.add)
+        mms(whole + [(E, IdN16, at("rE"))])
+        for gi, (lo, hi) in enumerate(PARTS):
+            mms([(at("c%d" % gi, (0, 32)), Id, at("low"))] + [(at("c%d" % gi, (16 * j, 16 * j + 16)), Id, at("cF", (lo, hi))) for j in range(2)], True, False)
 
         def gathers(gi):
+            now[1] = "gathers"
             lo, hi = PARTS[gi]
             bank, ub, o = "b%d" % gi, "b%d" % (2 + gi), 2 * lo
             ps = at(bank, (0, 8))
             mms([(at(bank, (0, 8), (0, 2), k), at("G", (16 * lo + k, 16 * hi, 16)), at("SEL", k)) for k in range(16)])
-            act(at("GT", (o, o + 256)), ps, F.Copy)
-            mms([(at(bank, (4 * j, 4 * j + 4)), at("GT", (o + 128 * j, o + 128 * j + 128)), Id) for j in range(2)])
-            plus("S", at("AB", (o, o + 256)), ps, 2048.0)
-            mine = [ch for ch in range(len(CHUNKS)) if lo <= CHUNKS[ch][0] < hi]
-            for ch in mine:
-                for c0, c1 in pieces(CHUNKS[ch][0], CHUNKS[ch][1], X_SUB[ch]):
-                    a, b = 16 * c0, 16 * c1
-                    act(at("Xa", (a, b)), ind(xwin, at("AB", (lo + c0, lo + c1))), F.Copy)
-                    tag.setdefault("a%d" % ch, []).append(len(ops) - 1)
-                    tt(at(D, (a, b)), ind(xwin, at("AB", (hi + c0, hi + c1))), at("Xa", (a, b)), A.subtract)
-                    tag.setdefault("d%d" % ch, []).append(len(ops) - 1)
-                for c0, c1 in pieces(CHUNKS[ch][0], CHUNKS[ch][1], Z_SUB[ch]):
-                    a, b = 16 * c0, 16 * c1
-                    if ABS_ON[ch] == "V":
-                        ts(at(Z, (a, b)), at(D, (a, b)), 0.0, A.max, 2.0, A.mult)
-                    else:
-                        act(at(Z, (a, b)), at(D, (a, b)), F.Abs)
-            relu = [CHUNKS[ch] for ch in mine if ABS_ON[ch] == "V"]
-            pre = [(at(ub, (0, 4)), Id, at("con", 1, (0, 128)))]
-            c0, c1 = min(c[0] for c in relu), max(c[1] for c in relu)
-            for k in range(16):
-                out = at(ub, (0, 4), (0, 2), k)
-                pre.append((dict(out, ap=T[ub][c0 - lo:c1 - lo, 0:4, 0:2, k]), at(D, (16 * c0 + k, 16 * c1, 16)), at("WG", 1)))
-            mms(pre, True, False)
-            ops[-1]["r"].append(at(ub, (4, 16))["acc"])
-            mms([(at(ub, (0, 4), (0, 2), k), at(Z, (16 * lo + k, 16 * hi, 16)), at("WG", 0)) for k in range(16)], False, True)
+            if len(AB_ON[gi]) == 2:
+                plus(AB_ON[gi][0], at("GT", (o, o + 256)), ps, 0.0)
+                mms([(at(bank, (4 * j, 4 * j + 4)), at("GT", (o + 128 * j, o + 128 * j + 128)), Id) for j in range(2)])
+                plus(AB_ON[gi][1], at("AB", (o, o + 256)), ps, 2048.0)
+            else:
+                for j in range(2):
+                    gt, wide = at("GT", (o + 128 * j, o + 128 * j + 128)), at("b%d" % (gi if j else 1 - gi), (0, 4))
+                    plus(AB_ON[gi][2 * j], gt, at(bank, (4 * j, 4 * j + 4)), 0.0)
+                    mms([(wide, gt, Id)])
+                    plus(AB_ON[gi][2 * j + 1], at("AB", (o + 128 * j, o + 128 * j + 128)), wide, 2048.0)
+            now[1] = "var%d" % gi
+            for c0, c1 in X_CUT[gi]:
+                a, b = 16 * c0, 16 * c1
+                act(at("Xa", (a, b)), ind(xwin, at("AB", (lo + c0, lo + c1))), F.Copy)
+                turn["S"].append(len(ops) - 1)
+                tt(at(D, (a, b)), ind(xwin, at("AB", (hi + c0, hi + c1))), at("Xa", (a, b)), A.subtract)
+                turn["V"].append(len(ops) - 1)
+            for c0, c1, q in Z_CUT[gi]:
+                a, b = 16 * c0, 16 * c1
+                if q == "V":
+                    ts(at(Z, (a, b)), at(D, (a, b)), 0.0, A.max, 2.0, A.mult)
+                else:
+                    act(at(Z, (a, b)), at(D, (a, b)), F.Abs)
+            mms([(at(ub, (0, 2)), IdR, at("RK", 0))], True, False)
+            for j, (c0, c1, src) in enumerate(U_CUT[gi]):
+                sums = [(dict(at(ub, (0, 2), (0, 4), k), ap=T[ub][c0 - lo:c1 - lo, 0:2, 0:4, k]), at(D if src == "D" else Z, (16 * c0 + k, 16 * c1, 16)),
+                         at("WG", int(src == "D"))) for k in range(16)]
+                end = j + 1 == len(U_CUT[gi])
+                if end and c1 - c0 < hi - lo:
+                    sums.append((at(ub, (0, 2), (0, 4), 15), Id, at("JC", 2, (0, 8))))
+                mms(sums, False, end)
 
         def claims(gi):
             lo, hi = PARTS[gi]
-            q0, q1, b0, b1, nb, m, w = lo // 16, hi // 16, lo // 32, hi // 32, (hi - lo) // 32, (hi - lo) // 16, hi - lo
-            Qt, JU, cs, ub = "Qt%d" % gi, "JU%d" % gi, "cs%d" % gi, "b%d" % (2 + gi)
+            q0, q1, k0, k1 = lo // 16, hi // 16, lo // 64, hi // 64
+            Qt, JU, ub, bank = "Qt%d" % gi, "JU%d" % gi, "b%d" % (2 + gi), "b%d" % gi
             h = lambda nm: at(nm, (lo, hi))
             q = lambda nm: at(nm, (q0, q1))
-            qt = lambda j, k=1: at(Qt, (j * nb, (j + k) * nb))
-            L = lambda j, k=1: at("L", (j, j + k), (q0, q1))
-            y = at(ub, (0, nb))
+            qt = lambda j, k=1: at(Qt, (4 * j, 4 * (j + k)))
+            cb = "c%d" % gi
+            L = lambda j, k=1: at(cb, (32 + j, 32 + j + k))
+            y, y1 = at(ub, (0, 2)), at(ub, (2, 4))
             now[1] = "claim%d" % gi
             act(h("rq"), y, F.Copy)
             tt(h("yT"), y, h("rq"), A.subtract)
-            mms([(y, h("yT"), Id)])
-            act(h("sq"), y, F.Square, scale=4096.0, bias=c16)
+            mms([(y, h("yT"), IdK)])
+            act(h("sq"), y, F.Square, bias=c16)
             ts(h("tb"), h("sq"), 5, A.arith_shift_right, 15, A.bitwise_and)
-            tt(h("Fc"), h("tb"), h("b4"), A.is_equal)
+            tt(h("Fc"), h("tb"), at("b4", (lo // 32, hi // 32)), A.is_equal)
             now[1] = "tables%d" % gi
-            s1, s2 = at("b0", (8 + b0, 8 + b1)), at("b1", (8 + b0, 8 + b1))
-            mms([(s1, at("CN2"), h("Fc"))])
-            mms([(s2, at("CN2"), h("Fc"))])
-            act(qt(4), s1, F.Relu, scale=-4096.0, bias=cm99)
-            ts(qt(5), s2, -99.0, A.is_equal, 4096.0, A.mult)
-            act(qt(6), y, F.Copy, scale=row0)
-            s3 = at("b5", (8 + b0, 8 + b1))
-            mms([(s3, Id, h("cF")), (s3, Id, at("c47", (lo, hi))), (s3, at("CN1"), h("Fc"))])
-            ts(qt(2), s3, 0.0, A.max, -2048.0, A.add)
-            tt(qt(3), qt(5), at("b5", (b0, b1)), A.mult)
-            tt(qt(7), qt(4), y, A.mult)
-            act(qt(0, 2), qt(4, 2), F.Copy, scale=kfr)
-            now[1] = "lowest%d" % gi
-            R = at("b4", (256 + lo, 256 + hi))
-            mms([(R, BM, qt(2))])
-            B0, B1 = at("b7", (b0, b1)), at("b7", (8 + b0, 8 + b1))
-            mms([(B0, Id, h("RM"))] + [(at("b7", (b0, b1), a), at("PM", 2 * a + b), at(Qt, (2 * nb, 3 * nb), b)) for a in range(2) for b in range(2)] +
-                [(at("b7", (8 + b0, 8 + b1), a), at("PM", 2 * a + 1), at(Qt, (2 * nb, 3 * nb), 0)) for a in range(2)])
-            mms([(at(ub, (nb + b * nb // 2, nb + (b + 1) * nb // 2), a), at("PF", a), at(Qt, (2 * nb, 3 * nb, 2), b)) for b in range(2) for a in range(2)])
+            act(qt(5), y, F.Copy, scale=row0)
+            mms([(at(cb, (0, 16)), CA, h("Fc")), (at(cb, (16, 32)), CB, h("Fc"))], False)
+            ts(qt(1), at(cb, (0, 16)), CEIL, A.min)
+            ts(qt(4), at(cb, (16, 32)), CEIL, A.min, -2048.0, A.max)
+            mms([(at(bank, (8, 12)), K1, h("Fc")), (at(bank, (12, 16)), K2, h("Fc"))])
+            act(qt(2, 2), at(bank, (8, 16)), F.Relu, bias=kb)
+            mms([(y1, h("yT"), IdK), (y1, CA, h("Fc"))])
+            ts(qt(0), y1, HIGH, A.add, CEIL, A.min)
             now[1] = "lists%d" % gi
-            mms([(L(0, NT), Id, at("JC", (0, NT), (q0, q1))), (L(6), Id5, q("sF")), (L(2), IdN, at("on", (0, m)))], True, False)
-            ops[-1]["r"].append(at("L", (0, NT), (q1, 16) if gi else (0, q0))["acc"])
-            for r0 in range(0, 16, LR_CUT):
-                mms([(L(0, NT), at("LR", r), at(Qt, (0, NT * nb), (0, 2), r)) for r in range(r0, r0 + LR_CUT)], False, r0 + LR_CUT == 16)
+            mms([(L(0, NT), IdJ, at("JC", (0, NT), (q0, q1))), (L(2, 2), Id16, at("JK", (0, 2), (q0, q1))), (L(5), Id5, q("sF"))], True, False)
+            for r0 in range(0, 16, LR_CUT[gi]):
+                mms([(L(0, NT), at("LR", r), at(Qt, (0, 4 * NT), (0, 2), r)) for r in range(r0, r0 + LR_CUT[gi])], False, r0 + LR_CUT[gi] == 16)
             now[1] = "lowest%d" % gi
-            plus("S", at("ch", (0, 2), (q0, q1)), at("L", (2, 5, 2), (q0, q1)), -2048.0)
-            RT = at("RT", (lo // 64, hi // 64))
-            add("V", lambda e: e.transpose(val(RT), val(R)), time("V", RT, R, 1), [RT], [R])
-            e0 = 3 * lo
-            tt(at("eq", (e0, e0 + 2 * w, 2)), RT, B0, A.is_equal)
-            tt(at("eq", (e0 + 1, e0 + 2 * w, 2)), RT, B1, A.is_equal)
-            for b in range(2):
-                tt(at("eq", (e0 + 2 * w + b, e0 + 3 * w, 2)), at("RT", (lo // 64, hi // 64), 1), at(ub, (nb + b * nb // 2, nb + (b + 1) * nb // 2)), A.is_equal)
-            lose, eq, rs = at("lose", (e0, e0 + 3 * w)), at("eq", (e0, e0 + 3 * w)), at("RS", (0, 3 * w))
-            add("V", lambda e: e.tensor_tensor_scan(val(lose), val(rs), val(eq), 0.0, A.mult, A.max), time("V", lose, lose, 0.5), [lose], [rs, eq])
-            P = at("b1", 0, 0, (q0, q1))
-            mms([(P, Id, at("ch", 0, (q0, q1))), (P, IdT, at("ch", 1, (q0, q1))), (P, Id, at("con", 3, (0, m)))] +
-                [(at("b1", 0, 0, (q0 + a, q1, 2)), at("UK", 2 * a + b), at("lose", (e0 + 32 * b + 31, e0 + 2 * w, 64))) for a in range(2) for b in range(2)] +
-                [(at("b1", 0, 0, (q0 + 2 + a, q1, 4)), at("UK", 2 * a + b), at("lose", (e0 + 2 * w + 32 * b + 31, e0 + 3 * w, 64))) for a in range(2) for b in range(2)])
-            tt(q("posU"), P, q("dump"), A.min)
-            now[1] = "column%d" % gi
-            act(at(JU), L(0, 3), F.Relu)
+            R = at("b4", (8 + lo // 32, 8 + hi // 32))
+            mms([(R, IdR, at("RK", 2))] + [(at("b4", (8 + lo // 32, 8 + hi // 32), a), at("PM", 2 * a + b), at(Qt, (4, 8), b)) for a in range(2) for b in range(2)])
+            turn32(at("O", (k0, k1)), R)
+            own = at("O", (k0, k1), (0, 4), 0)
+            mms([(at(ub, (4, 8)), IdR, at("RK", (1, 3))), (at(ub, (4, 6)), BM, qt(1)), (at(ub, (6, 8)), BM, qt(1))])
+            for d in range(4):
+                tt(at("EQ", (k0, k1), (64 * d + d, 256, 4)), at("O", (k0, k1), (d, 4)), at(ub, (6, 8) if d else (4, 6), (0, 4 - d)), A.is_equal)
+            for k in range(k1 - 1, k0 - 1, -1):
+                scan(at("lose", k), at("EQ", k), at("DM"))
+            tt(q("sc"), own, at("lose", (k0, k1), (63, 256, 64)), A.subtract)
+            tt(q("posU"), q("sc"), q("dump"), A.min)
             now[1] = "fork%d" % gi
-            tt(at("hm", (0, 2), (q0, q1)), L(4, 2), at("KT", (0, 2), (q0, q1)), A.mult)
-            tt(at(cs, (2 * t, 2 * t + 2)), L(2, 2), at("hm", (0, 2), (q0, q1)), A.add)
-            send(at("rcv", t, (q0, q1)), at(cs, 2 * t + 1), "n%d_%d" % (t, gi), dst)
-            tt(q("m0"), L(6), at(cs, 2 * t), A.max)
+            if gi in FAST:
+                mms([(at(bank, (4, 8), a), at("PM", 2 * a + b), at(Qt, (16, 20), b)) for a in range(2) for b in range(2)])
+                turn32(at("O2"), at(bank, (4, 8)))
+                plus(FAST[gi], at("cs", 2 * t + gi, 0), at("O2", (0, 128, 16)), fork0)
+                plus(CS_ON, at("cs", 2 * t + gi, 1), L(5), 0.0)
+            else:
+                plus(CS_ON, at("cs", 2 * t + gi), L(4, 2), 0.0)
+            send(at("rcv", t, (q0, q1)), at("cs", 2 * t + gi, 0), "n%d_%d" % (t, gi), dst)
+            tt(q("m0"), L(1), at("cs", 2 * t + gi, 1), A.min)
             now[1] = "column%d" % gi
+            ts(q("JC1"), own, -float(SPARE), A.add, 4095.0, A.min)
             if SUM_ON[gi] == "P":
-                plus("S", h("old"), ind(swin, at(JU, (2 * m, 3 * m))), -2048.0)
-                nc = at("b0", (b0, b1))
-                mms([(nc, Id, qt(7)), (nc, Id, h("old"))])
+                plus("S", h("old"), ind(swin, q("JC1")), -2048.0)
+                nc = at(bank, (0, 4))
+                mms([(nc, Id, qt(0)), (nc, Id, h("old"))])
                 plus("S", h("nc"), nc, 2048.0)
             else:
-                act(h("old2"), ind(swin, at(JU, (2 * m, 3 * m))), F.Copy)
-                tt(h("nc"), h("old2"), qt(7), A.add)
+                tt(h("nc"), ind(swin, q("JC1")), qt(0), A.add)
             ts(h("nd"), h("nc"), 4095, A.bitwise_and)
             now[1] = "X%d" % gi
-            act(at("zz", (2 * lo, 2 * hi)), ind(at(D), at(JU, (0, 2 * m))), F.Abs)
+            act(at(JU), L(2, 2), F.Relu)
+            act(at("zz", (2 * lo, 2 * hi)), ind(at(D), at(JU)), F.Abs)
 
         for gi in range(len(PARTS)):
             gathers(gi)
         for gi in range(len(PARTS)):
             claims(gi)
-        for names in TURNS:
+        for names in turn.values():
             for a, b in zip(names, names[1:]):
-                ops[tag[b][0]]["hard"].append(tag[a][-1])
+                ops[b]["hard"].append(a)
         now[1] = "S"
         for j in range(3, -1, -1):
             cp(ind(at("Si"), at("posU", (4 * j, 4 * j + 4))), at("nd", (64 * j, 64 * j + 64)))
         for gi, (lo, hi) in enumerate(PARTS):
             now[1] = "X%d" % gi
             q0, q1 = lo // 16, hi // 16
-            act(at("yi", (q0, q1)), at("L", 7, (q0, q1)), F.Copy)
-            ts(at("y7", (q0, q1)), at("yi", (q0, q1)), 7, A.bitwise_and)
-            tt(at("w8", (q0, q1)), at("I8", (q0, q1)), at("L", 4, (q0, q1)), A.subtract)
+            act(at("yi", (q0, q1)), at("c%d" % gi, 32), F.Copy)
+            ts(at("y7", (q0, q1)), at("yi", (q0, q1)), 8199, A.bitwise_and)
             w = at("WLU", (q0, q1))
-            tt(w, at("y7", (q0, q1)), at("w8", (q0, q1)), A.add)
-            cp(ind(at("XX", (0, 6144)), w), at("zz", (2 * lo, lo + hi)))
-        dma(T.yv[:] if last else at("XX", (2048, 4096)), at("XX", (0, 2048)))
+            tt(w, at("y7", (q0, q1)), at("I8", (q0, q1)), A.add)
+            cp(ind(at("XX", (0, X0 + 8 * hi)), w), at("zz", (2 * lo, lo + hi)))
+            dma(T.yv[:, 8 * lo:8 * hi] if last else at("XX", (X0 + 2048 + 8 * lo, X0 + 2048 + 8 * hi)), at("XX", (X0 + 8 * lo, X0 + 8 * hi)))
         for gi, (lo, hi) in enumerate(PARTS):
             now[1] = "place%d" % gi
             q = lambda nm: at(nm, (lo // 16, hi // 16))
-            tt(q("m1"), q("m0"), at("rcv", t, (lo // 16, hi // 16)), A.max)
+            tt(q("m1"), q("m0"), at("rcv", t, (lo // 16, hi // 16)), A.min)
             ts(q("sL"), q("m1"), 4095, A.bitwise_and)
             if not last:
-                act(q("sU"), q("sL"), F.Copy)
+                plus(C_ON[2 + gi], q("sU"), q("sL"), 0.0)
         if last:
             cp(at("yso"), at("sL"))
             dma(T.ys[:], at("yso"))
         else:
-            act(at("jk"), at("L", 5), F.Copy, acc=acc, scale=1.0 / 4096)
-            act(at("accB"), on, F.Identity, scale=-0.0625, bias=acc)
+            act(at("jk"), at("cs", (2 * t, 2 * t + 2), 0), F.Sign, acc=acc, scale=-1.0, bias=100000.0)
+            act(at("accB"), on, F.Identity, scale=kap, bias=acc)
         now[1] = "x"
-        xo, yh = at("XC", (x0, x0 + 256)), at("b3", (8, 16))
-        half = lambda lo, hi: at("b3", (8 + lo // 32, 8 + hi // 32))
-        mms([(yh, IdN, xo)] + [(half(lo, hi), Id, at("zz", (lo + hi, 2 * hi))) for lo, hi in PARTS])
-        act(at("Y", t), yh, F.Abs)
-        send(at("XC", (x0 + 256, x0 + 512)), at("Y", t), "x%d" % t, dst)
-        mms([(yh, IdH, xo), (yh, IdH, at("con", 2))] + [(half(lo, hi), IdH, at("zz", (2 * lo, lo + hi))) for lo, hi in PARTS])
-        act(at("ha"), yh, F.Identity, bias=MAGIC)
-        act(at("XC", (x0 + 512, x0 + 768)), at("ha"), F.Identity, bias=-MAGIC)
+        xo = at("XC", (x0 + 512, x0 + 768))
+        half = lambda b, lo, hi: at("b%d" % b, (lo // 32, hi // 32))
+        for gi, (c0, c1) in enumerate(PARTS if last else ((0, 256),)):
+            mms([(half(0, c0, c1), IdN, at("XC", (x0 + 512 + c0, x0 + 512 + c1)))] +
+                [(half(0, lo, hi), Id, at("zz", (lo + hi, 2 * hi))) for lo, hi in PARTS if c0 <= lo < c1])
+            act(at("Y", t, (c0, c1)), half(0, c0, c1), F.Abs)
+            send(at("XC", (x0 + 256 + c0, x0 + 256 + c1)), at("Y", t, (c0, c1)), "x%d" % (t + gi), dst)
+        yh = half(1, 0, 256)
+        mms([(yh, IdH, xo), (yh, IdH, at("con", 0))] + [(half(1, lo, hi), IdH, at("zz", (2 * lo, lo + hi))) for lo, hi in PARTS])
+        if HALF_ON == "V":
+            ts(at("XC", (x0, x0 + 256)), yh, MAGIC, A.add, -MAGIC, A.add)
+        else:
+            act(at("ha"), yh, F.Identity, bias=MAGIC)
+            act(at("XC", (x0, x0 + 256)), at("ha"), F.Identity, bias=-MAGIC)
         ts(at("xt"), at("m1"), 7, A.arith_shift_right, 768, A.bitwise_and)
         tt(at("XLU"), at("xt"), at("Ic"), A.add)
-        xn = at("XC", (x0 + 768, x0 + 1024))
+        xn = at("XC", (x0 + 1280, x0 + 1536))
         act(xn, ind(at("XC", (x0, x0 + 768)), at("XLU")), F.Copy)
         if last:
             dma(T.yx[:], xn)
@@ -418,12 +459,13 @@ def build(core, T, topo, ops, EST):
     for t in range(STEPS):
         step(t)
 
-    yt, blk, many = at("b0", (0, 8)), lambda nm, j, k=1: at(nm, (256 * j, 256 * (j + k))), 2 * len(YT_ON)
+    now[1] = "yt"
+    yt, blk, many = at("b0", (0, 8)), lambda nm, j, k=1, o=0: at(nm, (o + 256 * j, o + 256 * (j + k))), 2 * len(YT_ON)
     for j in range(0, many, 2):
-        plus(YT_ON[j // 2], blk("S16", j, 2), blk("Si", j, 2), -2048.0)
-        mms([(yt, Id, blk("S16", k)) for k in (j, j + 1)] + ([(yt, Id, at("con", 4))] if j == 0 else []), j == 0, j + 2 == many)
+        plus(YT_ON[j // 2], blk("S16", j, 2), blk("Si", j, 2, SPARE), -2048.0)
+        mms([(yt, Id, blk("S16", k)) for k in (j, j + 1)] + ([(yt, Id, at("con", 1))] if j == 0 else []), j == 0, j + 2 == many)
     k = (16 - many) // 2
-    tt(blk("ysum", 0, k), blk("Si", many, k), blk("Si", many + k, k), A.add)
+    tt(blk("ysum", 0, k), blk("Si", many, k, SPARE), blk("Si", many + k, k, SPARE), A.add)
     for j in range(1, k):
         tt(blk("ysum", 0), blk("ysum", 0), blk("ysum", j), A.add)
     tt(at("yto"), yt, blk("ysum", 0), A.add)
@@ -456,139 +498,114 @@ def plan(ops, cases):
     names = sorted(set(o["q"] for o in ops) | set(b for o in ops for b in o["banks"]))
     queue = [names.index(o["q"]) if o["kind"] != "recv" else -1 for o in ops]
     banks = [[names.index(b) for b in sorted(o["banks"])] for o in ops]
-    pred = [sorted(o["d"]) for o in ops]
     hard = [o["hard"] for o in ops]
-    allp = [set(pred[i]) | set(hard[i]) for i in range(n)]
+    allp = [sorted(o["d"] | set(o["hard"])) for o in ops]
     isdma = [o["kind"] == "dma" for o in ops]
     succ = [[] for _ in range(n)]
     for i in range(n):
         for j in allp[i]:
             succ[j].append(i)
-    slots = {}
-    slot = [slots.setdefault(o["slot"], len(slots)) for o in ops]
+    lags = [[[(j, same if queue[j] == queue[i] else wake) for j in sorted(ops[i]["d"])] for i in range(n)] for dur, wake, same in cases]
 
-    def run(dur, wake, same, order=None, rank=None):
-        end, why, issued, base, cause = [0.0] * n, [-1] * n, [0.0] * n, [0.0] * n, [-1] * n
-        free, last, user = [0.0] * len(names), [-1] * len(names), [[] for _ in names]
-        need, out = [len(x) for x in allp], []
-        ready = [i for i in range(n) if need[i] == 0]
-
-        def start(i):
-            s, w, q = base[i], cause[i], queue[i]
+    def run(c, order):
+        dur, wake, lag = cases[c][0], cases[c][1], lags[c]
+        end, why, issued = [0.0] * n, [-1] * n, [0.0] * n
+        free, last, user = [0.0] * len(names), [-1] * len(names), [{} for _ in names]
+        for i in order:
+            s, w, q = 0.0, -1, queue[i]
+            for j, d in lag[i]:
+                if end[j] + d > s:
+                    s, w = end[j] + d, j
+            for j in hard[i]:
+                if issued[j] > s:
+                    s, w = issued[j], j
             if q >= 0 and free[q] > s:
                 s, w = free[q], -2 - last[q]
             for b in banks[i]:
-                for j in user[b]:
-                    if queue[j] != q and end[j] + wake > s:
+                for p, j in user[b].items():
+                    if p != q and end[j] + wake > s:
                         s, w = end[j] + wake, -2 - j
-            return s, w
-
-        for pos in range(n):
-            if order:
-                i = order[pos]
-                s, w = start(i)
-            else:
-                cand = [(start(i), i) for i in ready]
-                (s0, w0), i0 = min(cand, key=lambda c: c[0][0] + (0.1 if isdma[c[1]] else dur[c[1]]))
-                lim, q0 = s0 + REACH * (0.1 if isdma[i0] else dur[i0]), queue[i0]
-                (s, w), i = max([c for c in cand if queue[c[1]] == q0 and c[0][0] <= lim], key=lambda c: rank[c[1]])
-                ready.remove(i)
-                out.append(i)
-            q = queue[i]
-            for b in banks[i]:
-                user[b] = [j for j in user[b] if queue[j] != q] + [i]
+                user[b][q] = i
             end[i], why[i] = s + dur[i], w
             issued[i] = s + 0.1 if isdma[i] else end[i]
             if q >= 0:
                 free[q], last[q] = issued[i], i
-            for k in succ[i]:
-                need[k] -= 1
-                if need[k] == 0:
-                    t, c = 0.0, -1
-                    for j in pred[k]:
-                        e = end[j] + (same if queue[j] == queue[k] else wake)
-                        if e > t:
-                            t, c = e, j
-                    for j in hard[k]:
-                        if issued[j] > t:
-                            t, c = issued[j], j
-                    base[k], cause[k] = t, c
-                    if not order:
-                        ready.append(k)
-        i = max(range(n), key=lambda x: end[x])
-        total, held = end[i] + EARLY * sum(end) / n, []
+        top = max(end)
+        i, held = end.index(top), []
         while why[i] != -1:
             j = why[i] if why[i] >= 0 else -2 - why[i]
             if why[i] < 0:
                 held.append((j, i))
             i = j
-        return total, held, out
+        return top + EARLY * sum(end) / n, held
 
-    way = [0.0] * n
-    for sweep in range(4):
-        for i in range(n - 1, -1, -1):
-            way[i] = cases[0][0][i] + max([way[k] + cases[0][1] for k in succ[i]] + [0.0])
+    turn = TURN.split()
+    period = 20.0
+    shift = [period * o["step"] for o in ops]
+    slots = {}
+    slot = [slots.setdefault(o["slot"], len(slots)) for o in ops]
+    place = [None] * len(slots)
+    for i, o in enumerate(ops):
+        nm = o["slot"]
+        if o["task"] == "start":
+            place[slot[i]] = max([place[slot[j]] + 0.3 for j in allp[i]] + [0.001 * i - period])
+        elif place[slot[i]] is None:
+            place[slot[i]] = place[slot[i - 1]] + 0.01
+            for mark, late in (("", 0), ("+", 1), ("-", -1)):
+                if nm + mark in turn:
+                    place[slot[i]] = period * (turn.index(nm + mark) / len(turn) + late)
 
-    def judge(gain):
-        first = run(*cases[0], None, [way[i] + gain[slot[i]] for i in range(n)])
-        res = [first] + [run(*c, first[2]) for c in cases[1:]]
-        return sum(x[0] for x in res), res
+    def judge(place):
+        key = [0.0] * n
+        for i in range(n):
+            k = place[slot[i]] + shift[i]
+            for j in allp[i]:
+                if key[j] >= k:
+                    k = key[j] + 1e-6
+            key[i] = k
+        order = sorted(range(n), key=lambda i: key[i])
+        res = [run(c, order) for c in range(len(cases))]
+        return sum(x[0] for x in res), res, order
 
     rng = np.random.default_rng(SEED)
-    gain = [0.0] * len(slots)
-    for i in range(n):
-        gain[slot[i]] = URGENT.get(ops[i]["task"], 0.0)
-    cost, now = judge(gain)
-    best = (cost, now[0][2])
-    for it in range(SHIFTS):
-        if it == SHIFTS * 2 // 3:
-            for i in range(n):
-                if ops[i]["step"] in (0, STEPS - 1):
-                    gain.append(gain[slot[i]])
-                    slot[i] = len(gain) - 1
-        held = now[int(rng.integers(len(cases)))][1]
-        new = list(gain)
-        for rep in range(1 + int(rng.random() < 0.3)):
-            if rng.random() < TASKS:
-                task, d = ops[int(rng.integers(n))]["task"], float(rng.normal())
-                for x in set(slot[i] for i in range(n) if ops[i]["task"] == task):
-                    new[x] += d
-            elif held and rng.random() < 0.8:
-                j, i = held[int(rng.integers(len(held)))]
-                gap = max(way[j] + gain[slot[j]] - way[i] - gain[slot[i]], 0.0) + float(rng.random())
-                if rng.random() < 0.5:
-                    new[slot[i]] += gap
-                else:
-                    new[slot[j]] -= gap
+    cost, now, order = judge(place)
+    best = (cost, order, place)
+    for stage, rounds in enumerate(ROUNDS):
+        if stage == 1:
+            place = [best[2][slot[i]] for i in range(n)]
+            slot = list(range(n))
+            cost, now, order = judge(place)
+            best = (cost, order, place)
+        for it in range(rounds):
+            held = now[int(rng.integers(len(cases)))][1]
+            new = list(place)
+            way = 1 if rng.random() < 0.5 else -1
+            if rng.random() < 0.85:
+                j, i = held[int(rng.integers(len(held)))][::-way]
+                todo = [(i, new[slot[j]] + shift[j] + way * (0.001 + float(rng.random()) ** 3))]
             else:
-                new[int(rng.integers(len(new)))] += float(rng.normal()) * 2
-        c, res = judge(new)
-        if c <= cost + MARGIN * (1 - it / SHIFTS) * float(rng.random()):
-            gain, now, cost = new, res, c
-            if c < best[0]:
-                best = (c, res[0][2])
-    cost, order = best
-    now = [run(*c, order) for c in cases]
-    for it in range(MOVES):
-        held = now[int(rng.integers(len(cases)))][1]
-        j, i = held[int(rng.integers(len(held)))]
-        a, b = order.index(j), order.index(i)
-        take = {i}
-        for x in reversed(order[a:b + 1]):
-            if x in take:
-                take |= allp[x]
-        if j not in take:
-            trial = order[:a] + [x for x in order[a:b + 1] if x in take] + [x for x in order[a:b + 1] if x not in take] + order[b + 1:]
-            new = [run(*c, trial) for c in cases]
-            if sum(x[0] for x in new) <= cost:
-                order, now, cost = trial, new, sum(x[0] for x in new)
+                i = int(rng.integers(n))
+                todo = [(i, new[slot[i]] + shift[i] + way * 1.5 * float(rng.random()))]
+            count = 0
+            while todo and count < 40:
+                x, k = todo.pop()
+                if (new[slot[x]] + shift[x] - k) * way < 0:
+                    new[slot[x]] = k - shift[x]
+                    todo += [(y, k + way * 0.001) for y in (succ if way > 0 else allp)[x]]
+                    count += 1
+            if count < 40:
+                c, res, o = judge(new)
+                if c <= cost + MARGIN * (1 - it / rounds) * float(rng.random()):
+                    place, now, cost = new, res, c
+                    if c < best[0]:
+                        best = (c, o, place)
     extra, users = [], {}
-    for i in order:
+    for i in best[1]:
         for b in sorted(ops[i]["banks"]):
             u = users.setdefault(b, {})
             extra += [(i, j) for q, j in u.items() if q != ops[i]["q"]]
             u[ops[i]["q"]] = i
-    return order, extra, cost / len(cases)
+    return best[1], extra, best[0] / len(cases)
 
 
 def rank_program(g, core, T, topo):

@@ -3,77 +3,83 @@ from concourse.mybir import AluOpType as A, ActivationFunctionType as F
 
 STEPS = 4
 PARTS = ((128, 256), (0, 128))
-G_CUT = ((208, 256, "V"), (128, 208, "S"), (64, 128, "V"), (32, 64, "V"), (0, 32, "S"))
-X_CUT = (((224, 256), (192, 224), (128, 192)), ((96, 128), (64, 96), (32, 64), (0, 32)))
+G_CUT = ((224, 256, "V"), (192, 224, "S"), (160, 192, "V"), (128, 160, "S"), (64, 128, "V"), (32, 64, "V"), (0, 32, "S"))
+AB_CUT = (((192, 256, 0, 5, "S"), (128, 192, 0, 5, "S")), ((64, 128, 0, 1, "V"), (0, 64, 0, 5, "V")))
+X_CUT = (((192, 256), (128, 192)), ((64, 128), (32, 64), (0, 32)))
 Z_CUT = (((192, 256, "S"), (128, 192, "V")), ((64, 128, "S"), (32, 64, "S"), (0, 32, "V")))
 U_CUT = (((128, 192, "D"), (128, 256, "Z")), ((0, 32, "D"), (0, 128, "Z")))
-HALF_ON = "S"
-SUM_ON = "PP"
-C_ON = "SSSS"
-E_ON = "VVS"
+GT_ON = "SV"
+ROUND = (1,)
+KEEP = 1
+JOIN = "110"
 LR_CUT = (8, 16)
-FAST = {0: "S", 1: "S"}
-AB_ON = ("SSVV", "VV")
-CS_ON = "S"
-YT_ON = "SVSSSS"
-TURN = """
-cU.gathers.1 jk.place1.1+ sL.place1.1+ G.gathers.2 G.gathers.1 b0.gathers.1 sU.place1.1+ cU.gathers.2 sF.gathers.1 G.gathers.5 GT.gathers.1 b1.gathers.1 AB.gathers.1
-G.gathers.3 accB.place1.1+ XX.X1.2+ GT.gathers.2 b0.gathers.2 G.gathers.4 AB.gathers.2 Xa.var0.1 Xa.var0.2 b1.gathers.2 cF.gathers.1 GT.gathers.3 b1.gathers.3 D.var0.1
-AB.gathers.3 b4.E.1 Xa.var0.3 c0.E.1 D.var0.2 D.var0.3 Xa.var1.1 D.var1.1 rE.E.1 Z.var0.2 Xa.var1.2 Z.var0.1 c1.E.1 D.var1.2 Xa.var1.3 Xa.var1.4 b4.E.2 D.var1.3 b2.var0.2
-b2.var0.3 rq.claim0.1 yT.claim0.1 b2.claim0.1 D.var1.4 Z.var1.2 sq.claim0.1 tb.claim0.1 Fc.claim0.1 b3.var1.2 Z.var1.3 b0.tables0.1 c0.tables0.1 Z.var1.1 XC.x.2+
-Qt0.tables0.1 b3.var1.3 Qt0.tables0.4 Qt0.tables0.2 rq.claim1.1 Qt0.tables0.3 b2.tables0.1 b0.fork0.1 b4.lowest0.1 c0.lists0.1 Qt0.tables0.5 yT.claim1.1 b3.claim1.1
-b2.lowest0.1 O2.fork0.1 cs.fork0.1 O.lowest0.1 JC1.column0.1 sq.claim1.1 tb.claim1.1 xt.x.1+ old.column0.1 Qt1.tables1.1 c0.lists0.2 c0.lists0.3 yi.X0.1 b0.column0.1
-EQ.lowest0.3 Fc.claim1.1 XLU.x.1+ EQ.lowest0.4 EQ.lowest0.1 cs.fork0.2 EQ.lowest0.2 c1.tables1.1 JU0.X0.1 zz.X0.1 Qt1.tables1.3 Qt1.tables1.2 b3.tables1.1 Qt1.tables1.5
-lose.lowest0.2 b1.tables1.1 b1.fork1.1 lose.lowest0.1 nc.column0.1 O2.fork1.1 b4.lowest1.1 O.lowest1.1 nd.column0.1 c1.lists1.1 sc.lowest0.1 JC1.column1.1 b3.lowest1.1
-Y.x.2+ EQ.lowest1.4 EQ.lowest1.3 Qt1.tables1.4 cs.fork0.3 EQ.lowest1.2 EQ.lowest1.1 c1.lists1.2 cs.fork1.1 cs.fork1.3 old.column1.1 posU.lowest0.1 XC.x.1+ XC.x.3+
-m0.fork0.1 lose.lowest1.1 lose.lowest1.2 rcv.fork0.1 JU1.X1.1 b1.column1.1 nc.column1.1 Si.S.1 sc.lowest1.1 nd.column1.1 Si.S.2 posU.lowest1.1 b3.var1.1- y7.X0.1
-rcv.fork1.1 m1.place0.1 b2.var0.1- Si.S.3 zz.X1.1 WLU.X0.1 sL.place0.1 b0.x.1 Y.x.1 cs.fork1.2 yi.X1.1 Si.S.4 y7.X1.1 XX.X0.1 XX.X0.2 sU.place0.1 m0.fork1.1 WLU.X1.1
-b1.x.1 XX.X1.1 m1.place1.1 ha.x.1
-"""
+POS_CUT = (1, 2)
+YT_CUT = (("S", 1), ("V", 2), ("S", 2), ("V", 2), ("S", 2), ("V", 2), ("S", 2), ("S", 2), ("V", 1))
+ER_ON = "VVVS"
+W_FILL = 8
 MAGIC = 12582912.0
 HIGH = 65536.0
-CEIL = 61440.0
+FLOOR = 33024.0
+OFF = 33280.0
+TOP = 49152.0
 SPARE = 256
-X0 = 8192
-NT = 6
+X0 = 4096
+NT = 4
+ORDER = """
+cU.gathers.1 XC.x.1+ G.gathers.1 m1.place1.1+ G.gathers.2 XX.X1.2+ sL.place1.1+ G.gathers.4 sU.place1.1+ b5.gathers.1 G.gathers.3 cU.gathers.2 xt.x.1+ b0.gathers.1
+AB.gathers.1 G.gathers.5 G.gathers.7 So.var0.1 b5.gathers.2 sF.gathers.1 GT.gathers.1 AB.gathers.2 b0.gathers.2 Xa.var0.1 G.gathers.6 b1.gathers.1 AB.gathers.3
+b5.gathers.3 XLU.x.1+ AB.gathers.4 cF.gathers.1 Xa.var0.2 D.var0.1 b1.gathers.2 b4.E.1 Xa.var1.1 GT.gathers.2 AB.gathers.5 D.var0.2 b1.gathers.3 c0.E.1 c1.E.1
+Z.var0.1 AB.gathers.6 b2.var0.2 Z.var0.2 rE.E.1 D.var1.1 b2.var0.3 Xa.var1.2 b4.E.2 Xa.var1.3 D.var1.2 rq.claim0.1 Z.var1.1 D.var1.3 yT.claim0.1 b3.var1.2 Z.var1.2
+Z.var1.3 b2.claim0.1 sq.claim0.1 b3.var1.3 XC.x.3+ tb.claim0.1 Qt.tables0.1 Fc.claim0.1 rq.claim1.1 c0.tables0.1 b2.tables0.1 yT.claim1.1 Qt.tables0.3 Qt.tables0.2
+b3.claim1.1 Qt.tables0.4 b0.fork0.1 sq.claim1.1 b4.lowest0.1 Qt.tables1.1 O2.fork0.1 b2.lowest0.1 tb.claim1.1 O.lowest0.1 cs.fork0.1 b2.var0.1- Fc.claim1.1
+cs.fork0.2 JC1.column0.1 EQ.lowest0.3 EQ.lowest0.5 EQ.lowest0.1 c1.tables1.1 EQ.lowest0.2 old.column0.1 EQ.lowest0.4 b3.tables1.1 Qt.tables1.3 rcv.fork0.1
+Qt.tables1.2 Qt.tables1.4 b1.fork1.1 lose.lowest0.2 b0.column0.1 O2.fork1.1 b4.lowest1.1 lose.lowest0.1 b3.lowest1.1 cs.fork1.1 O.lowest1.1 nc.column0.1 c1.lists1.1
+cs.fork1.2 posU.lowest0.1 c1.lists1.2 JC1.column1.1 nd.column0.1 EQ.lowest1.5 EQ.lowest1.4 EQ.lowest1.1 old.column1.1 Si.S.1 rcv.fork1.1 jk.place1.1 EQ.lowest1.2
+JU.lists1.1 b1.column1.1 yi.lists1.1 EQ.lowest1.3 Si.S.2 none.lists1.1 zz.lists1.2 y7.X0.1 b3.var1.1- m0.lists1.1 lose.lowest1.2 nd.column1.1 WLU.X0.1 zz.lists1.1
+lose.lowest1.1 b1.x.1 XX.X0.1 posU.lowest1.1 posU.lowest1.2 b0.x.1 ha.x.1 m1.place0.1 Si.S.3 accB.place1.1 XX.X0.2 Y.x.1 sL.place0.1 Si.S.4 sU.place0.1 Y.x.2
+XC.x.2 XX.X1.1
+"""
 
 SCRATCH = {
-    "Si": ("sbuf", [128, SPARE + 4096 + 272], "int32"),
+    "Si": ("sbuf", [128, SPARE + 8192], "int32"),
+    "So": ("sbuf", [128, 4096], "int32"),
     "XX": ("sbuf", [128, X0 + 4096], "bfloat16"),
     "XC": ("sbuf", [128, (STEPS + 1) * 768], "bfloat16"),
     "c0": ("psum", [128, 64, 8], "float32"),
     "c1": ("psum", [128, 64, 8], "float32"),
 }
 for _dt, _shapes in (
-        ("bfloat16", {"Xa": [4096], "on": [256], "SEL": [16, 2, 8], "ER": [16, 128], "LR": [16, 8, 16], "WG": [2, 8], "PM": [4, 4, 32],
-                      "BI": [128], "BM": [4, 32], "Id": [4, 32], "CNT": [128], "mat": [16, 128], "con": [2, 256], "low": [256], "RM": [128], "jk": [16],
-                      "EQ": [4, 256], "lose": [4, 256], "DM": [256], "zz": [512], "Y": [STEPS, 256],
+        ("bfloat16", {"Xa": [4096], "on": [256], "SEL": [16, 2, 8], "ER": [16, 128], "LR": [144], "WG": [2, 8], "PM": [4, 4, 32], "W": [32, 144],
+                      "BI": [128], "BM": [4, 32], "Id": [4, 32], "mat": [16, 128], "con": [4, 256], "jk": [16], "zz": [512], "Y": [STEPS, 256], "RK": [128],
                       "D0": [4096], "D1": [4096], "Z0": [4096], "Z1": [4096]}),
-        ("float16", {"G": [4096], "S16": [4096], "GT": [512], "yT": [256], "JC": [NT, 16], "JK": [2, 16], "sF": [16], "accB": [128], "cF": [256], "rq": [256],
-                     "rE": [256], "RK": [3, 128], "old": [256], "Fc": [256], "Qt0": [4 * NT, 2, 16], "Qt1": [4 * NT, 2, 16]}),
-        ("float32", {"r256": [256], "EQc": [16], "q16": [16], "Ic": [16], "I8": [16], "col": [8], "m0": [16], "O": [4, 4, 16], "O2": [128], "sc": [16], "dump": [16], "ha": [256],
-                     "ysum": [1024], "yto": [256], "yso": [16], "rcv": [STEPS, 16], "cs": [2 * STEPS, 2, 8]}),
-        ("int32", {"pI": [4], "wI": [1], "sL0": [16], "sL": [16], "m1": [16], "yi": [16], "y7": [16], "xt": [16], "sq": [256], "tb": [256],
-                   "nc": [256], "nd": [256]}),
-        ("uint16", {"AB": [512], "sU": [16], "WLU": [16], "XLU": [16], "posU": [16], "cU": [256], "JC1": [16], "JU0": [16], "JU1": [16]})):
+        ("float16", {"GT": [512], "rE": [256], "G": [4096], "S16": [4096], "yT": [256], "JC": [NT, 16], "sF": [16], "accB": [128], "cF": [256], "rq": [256],
+                     "old": [256], "Fc": [256], "Qt": [NT, 2, 8, 16], "EQ": [4, 320], "lose": [4, 320], "DM": [320]}),
+        ("float32", {"r128": [128], "EQc": [16], "q16": [16], "Ic": [16], "I8": [16], "col": [8], "m0": [16], "O": [4, 4, 16], "O2": [128],
+                     "yto": [256], "yso": [16], "rcv": [STEPS, 16], "cs": [STEPS, 16], "none": [16]}),
+        ("int32", {"nc": [256], "ha": [256], "pI": [4], "wI": [1], "sL0": [16], "sL": [16], "m1": [16], "yi": [16], "y7": [16], "xt": [16], "sq": [256], "tb": [256], "nd": [256]}),
+        ("uint16", {"AB": [512], "sU": [16], "WLU": [16], "XLU": [16], "posU": [16], "cU": [256], "JC1": [16], "JU": [32]})):
     for _nm in _shapes:
         SCRATCH[_nm] = ("sbuf", [128] + _shapes[_nm], _dt)
-for _b in (0, 1, 4):
+for _b in (0, 1, 4, 5):
     SCRATCH["b%d" % _b] = ("psum", [128, 16, 2, 16], "float32")
 for _b in (2, 3):
     SCRATCH["b%d" % _b] = ("psum", [128, 8, 4, 16], "float32")
 
-SEMAPHORES = ["eV", "eS", "eP", "eG", "ax%d" % STEPS, "lx%d" % STEPS] + ["m%d" % i for i in range(20)]
+SEMAPHORES = ["eV", "eS", "eP", "eG", "ax%d" % STEPS, "lx%d" % STEPS] + ["m%d" % i for i in range(24)]
 for _t in range(STEPS):
     for _nm in ("x%d" % _t, "n%d_0" % _t, "n%d_1" % _t):
         SEMAPHORES += ["a" + _nm, "l" + _nm]
 
-EST = {"cyc": 0.00083 * 1.05, "V": 0.02, "S": 0.04, "ind": 0.12, "ga": 1.2, "sc": 3.5, "pe": 0.0005, "wake": 0.14, "same": 0.19, "net": 3.2, "dma": 1.3, "rate": 350e3}
-CASES = ({}, {"cyc": 0.00083 * 1.4, "pe": 0.0007, "ga": 1.35}, {"net": 3.8, "ga": 1.05, "cyc": 0.00083})
-SEED = 1
-ROUNDS = (2500, 8000)
-MARGIN = 0.4
-EARLY = 0.1
+EST = {"cyc": 0.00083 * 1.05, "V": 0.02, "S": 0.04, "ind": 0.12, "ga": 1.2, "sc": 3.5, "pe": 0.00058, "wake": 0.14, "same": 0.19, "net": 3.2, "dma": 1.3, "rate": 450e3}
+CASES = ({}, {"pe": 0.0008}, {"cyc": 0.00083 * 1.4, "pe": 0.0008, "ga": 1.5, "sc": 5.0}, {"net": 4.2, "ga": 1.05, "sc": 2.0, "cyc": 0.00083, "pe": 0.00045, "rate": 280e3, "dma": 2.0, "ind": 0.06})
+ISSUE = 0.1
+SEED = 2
+TRIES = 6000
+TIED = 0.2
+ALIKE = 0.15
+SPAN = 3.0
+NOISE = 1.0
+SLACK = 0.08
 COLUMNS = {}
 PLAN = {}
 SIZE = {"float32": 4, "int32": 4, "bfloat16": 2, "float16": 2, "uint16": 2}
@@ -101,7 +107,7 @@ def build(core, T, topo, ops, EST):
     def val(x):
         return x["ap"] if isinstance(x, dict) else x
 
-    def add(q, fn, dur, outs, ins, kind="c", sem=None, cnt=1):
+    def add(q, fn, dur, outs, ins, kind="c", sem=None, cnt=1, hold=None):
         r = [x["acc"] for x in ins if isinstance(x, dict)] + [x["off"] for x in ins + outs if isinstance(x, dict) and x["off"]]
         w = [x["acc"] for x in outs]
         banks = set(x["acc"][0] for x in ins + outs if isinstance(x, dict) and x["ps"])
@@ -109,7 +115,7 @@ def build(core, T, topo, ops, EST):
         name = "%s.%s" % (buf[0] if buf in ("D0", "D1", "Z0", "Z1") else buf, now[1])
         times[name] = times.get(name, 0) + 1
         ops.append({"slot": "%s.%d" % (name, times[name]), "task": now[1], "step": max(now[0], 0), "q": q, "fn": fn, "dur": dur, "r": r, "w": w,
-                    "kind": kind, "sem": sem, "cnt": cnt, "banks": banks, "hard": []})
+                    "kind": kind, "sem": sem, "cnt": cnt, "banks": banks, "hard": [], "hold": hold})
 
     def time(q, out, i0, per):
         if out["off"]:
@@ -135,7 +141,7 @@ def build(core, T, topo, ops, EST):
         add("V", lambda e: e.transpose(val(out), val(i0)), time("V", out, i0, 1), [out], [i0])
 
     def scan(out, i0, i1):
-        add("V", lambda e: e.tensor_tensor_scan(val(out), val(i0), val(i1), 0.0, A.max, A.mult), time("V", out, out, 0.5), [out], [i0, i1])
+        add("V", lambda e: e.tensor_tensor_scan(val(out), val(i0), val(i1), 0.0, A.max, A.add), time("V", out, out, 0.5), [out], [i0, i1])
 
     def act(out, i0, f, acc=None, **k):
         kw = {n: val(v) for n, v in k.items()}
@@ -148,6 +154,12 @@ def build(core, T, topo, ops, EST):
             act(out, i0, F.Identity, bias=c)
         else:
             ts(out, i0, c, A.add)
+
+    def scaled(q, out, i0, c, b=0.0):
+        if q == "S":
+            act(out, i0, F.Identity, scale=c, bias=b)
+        else:
+            ts(out, i0, c, A.mult, b, A.add)
 
     def mms(calls, start=True, stop=True):
         first, m = [], 0
@@ -173,20 +185,20 @@ def build(core, T, topo, ops, EST):
         elif stop:
             closed[:], since[:] = [len(ops) - 1], []
 
-    def asel(out, i0, pat, op, base, cm):
-        add("G", lambda e: e.affine_select(val(out), val(i0), pat, op, 0.0, base, cm), 0.17 + 2 * cyc * out["n"], [out], [i0])
+    def asel(out, i0, pat, op, base, cm, other=0.0):
+        add("G", lambda e: e.affine_select(val(out), val(i0), pat, op, other, base, cm), 0.17 + 2 * cyc * out["n"], [out], [i0])
 
     def iota(out, pat, cm, **k):
         add("G", lambda e: e.iota(val(out), pat, 0, cm, **k), 0.13 + 2 * cyc * out["n"], [out], [])
 
     ndma = [0]
 
-    def dma(out, i0, behind=0.0):
+    def dma(out, i0, behind=0.0, after=None):
         s = "m%d" % ndma[0]
         ndma[0] += 1
         sb = out if isinstance(out, dict) else i0
-        add("Y", lambda e: e.dma_start(val(out), val(i0)), EST["dma"] + behind + sb["bytes"] / EST["rate"], [out] if isinstance(out, dict) else [],
-            [i0], "dma", s, 16)
+        add("Y", lambda e: e.dma_start(val(out), val(i0)), EST["dma"] + (behind + sb["bytes"]) / EST["rate"], [out] if isinstance(out, dict) else [],
+            [i0, after], "dma", s, 16, ISSUE)
 
     def send(out, i0, sem, dst):
         rid, pid = topo.addr(dst)[0], topo.addr(dst)[1]
@@ -196,74 +208,74 @@ def build(core, T, topo, ops, EST):
         add("N", None, EST["net"] + out["bytes"] / 60e3, [out], [i0], "recv", "a" + sem, len(eng))
         ops[-1]["hard"].append(len(ops) - 2)
 
-    dma(at("sL0"), T.s0[:])
-    dma(at("Si", (SPARE, SPARE + 4096)), T.stm[:])
-    dma(at("wI"), T.wt[:], 6.0)
-    dma(at("XX", (X0, X0 + 2048)), T.vx[:], 6.0)
-    dma(at("XX", (X0 + 2048, X0 + 4096)), T.vx[:], 7.5)
-    dma(at("XC", (512, 768)), T.x0[:], 8.0)
+    behind = 0
+    for out, src in ((at("sL0"), T.s0), (at("Si", (SPARE, SPARE + 4096)), T.stm), (at("XX", (X0, X0 + 2048)), T.vx),
+                     (at("XX", (X0 + 2048, X0 + 4096)), T.vx), (at("wI"), T.wt), (at("XC", (0, 256)), T.x0)):
+        dma(out, src[:], behind)
+        behind += out["bytes"]
     for j in range(1, len(ops)):
         ops[j]["hard"].append(j - 1)
 
     Id, BM, on = at("Id"), at("BM"), at("on", (0, 128))
-    kcol, row0, c16, wF, acc, kap, kb = [at("col", (j, j + 1)) for j in (0, 2, 3, 4, 5, 6, 7)]
-    IdK, Id5, IdN, IdH, Id16, IdN16, IdJ, IdR, IdC, CA, CB, K1, K2, t0, t1 = [at("mat", j) for j in range(15)]
+    kcol, row8, c16, wF, acc, kap, off, top = [at("col", (j, j + 1)) for j in range(8)]
+    IdK, Id5, IdH, IdN, IdN16, Id8, Id8i, Id512, IdU, IdLow, IdN8, BMn, CA, CB = [at("mat", j) for j in range(14)]
+    con = lambda j, n=256: at("con", j, (0, n))
     fill(at("on"), 1.0)
     iota(at("pI", (0, 1)), [[0, 1]], 1)
     iota(at("q16"), [[16, 16]], 0, allow_small_or_imprecise_dtypes=True)
-    iota(at("r256"), [[0, 16], [1, 16]], 0, allow_small_or_imprecise_dtypes=True)
+    iota(at("r128"), [[0, 8], [1, 16]], 0, allow_small_or_imprecise_dtypes=True)
     asel(Id, on, [[-1, 128]], A.is_equal, 0, 1)
     asel(at("BI"), on, [[-16, 8], [0, 16]], A.is_ge, 0, 1)
     asel(BM, at("BI"), [[16, 8], [0, 16]], A.is_ge, 15, -1)
-    asel(at("CNT"), BM, [[1, 128]], A.is_ge, -1, -1)
     asel(at("SEL", (0, 16), 0), on, [[-1, 16], [-16, 8]], A.is_equal, 0, 1)
     asel(at("SEL", (0, 16), 1), on, [[-2, 8], [1, 2], [-16, 8]], A.is_equal, -1, 1)
+    moved = len(set(c[2] for part in AB_CUT for c in part))
+    if moved:
+        fill(at("W", (0, W_FILL)), 0.0)
+    for r in range(W_FILL, 16 * moved, W_FILL):
+        k = min(W_FILL, 16 * moved - r)
+        act(at("W", (r, r + k)), at("W", (0, k)), F.Copy)
+    for j in range(moved):
+        cp(at("W", (16 * j, 16 * j + 16), (15, 143, 16)), at("SEL", (0, 16), j))
+    ts(BMn, BM, -HIGH, A.mult)
+    asel(at("BI"), BMn, [[1, 128]], A.is_ge, -1, -1)
+    asel(CA, at("BI"), [[-1, 128]], A.not_equal, 0, 1, HIGH)
+    asel(CB, at("BI"), [[-1, 128]], A.not_equal, 0, 1, 2 * HIGH)
     ts(at("pI", (2, 3)), at("pI", (0, 1)), 15, A.bitwise_and)
     cp(kcol, at("pI", (2, 3)))
-    ts(row0, kcol, 0.0, A.is_equal)
-    ts(kap, row0, -2.0, A.mult, -384.0, A.add)
-    ts(kb, kcol, -128.0, A.add)
+    ts(row8, kcol, 0.0, A.is_equal, 0.125, A.mult)
+    ts(kap, row8, -16.0, A.mult, -384.0, A.add)
+    ts(off, kcol, -1024.0, A.mult, -OFF, A.add)
+    ts(top, kcol, -1024.0, A.mult, TOP - OFF, A.add)
     fill(c16, 16.0)
     cp(wF, at("wI"))
-    ts(at("EQc"), at("r256", (0, 16)), kcol, A.is_equal)
-    fill(at("LR"), 0.0)
+    ts(at("EQc"), at("r128", (0, 16)), kcol, A.is_equal)
     for r in range(16):
-        ts(at("ER", r), BM, at("EQc", (r, r + 1)), A.mult)
-        act(at("LR", r, (0, 8), r), at("BM", (0, 4), (0, 32, 16)), F.Copy)
+        scaled(ER_ON[r % len(ER_ON)], at("ER", r), BM, at("EQc", (r, r + 1)))
+    fill(at("LR"), 0.0)
+    ts(at("LR", (15, 143, 16)), at("BM", (0, 4), (0, 32, 16)), 8.0, A.mult)
     for j in range(2):
         ts(at("WG", j), at("BM", (0, 4), (0, 32, 16)), wF, A.mult, (1.0 - 2 * j) / 4096, A.mult)
-    for m, f in ((IdK, 4096.0), (Id5, 5.0), (IdN, -1.0), (IdH, 0.5), (Id16, 16.0), (IdN16, -16.0), (IdJ, 1024.0), (IdR, 2304.0)):
-        act(m, Id, F.Copy, scale=f)
-    tt(IdC, Id, at("CNT"), A.subtract)
-    act(CA, IdC, F.Copy, scale=-HIGH)
-    act(K1, IdC, F.Copy, scale=128.0)
-    tt(t0, Id, IdC, A.add)
-    act(CB, t0, F.Copy, scale=-HIGH)
-    ts(t1, at("r256", (0, 128)), -1.0, A.mult, 32.0, A.add)
-    tt(t0, t1, IdC, A.mult)
-    act(t1, Id, F.Copy, scale=128.0)
-    tt(K2, t0, t1, A.add)
-    for j, c in enumerate((-0.5, 4096.0 * len(YT_ON))):
-        fill(at("con", j), c)
-    fill(at("low"), HIGH)
-    fill(at("RK", 0), 0.5)
-    fill(at("RK", 2), -399.0)
-    ts(at("RM"), at("r256", (0, 128)), kcol, A.is_ge, 2.0, A.mult)
-    ts(at("RK", 1), at("RM"), -399.0, A.add)
+    for m, f in ((IdLow, -HIGH), (Id8i, 0.125), (IdN, -1.0), (IdN16, -16.0), (IdU, 1152.0), (IdK, 4096.0), (Id512, 512.0),
+                 (Id5, 5.0), (Id8, 8.0), (IdN8, -8.0), (IdH, 0.5)):
+        asel(m, Id, [[-1, 128]], A.not_equal, 0, 1, f)
+    for j, c in enumerate((-0.5, MAGIC, -MAGIC)):
+        fill(con(j, 128 if j else 256), c)
+    ts(at("RK"), at("r128"), kcol, A.is_ge)
     ts(at("Ic"), at("q16"), kcol, A.add)
-    ts(at("dump"), at("Ic"), SPARE + 4096.0, A.add)
     fill(at("EQ"), 0.0)
-    fill(at("DM"), 1.0)
-    fill(at("DM", (63, 256, 64)), -8192.0)
+    fill(at("DM"), 0.0)
+    fill(at("DM", (79, 320, 80)), -4.0)
+    ts(at("DM", (77, 320, 80)), at("Ic", (0, 4)), -1.0 / 2048, A.mult, -0.25 - 1.0 / 2048, A.add)
     fill(at("PM"), 0.0)
     for a in range(2):
         for b in range(2):
             act(at("PM", 2 * a + b, (0, 4), (16 * b, 16 * b + 16)), at("BM", (0, 4), (16 * a, 16 * a + 16)), F.Copy)
-    fork0 = 4096 + 61440 - 14 * CEIL
-    for j, c in enumerate((10240 - 15 * CEIL, 2048 + 28672 - 15 * CEIL, 0.0, 0.0, fork0, 69632.0 + 10240)):
-        fill(at("JC", j), c / 1024)
-    for j in range(2):
-        ts(at("JK", j), at("Ic"), -2.0 * j, A.add)
+    lanes = 16 * OFF + 1024 * 120
+    for j, c in enumerate((1 + (lanes - OFF) / 512, 1 + (lanes - OFF - TOP) / 512)):
+        ts(at("JC", j), at("Ic"), 32.0, A.mult, c - 4096, A.add)
+    fill(at("JC", 2), 0.0)
+    fill(at("JC", 3), 64.5 + 15 * FLOOR / 512)
     ts(at("I8"), at("Ic"), 8.0, A.mult)
     act(at("accB"), on, F.Identity, scale=kap)
     cp(at("sU"), at("sL0"))
@@ -274,185 +286,180 @@ def build(core, T, topo, ops, EST):
         last = t + 1 == STEPS
         D, Z = "D%d" % (t % 2), "Z%d" % (t % 2)
         x0 = 768 * t
-        turn = {"V": [], "S": []}
         now[:] = [t, "gathers"]
         times.clear()
         dst = T.cores[(rank + 1 + t % (len(T.cores) - 1)) % len(T.cores)]
-        for gi, (lo, hi) in enumerate(PARTS):
-            plus(C_ON[gi], at("cU", (lo, hi)), ind(swin, at("sU", (lo // 16, hi // 16))), 0.0)
-        plus(E_ON[0], at("sF", (0, 16)), at("sU", (0, 16)), -2048.0)
-        plus(E_ON[1], at("cF", (0, 256)), at("cU", (0, 256)), -2048.0)
+        join = [c == "1" and not last for c in JOIN]
+        both = ((0, 256),) if join[0] else PARTS
+        z1 = lambda lo, hi: at("zz", (lo, hi) if join[0] else (2 * lo, lo + hi))
+        z2 = lambda lo, hi: at("zz", (256 + lo, 256 + hi) if join[0] else (lo + hi, 2 * hi))
+        for lo, hi in PARTS:
+            plus("S", at("cU", (lo, hi)), ind(swin, at("sU", (lo // 16, hi // 16))), 0.0)
+        plus("S", at("sF"), at("sU"), -2048.0)
+        plus("V", at("cF"), at("cU"), -2048.0)
         for lo, hi, q in G_CUT:
             plus(q, at("G", (16 * lo, 16 * hi)), ind(swin, at("cU", (lo, hi))), -2048.0)
-            turn[q].append(len(ops) - 1)
         now[1] = "E"
         E = at("b4", (0, 8))
-        whole = [(E, IdN, at("cF", (0, 256))), (E, at("accB"), at("con", 0, (0, 256)))]
-        whole += [(at("b4", (0, 8), (0, 2), r), at("ER", r), at("sF", (0, 16))) for r in range(16)]
+        whole = [(E, IdN, at("cF")), (E, at("accB"), con(0))] + [(at("b4", (0, 8), (0, 2), r), at("ER", r), at("sF")) for r in range(16)]
         mms(whole)
-        if E_ON[2] == "S":
-            act(at("rE"), E, F.Identity, scale=1.0 / 16, bias=-15.0 / 32)
-        else:
-            ts(at("rE"), E, 1.0 / 16, A.mult, -15.0 / 32, A.add)
+        scaled("S", at("rE"), E, 1.0 / 16, -15.0 / 32)
         mms(whole + [(E, IdN16, at("rE"))])
         for gi, (lo, hi) in enumerate(PARTS):
-            mms([(at("c%d" % gi, (0, 32)), Id, at("low"))] + [(at("c%d" % gi, (16 * j, 16 * j + 16)), Id, at("cF", (lo, hi))) for j in range(2)], True, False)
+            mms([(at("c%d" % gi, (0, 32)), IdLow, at("on"))] + [(at("c%d" % gi, (16 * j, 16 * j + 16)), Id8i, at("cF", (lo, hi))) for j in range(2)], True, False)
 
         def gathers(gi):
             now[1] = "gathers"
             lo, hi = PARTS[gi]
-            bank, ub, o = "b%d" % gi, "b%d" % (2 + gi), 2 * lo
-            ps = at(bank, (0, 8))
-            mms([(at(bank, (0, 8), (0, 2), k), at("G", (16 * lo + k, 16 * hi, 16)), at("SEL", k)) for k in range(16)])
-            if len(AB_ON[gi]) == 2:
-                plus(AB_ON[gi][0], at("GT", (o, o + 256)), ps, 0.0)
-                mms([(at(bank, (4 * j, 4 * j + 4)), at("GT", (o + 128 * j, o + 128 * j + 128)), Id) for j in range(2)])
-                plus(AB_ON[gi][1], at("AB", (o, o + 256)), ps, 2048.0)
-            else:
-                for j in range(2):
-                    gt, wide = at("GT", (o + 128 * j, o + 128 * j + 128)), at("b%d" % (gi if j else 1 - gi), (0, 4))
-                    plus(AB_ON[gi][2 * j], gt, at(bank, (4 * j, 4 * j + 4)), 0.0)
-                    mms([(wide, gt, Id)])
-                    plus(AB_ON[gi][2 * j + 1], at("AB", (o + 128 * j, o + 128 * j + 128)), wide, 2048.0)
+            ub = "b%d" % (2 + gi)
+            bank, o = "b%d" % gi, 2 * lo
+            for c0, c1, j, b, q in AB_CUT[gi]:
+                wide = at("b%d" % b, (0, (c1 - c0) // 32))
+                mms([(wide, at("W", 16 * j + k, (15 - k, 143 - k)), at("G", (16 * c0 + k, 16 * c1, 16))) for k in range(16)])
+                plus(q, at("AB", (lo + 128 * j + c0, lo + 128 * j + c1)), wide, 2048.0)
+            sides = [j for j in range(2) if j not in [c[2] for c in AB_CUT[gi]]]
+            if sides:
+                j0, j1 = sides[0], sides[-1] + 1
+                mms([(at(bank, (4 * j0, 4 * j1), (0, 2), k), at("G", (16 * lo + k, 16 * hi, 16)), at("SEL", k, (j0, j1))) for k in range(16)])
+                plus(GT_ON[gi], at("GT", (o + 128 * j0, o + 128 * j1)), at(bank, (4 * j0, 4 * j1)), 0.0)
+                mms([(at(bank, (4 * j, 4 * j + 4)), at("GT", (o + 128 * j, o + 128 * j + 128)), Id) for j in sides])
+                plus("V", at("AB", (o + 128 * j0, o + 128 * j1)), at(bank, (4 * j0, 4 * j1)), 2048.0)
             now[1] = "var%d" % gi
+            if gi == KEEP - 1:
+                dma(at("So"), swin, after=at("AB", (o + 64, o + 128)))
+                ops[-1]["hard"] += [j for j in range(len(ops) - 1) if ops[j]["kind"] == "dma"]
+            for c0, c1 in X_CUT[gi]:
+                plus("S", at("Xa", (16 * c0, 16 * c1)), ind(xwin, at("AB", (lo + c0, lo + c1))), 0.0)
             for c0, c1 in X_CUT[gi]:
                 a, b = 16 * c0, 16 * c1
-                act(at("Xa", (a, b)), ind(xwin, at("AB", (lo + c0, lo + c1))), F.Copy)
-                turn["S"].append(len(ops) - 1)
                 tt(at(D, (a, b)), ind(xwin, at("AB", (hi + c0, hi + c1))), at("Xa", (a, b)), A.subtract)
-                turn["V"].append(len(ops) - 1)
             for c0, c1, q in Z_CUT[gi]:
                 a, b = 16 * c0, 16 * c1
                 if q == "V":
                     ts(at(Z, (a, b)), at(D, (a, b)), 0.0, A.max, 2.0, A.mult)
                 else:
                     act(at(Z, (a, b)), at(D, (a, b)), F.Abs)
-            mms([(at(ub, (0, 2)), IdR, at("RK", 0))], True, False)
-            for j, (c0, c1, src) in enumerate(U_CUT[gi]):
-                sums = [(dict(at(ub, (0, 2), (0, 4), k), ap=T[ub][c0 - lo:c1 - lo, 0:2, 0:4, k]), at(D if src == "D" else Z, (16 * c0 + k, 16 * c1, 16)),
-                         at("WG", int(src == "D"))) for k in range(16)]
-                end = j + 1 == len(U_CUT[gi])
-                if end and c1 - c0 < hi - lo:
-                    sums.append((at(ub, (0, 2), (0, 4), 15), Id, at("JC", 2, (0, 8))))
-                mms(sums, False, end)
+            mms([(at(ub, (0, 2)), IdU, on)], True, False)
+            for c0, c1, src in U_CUT[gi]:
+                mms([(dict(at(ub, (0, 2), (0, 4), k), ap=T[ub][c0 - lo:c1 - lo, 0:2, 0:4, k]), at(D if src == "D" else Z, (16 * c0 + k, 16 * c1, 16)),
+                      at("WG", int(src == "D"))) for k in range(16)], False, src == "Z")
 
         def claims(gi):
             lo, hi = PARTS[gi]
-            q0, q1, k0, k1 = lo // 16, hi // 16, lo // 64, hi // 64
-            Qt, JU, ub, bank = "Qt%d" % gi, "JU%d" % gi, "b%d" % (2 + gi), "b%d" % gi
+            p, q0, q1, k0, k1 = lo // 128, lo // 16, hi // 16, lo // 64, hi // 64
+            ub, bank, cb = "b%d" % (2 + gi), "b%d" % gi, "c%d" % gi
             h = lambda nm: at(nm, (lo, hi))
             q = lambda nm: at(nm, (q0, q1))
-            qt = lambda j, k=1: at(Qt, (4 * j, 4 * (j + k)))
-            cb = "c%d" % gi
-            L = lambda j, k=1: at(cb, (32 + j, 32 + j + k))
+            qt = lambda j: at("Qt", j, p)
             y, y1 = at(ub, (0, 2)), at(ub, (2, 4))
             now[1] = "claim%d" % gi
-            act(h("rq"), y, F.Copy)
+            act(h("rq"), y, F.Identity, bias=1.0 / 8192)
             tt(h("yT"), y, h("rq"), A.subtract)
             mms([(y, h("yT"), IdK)])
             act(h("sq"), y, F.Square, bias=c16)
             ts(h("tb"), h("sq"), 5, A.arith_shift_right, 15, A.bitwise_and)
             tt(h("Fc"), h("tb"), at("b4", (lo // 32, hi // 32)), A.is_equal)
             now[1] = "tables%d" % gi
-            act(qt(5), y, F.Copy, scale=row0)
+            act(qt(2), y, F.Copy, scale=row8)
             mms([(at(cb, (0, 16)), CA, h("Fc")), (at(cb, (16, 32)), CB, h("Fc"))], False)
-            ts(qt(1), at(cb, (0, 16)), CEIL, A.min)
-            ts(qt(4), at(cb, (16, 32)), CEIL, A.min, -2048.0, A.max)
-            mms([(at(bank, (8, 12)), K1, h("Fc")), (at(bank, (12, 16)), K2, h("Fc"))])
-            act(qt(2, 2), at(bank, (8, 16)), F.Relu, bias=kb)
-            mms([(y1, h("yT"), IdK), (y1, CA, h("Fc"))])
-            ts(qt(0), y1, HIGH, A.add, CEIL, A.min)
-            now[1] = "lists%d" % gi
-            mms([(L(0, NT), IdJ, at("JC", (0, NT), (q0, q1))), (L(2, 2), Id16, at("JK", (0, 2), (q0, q1))), (L(5), Id5, q("sF"))], True, False)
-            for r0 in range(0, 16, LR_CUT[gi]):
-                mms([(L(0, NT), at("LR", r), at(Qt, (0, 4 * NT), (0, 2), r)) for r in range(r0, r0 + LR_CUT[gi])], False, r0 + LR_CUT[gi] == 16)
+            ts(qt(3), at(cb, (0, 16)), -FLOOR, A.max)
+            ts(qt(1), at(cb, (16, 32)), off, A.max, top, A.min)
+            mms([(y1, h("yT"), Id512), (y1, CA, h("Fc"))])
+            ts(qt(0), y1, -HIGH, A.add, off, A.max)
             now[1] = "lowest%d" % gi
-            R = at("b4", (8 + lo // 32, 8 + hi // 32))
-            mms([(R, IdR, at("RK", 2))] + [(at("b4", (8 + lo // 32, 8 + hi // 32), a), at("PM", 2 * a + b), at(Qt, (4, 8), b)) for a in range(2) for b in range(2)])
-            turn32(at("O", (k0, k1)), R)
+            pairs = lambda nm, a0, j: [(at(nm, (a0, a0 + 4), a), at("PM", 2 * a + b), at("Qt", j, p, (b, 8, 2))) for a in range(2) for b in range(2)]
+            mms(pairs("b4", 8 + 4 * p, 3))
+            turn32(at("O", (k0, k1)), at("b4", (8 + 4 * p, 12 + 4 * p)))
             own = at("O", (k0, k1), (0, 4), 0)
-            mms([(at(ub, (4, 8)), IdR, at("RK", (1, 3))), (at(ub, (4, 6)), BM, qt(1)), (at(ub, (6, 8)), BM, qt(1))])
+            mms([(at(ub, (4, 6)), IdK, at("RK")), (at(ub, (4, 6)), BM, qt(3)), (at(ub, (6, 8)), BM, qt(3))])
             for d in range(4):
-                tt(at("EQ", (k0, k1), (64 * d + d, 256, 4)), at("O", (k0, k1), (d, 4)), at(ub, (6, 8) if d else (4, 6), (0, 4 - d)), A.is_equal)
+                tt(at("EQ", (k0, k1), (80 * d + (d - 1) % 5, 320, 5)), at("O", (k0, k1), (d, 4)), at(ub, (6, 8) if d else (4, 6), (0, 4 - d)), A.is_equal)
+            scaled("S", at("EQ", (k0, k1), (78, 320, 80)), own, 1.0 / 1024, 15 * FLOOR / 1024)
             for k in range(k1 - 1, k0 - 1, -1):
                 scan(at("lose", k), at("EQ", k), at("DM"))
-            tt(q("sc"), own, at("lose", (k0, k1), (63, 256, 64)), A.subtract)
-            tt(q("posU"), q("sc"), q("dump"), A.min)
+            for ka, kb in ((k0, k1),) if POS_CUT[gi] == 1 else ((k0 + 1, k1), (k0, k0 + 1)):
+                scaled("S", at("posU", (4 * ka, 4 * kb)), at("lose", (ka, kb), (78, 320, 80)), 8192.0, 2048.0 + SPARE)
             now[1] = "fork%d" % gi
-            if gi in FAST:
-                mms([(at(bank, (4, 8), a), at("PM", 2 * a + b), at(Qt, (16, 20), b)) for a in range(2) for b in range(2)])
-                turn32(at("O2"), at(bank, (4, 8)))
-                plus(FAST[gi], at("cs", 2 * t + gi, 0), at("O2", (0, 128, 16)), fork0)
-                plus(CS_ON, at("cs", 2 * t + gi, 1), L(5), 0.0)
-            else:
-                plus(CS_ON, at("cs", 2 * t + gi), L(4, 2), 0.0)
-            send(at("rcv", t, (q0, q1)), at("cs", 2 * t + gi, 0), "n%d_%d" % (t, gi), dst)
-            tt(q("m0"), L(1), at("cs", 2 * t + gi, 1), A.min)
+            mms(pairs(bank, 4, 1))
+            turn32(at("O2"), at(bank, (4, 8)))
+            scaled("S", at("cs", t, (q0, q1)), at("O2", (0, 128, 16)), 8.0, 131072.0 + 6144 + 8 * (lanes - OFF - TOP))
+            send(at("rcv", t, (q0, q1)), at("cs", t, (q0, q1)), "n%d_%d" % (t, gi), dst)
             now[1] = "column%d" % gi
-            ts(q("JC1"), own, -float(SPARE), A.add, 4095.0, A.min)
-            if SUM_ON[gi] == "P":
-                plus("S", h("old"), ind(swin, q("JC1")), -2048.0)
-                nc = at(bank, (0, 4))
-                mms([(nc, Id, qt(0)), (nc, Id, h("old"))])
-                plus("S", h("nc"), nc, 2048.0)
+            act(q("JC1"), own, F.Relu, scale=8.0, bias=2048.0 + 120 * FLOOR)
+            nc = at(bank, (0, 4))
+            plus("S", h("old"), ind(at("So") if gi and KEEP else swin, q("JC1")), -2048.0)
+            if gi in ROUND:
+                mms([(nc, IdN8, qt(0)), (nc, Id, con(0, 128)), (nc, IdN, h("old")), (nc, IdK, con(1, 128)), (nc, IdK, con(2, 128)), (nc, Id8, qt(0)), (nc, Id, h("old"))])
+                plus("S", h("nd"), nc, 2048.0)
             else:
-                tt(h("nc"), ind(swin, q("JC1")), qt(0), A.add)
-            ts(h("nd"), h("nc"), 4095, A.bitwise_and)
-            now[1] = "X%d" % gi
-            act(at(JU), L(2, 2), F.Relu)
-            act(at("zz", (2 * lo, 2 * hi)), ind(at(D), at(JU)), F.Abs)
+                mms([(nc, Id8, qt(0)), (nc, Id, h("old"))])
+                plus("S", h("nc"), nc, 2048.0)
+                ts(h("nd"), h("nc"), 4095, A.bitwise_and)
 
-        for gi in range(len(PARTS)):
+        def lists(gi, lo, hi):
+            now[1] = "lists%d" % gi
+            p0, p1, q0, q1 = lo // 128, hi // 128, lo // 16, hi // 16
+            w, n = p1 - p0, q1 - q0
+            L = lambda j, k=1: at("c%d" % gi, (32 + w * j, 32 + w * (j + k)))
+            q = lambda nm: at(nm, (q0, q1))
+            mms([(L(0, NT), IdK, at("JC", (0, NT), (q0, q1))), (L(2), Id5, q("sF"))], True, False)
+            for r0 in range(0, 16, LR_CUT[gi]):
+                mms([(L(0, NT), at("LR", (15 - r, 143 - r)), at("Qt", (0, NT), (p0, p1), (0, 8), r)) for r in range(r0, r0 + LR_CUT[gi])], False, r0 + LR_CUT[gi] == 16)
+            plus("S", q("none"), L(2), 14336.0)
+            tt(q("m0"), L(3), q("none"), A.max)
+            plus("S", q("yi"), L(0), 2048.0)
+            act(at("JU", (2 * q0, 2 * q1)), L(0, 2), F.Relu, scale=1.0 / 8192, bias=2047.5 - 16 * lo)
+            for a, b in ((n, 2 * n), (0, n)) if gi else ((0, 2 * n),):
+                act(at("zz", (2 * lo + 16 * a, 2 * lo + 16 * b)), ind(at(D, (16 * lo, 16 * hi)), at("JU", (2 * q0 + a, 2 * q0 + b))), F.Abs)
+
+        for gi in range(2):
             gathers(gi)
-        for gi in range(len(PARTS)):
+        for gi, (lo, hi) in enumerate(PARTS):
             claims(gi)
-        for names in turn.values():
-            for a, b in zip(names, names[1:]):
-                ops[b]["hard"].append(a)
+            if not join[0]:
+                lists(gi, lo, hi)
+        if join[0]:
+            lists(1, 0, 256)
         now[1] = "S"
         for j in range(3, -1, -1):
             cp(ind(at("Si"), at("posU", (4 * j, 4 * j + 4))), at("nd", (64 * j, 64 * j + 64)))
-        for gi, (lo, hi) in enumerate(PARTS):
+        for gi, (lo, hi) in enumerate(((0, 256),) if join[1] else PARTS):
             now[1] = "X%d" % gi
-            q0, q1 = lo // 16, hi // 16
-            act(at("yi", (q0, q1)), at("c%d" % gi, 32), F.Copy)
-            ts(at("y7", (q0, q1)), at("yi", (q0, q1)), 8199, A.bitwise_and)
-            w = at("WLU", (q0, q1))
-            tt(w, at("y7", (q0, q1)), at("I8", (q0, q1)), A.add)
-            cp(ind(at("XX", (0, X0 + 8 * hi)), w), at("zz", (2 * lo, lo + hi)))
+            q = lambda nm: at(nm, (lo // 16, hi // 16))
+            ts(q("y7"), q("yi"), X0 + 7, A.bitwise_and)
+            tt(q("WLU"), q("y7"), q("I8"), A.add)
+        for gi, (lo, hi) in enumerate(((0, 256),) if join[2] else PARTS):
+            now[1] = "X%d" % gi
+            cp(ind(at("XX", (0, X0 + 8 * hi)), at("WLU", (lo // 16, hi // 16))), z1(lo, hi))
             dma(T.yv[:, 8 * lo:8 * hi] if last else at("XX", (X0 + 2048 + 8 * lo, X0 + 2048 + 8 * hi)), at("XX", (X0 + 8 * lo, X0 + 8 * hi)))
         for gi, (lo, hi) in enumerate(PARTS):
             now[1] = "place%d" % gi
             q = lambda nm: at(nm, (lo // 16, hi // 16))
-            tt(q("m1"), q("m0"), at("rcv", t, (lo // 16, hi // 16)), A.min)
+            tt(q("m1"), q("m0"), at("rcv", t, (lo // 16, hi // 16)), A.max)
             ts(q("sL"), q("m1"), 4095, A.bitwise_and)
             if not last:
-                plus(C_ON[2 + gi], q("sU"), q("sL"), 0.0)
+                plus("S", q("sU"), q("sL"), 0.0)
         if last:
             cp(at("yso"), at("sL"))
             dma(T.ys[:], at("yso"))
         else:
-            act(at("jk"), at("cs", (2 * t, 2 * t + 2), 0), F.Sign, acc=acc, scale=-1.0, bias=100000.0)
+            act(at("jk"), at("cs", t), F.Sign, acc=acc)
             act(at("accB"), on, F.Identity, scale=kap, bias=acc)
         now[1] = "x"
-        xo = at("XC", (x0 + 512, x0 + 768))
+        xo = at("XC", (x0, x0 + 256))
         half = lambda b, lo, hi: at("b%d" % b, (lo // 32, hi // 32))
         for gi, (c0, c1) in enumerate(PARTS if last else ((0, 256),)):
-            mms([(half(0, c0, c1), IdN, at("XC", (x0 + 512 + c0, x0 + 512 + c1)))] +
-                [(half(0, lo, hi), Id, at("zz", (lo + hi, 2 * hi))) for lo, hi in PARTS if c0 <= lo < c1])
+            mms([(half(0, c0, c1), IdN, at("XC", (x0 + c0, x0 + c1)))] + [(half(0, lo, hi), Id, z2(lo, hi)) for lo, hi in both if c0 <= lo < c1])
             act(at("Y", t, (c0, c1)), half(0, c0, c1), F.Abs)
             send(at("XC", (x0 + 256 + c0, x0 + 256 + c1)), at("Y", t, (c0, c1)), "x%d" % (t + gi), dst)
         yh = half(1, 0, 256)
-        mms([(yh, IdH, xo), (yh, IdH, at("con", 0))] + [(half(1, lo, hi), IdH, at("zz", (2 * lo, lo + hi))) for lo, hi in PARTS])
-        if HALF_ON == "V":
-            ts(at("XC", (x0, x0 + 256)), yh, MAGIC, A.add, -MAGIC, A.add)
-        else:
-            act(at("ha"), yh, F.Identity, bias=MAGIC)
-            act(at("XC", (x0, x0 + 256)), at("ha"), F.Identity, bias=-MAGIC)
-        ts(at("xt"), at("m1"), 7, A.arith_shift_right, 768, A.bitwise_and)
+        mms([(yh, IdH, xo)] + [(half(1, lo, hi), IdH, z1(lo, hi)) for lo, hi in both])
+        plus("S", at("ha"), yh, -0.25)
+        plus("S", at("XC", (x0 + 512, x0 + 768)), at("ha"), 0.0)
+        ts(at("xt"), at("m1"), 9, A.arith_shift_right, 768, A.bitwise_and)
         tt(at("XLU"), at("xt"), at("Ic"), A.add)
-        xn = at("XC", (x0 + 1280, x0 + 1536))
-        act(xn, ind(at("XC", (x0, x0 + 768)), at("XLU")), F.Copy)
+        xn = at("XC", (x0 + 768, x0 + 1024))
+        plus("S", xn, ind(at("XC", (x0, x0 + 768)), at("XLU")), 0.0)
         if last:
             dma(T.yx[:], xn)
 
@@ -460,15 +467,13 @@ def build(core, T, topo, ops, EST):
         step(t)
 
     now[1] = "yt"
-    yt, blk, many = at("b0", (0, 8)), lambda nm, j, k=1, o=0: at(nm, (o + 256 * j, o + 256 * (j + k))), 2 * len(YT_ON)
-    for j in range(0, many, 2):
-        plus(YT_ON[j // 2], blk("S16", j, 2), blk("Si", j, 2, SPARE), -2048.0)
-        mms([(yt, Id, blk("S16", k)) for k in (j, j + 1)] + ([(yt, Id, at("con", 1))] if j == 0 else []), j == 0, j + 2 == many)
-    k = (16 - many) // 2
-    tt(blk("ysum", 0, k), blk("Si", many, k, SPARE), blk("Si", many + k, k, SPARE), A.add)
-    for j in range(1, k):
-        tt(blk("ysum", 0), blk("ysum", 0), blk("ysum", j), A.add)
-    tt(at("yto"), yt, blk("ysum", 0), A.add)
+    yt, a = at("b0", (0, 8)), 0
+    for q, k in YT_CUT:
+        b = a + 256 * k
+        plus(q, at("S16", (a, b)), at("Si", (SPARE + a, SPARE + b)), -2048.0)
+        mms([(yt, Id, at("S16", (c, c + 256))) for c in range(a, b, 256)], a == 0, b == 4096)
+        a = b
+    plus("V", at("yto"), yt, 16 * 2048.0)
     dma(T.yt[:], at("yto"))
 
 
@@ -498,114 +503,136 @@ def plan(ops, cases):
     names = sorted(set(o["q"] for o in ops) | set(b for o in ops for b in o["banks"]))
     queue = [names.index(o["q"]) if o["kind"] != "recv" else -1 for o in ops]
     banks = [[names.index(b) for b in sorted(o["banks"])] for o in ops]
-    hard = [o["hard"] for o in ops]
-    allp = [sorted(o["d"] | set(o["hard"])) for o in ops]
-    isdma = [o["kind"] == "dma" for o in ops]
-    succ = [[] for _ in range(n)]
+    near, hard, before = [], [], []
+    for o in ops:
+        far = 0
+        for j in o["d"]:
+            far |= before[j]
+        near.append(sorted(j for j in o["d"] if not far >> j & 1))
+        hard.append(sorted(j for j in set(o["hard"]) - o["d"] if not far >> j & 1))
+        before.append(far | sum(1 << j for j in o["d"]))
+    ways = []
+    for dur, wake, same in cases:
+        hold = [ops[i]["hold"] or dur[i] for i in range(n)]
+        ahead = [[(j, dur[j] + (same if queue[j] == queue[i] else wake)) for j in near[i]] + [(j, hold[j]) for j in hard[i]] for i in range(n)]
+        ways.append((dur, hold, wake, ahead))
+    dur, hold, wake, ahead = ways[0]
+    back = [[] for _ in range(n)]
     for i in range(n):
-        for j in allp[i]:
-            succ[j].append(i)
-    lags = [[[(j, same if queue[j] == queue[i] else wake) for j in sorted(ops[i]["d"])] for i in range(n)] for dur, wake, same in cases]
+        for j, w in ahead[i]:
+            back[j].append((i, dur[i] + w - dur[j]))
+    span, rank = np.array(dur), np.arange(n)
+    fore = [(i, queue[i], ahead[i], hold[i] - 1e-9, 0.0, banks[i]) for i in range(n)]
+    aft = [(i, queue[i], back[i], hold[i] - 1e-9, dur[i] - hold[i], banks[i]) for i in range(n)]
+
+    def fit(order, calls):
+        begin = [0.0] * n
+        used = [[] for _ in names]
+        for x in order:
+            i, q, edges, h, late, bs = calls[x]
+            s = 0.0
+            for j, w in edges:
+                w += begin[j]
+                if w > s:
+                    s = w
+            if q >= 0:
+                s += late
+                u = used[q]
+                while True:
+                    k = m = len(u)
+                    while k and u[k - 1][1] > s:
+                        k -= 1
+                    while k < m and u[k][0] < s + h:
+                        s = u[k][1]
+                        k += 1
+                    t = s
+                    for b in bs:
+                        for y, z, p in used[b][-8:]:
+                            if p != q and y < s + h + wake and z > s:
+                                s = z
+                    if s == t:
+                        break
+                u.insert(k, (s, s + h))
+                for b in bs:
+                    used[b].append((s, s + h + wake, q))
+                s -= late
+            begin[i] = s
+        return np.array(begin)
 
     def run(c, order):
-        dur, wake, lag = cases[c][0], cases[c][1], lags[c]
-        end, why, issued = [0.0] * n, [-1] * n, [0.0] * n
-        free, last, user = [0.0] * len(names), [-1] * len(names), [{} for _ in names]
+        dur, hold, wake, ahead = ways[c]
+        begin, free, user = [0.0] * n, [0.0] * len(names), [{} for _ in names]
+        top = 0.0
         for i in order:
-            s, w, q = 0.0, -1, queue[i]
-            for j, d in lag[i]:
-                if end[j] + d > s:
-                    s, w = end[j] + d, j
-            for j in hard[i]:
-                if issued[j] > s:
-                    s, w = issued[j], j
-            if q >= 0 and free[q] > s:
-                s, w = free[q], -2 - last[q]
+            q = queue[i]
+            s = free[q] if q >= 0 else 0.0
+            for j, w in ahead[i]:
+                w += begin[j]
+                if w > s:
+                    s = w
             for b in banks[i]:
-                for p, j in user[b].items():
-                    if p != q and end[j] + wake > s:
-                        s, w = end[j] + wake, -2 - j
-                user[b][q] = i
-            end[i], why[i] = s + dur[i], w
-            issued[i] = s + 0.1 if isdma[i] else end[i]
+                for p, y in user[b].items():
+                    if p != q and y > s:
+                        s = y
+            e = s + dur[i]
+            for b in banks[i]:
+                user[b][q] = e + wake
+            begin[i] = s
             if q >= 0:
-                free[q], last[q] = issued[i], i
-        top = max(end)
-        i, held = end.index(top), []
-        while why[i] != -1:
-            j = why[i] if why[i] >= 0 else -2 - why[i]
-            if why[i] < 0:
-                held.append((j, i))
-            i = j
-        return top + EARLY * sum(end) / n, held
+                free[q] = s + hold[i]
+            if e > top:
+                top = e
+        return top
 
-    turn = TURN.split()
-    period = 20.0
-    shift = [period * o["step"] for o in ops]
-    slots = {}
-    slot = [slots.setdefault(o["slot"], len(slots)) for o in ops]
-    place = [None] * len(slots)
-    for i, o in enumerate(ops):
-        nm = o["slot"]
-        if o["task"] == "start":
-            place[slot[i]] = max([place[slot[j]] + 0.3 for j in allp[i]] + [0.001 * i - period])
-        elif place[slot[i]] is None:
-            place[slot[i]] = place[slot[i - 1]] + 0.01
-            for mark, late in (("", 0), ("+", 1), ("-", -1)):
-                if nm + mark in turn:
-                    place[slot[i]] = period * (turn.index(nm + mark) / len(turn) + late)
-
-    def judge(place):
-        key = [0.0] * n
+    def both(key, limit):
         for i in range(n):
-            k = place[slot[i]] + shift[i]
-            for j in allp[i]:
-                if key[j] >= k:
-                    k = key[j] + 1e-6
-            key[i] = k
-        order = sorted(range(n), key=lambda i: key[i])
-        res = [run(c, order) for c in range(len(cases))]
-        return sum(x[0] for x in res), res, order
+            for j, w in ahead[i]:
+                if key[j] > key[i]:
+                    key[i] = key[j]
+        a = fit(np.lexsort((rank, key)).tolist(), fore)
+        b = fit(np.lexsort((-rank, -a - span)).tolist(), aft)
+        a = fit(np.lexsort((rank, -b - span)).tolist(), fore)
+        top = (a + span).max()
+        if top > limit:
+            return None
+        order = np.lexsort((rank, a)).tolist()
+        return sum(run(k, order) for k in range(len(cases))) / len(cases), a, order, top
 
     rng = np.random.default_rng(SEED)
-    cost, now, order = judge(place)
-    best = (cost, order, place)
-    for stage, rounds in enumerate(ROUNDS):
-        if stage == 1:
-            place = [best[2][slot[i]] for i in range(n)]
-            slot = list(range(n))
-            cost, now, order = judge(place)
-            best = (cost, order, place)
-        for it in range(rounds):
-            held = now[int(rng.integers(len(cases)))][1]
-            new = list(place)
-            way = 1 if rng.random() < 0.5 else -1
-            if rng.random() < 0.85:
-                j, i = held[int(rng.integers(len(held)))][::-way]
-                todo = [(i, new[slot[j]] + shift[j] + way * (0.001 + float(rng.random()) ** 3))]
-            else:
-                i = int(rng.integers(n))
-                todo = [(i, new[slot[i]] + shift[i] + way * 1.5 * float(rng.random()))]
-            count = 0
-            while todo and count < 40:
-                x, k = todo.pop()
-                if (new[slot[x]] + shift[x] - k) * way < 0:
-                    new[slot[x]] = k - shift[x]
-                    todo += [(y, k + way * 0.001) for y in (succ if way > 0 else allp)[x]]
-                    count += 1
-            if count < 40:
-                c, res, o = judge(new)
-                if c <= cost + MARGIN * (1 - it / rounds) * float(rng.random()):
-                    place, now, cost = new, res, c
-                    if c < best[0]:
-                        best = (c, o, place)
+    slots = {}
+    slot = np.array([slots.setdefault(o["slot"], len(slots)) for o in ops])
+    step = np.array([o["step"] for o in ops])
+    inner = np.array([o["task"] not in ("start", "yt") for o in ops])
+    first = [i for i in range(n) if ops[i]["slot"] == "cU.gathers.1"]
+    late = -fit(range(n - 1, -1, -1), aft) - span
+    turn = ORDER.split()
+    place = {x.strip("+-"): j / len(turn) + x.count("+") - x.count("-") for j, x in enumerate(turn)}
+    now = best = both([late[i] - 1e3 if o["task"] == "start" else o["step"] + place.get(o["slot"], 0.0) for i, o in enumerate(ops)], 1e9)
+    for it in range(TRIES):
+        key = now[1]
+        tied = it < TIED * TRIES
+        if tied or rng.random() < ALIKE:
+            t0, mine = key[first], inner & (step == (1 if tied else rng.integers(len(first))))
+            rel = np.full(len(slots), 1e9)
+            rel[slot[mine]] = (key - t0[step])[mine]
+            close = np.abs(rel - rng.random() * 24) < (1 if tied else 2) * SPAN * rng.random()
+            if tied:
+                rel += close * rng.normal(0, NOISE * rng.random(), len(slots))
+            key = np.where(inner & (rel < 1e8 if tied else close)[slot], rel[slot] + t0[step], key)
+        else:
+            key = key + (np.abs(key - rng.random() * key.max()) < SPAN * rng.random()) * rng.normal(0, NOISE * rng.random(), n)
+        new = both(key.tolist(), now[3] + 1.0)
+        if new and new[0] <= now[0] + SLACK * (1 - it / TRIES) * rng.random():
+            now = new
+            if new[0] < best[0]:
+                best = new
     extra, users = [], {}
-    for i in best[1]:
+    for i in best[2]:
         for b in sorted(ops[i]["banks"]):
             u = users.setdefault(b, {})
             extra += [(i, j) for q, j in u.items() if q != ops[i]["q"]]
             u[ops[i]["q"]] = i
-    return best[1], extra, best[0] / len(cases)
+    return best[2], extra, best[0]
 
 
 def rank_program(g, core, T, topo):

import numpy as np
from concourse.mybir import AluOpType as A, ActivationFunctionType as F

STEPS = 4
PARTS = ((128, 256), (0, 128))
G_CUT = ((224, 256, "V"), (192, 224, "S"), (160, 192, "V"), (128, 160, "S"), (64, 128, "V"), (32, 64, "V"), (0, 32, "S"))
AB_CUT = (((192, 256, 0, 5, "S"), (128, 192, 0, 5, "S")), ((64, 128, 0, 1, "V"), (0, 64, 0, 5, "V")))
X_CUT = (((192, 256), (128, 192)), ((64, 128), (32, 64), (0, 32)))
Z_CUT = (((192, 256, "S"), (128, 192, "V")), ((64, 128, "S"), (32, 64, "S"), (0, 32, "V")))
U_CUT = (((128, 192, "D"), (128, 256, "Z")), ((0, 32, "D"), (0, 128, "Z")))
GT_ON = "SV"
ROUND = (1,)
KEEP = 1
JOIN = "110"
LR_CUT = (8, 16)
POS_CUT = (1, 2)
YT_CUT = (("S", 1), ("V", 2), ("S", 2), ("V", 2), ("S", 2), ("V", 2), ("S", 2), ("S", 2), ("V", 1))
ER_ON = "VVVS"
W_FILL = 8
MAGIC = 12582912.0
HIGH = 65536.0
FLOOR = 33024.0
OFF = 33280.0
TOP = 49152.0
SPARE = 256
X0 = 4096
NT = 4
ORDER = """
cU.gathers.1 XC.x.1+ G.gathers.1 m1.place1.1+ G.gathers.2 XX.X1.2+ sL.place1.1+ G.gathers.4 sU.place1.1+ b5.gathers.1 G.gathers.3 cU.gathers.2 xt.x.1+ b0.gathers.1
AB.gathers.1 G.gathers.5 G.gathers.7 So.var0.1 b5.gathers.2 sF.gathers.1 GT.gathers.1 AB.gathers.2 b0.gathers.2 Xa.var0.1 G.gathers.6 b1.gathers.1 AB.gathers.3
b5.gathers.3 XLU.x.1+ AB.gathers.4 cF.gathers.1 Xa.var0.2 D.var0.1 b1.gathers.2 b4.E.1 Xa.var1.1 GT.gathers.2 AB.gathers.5 D.var0.2 b1.gathers.3 c0.E.1 c1.E.1
Z.var0.1 AB.gathers.6 b2.var0.2 Z.var0.2 rE.E.1 D.var1.1 b2.var0.3 Xa.var1.2 b4.E.2 Xa.var1.3 D.var1.2 rq.claim0.1 Z.var1.1 D.var1.3 yT.claim0.1 b3.var1.2 Z.var1.2
Z.var1.3 b2.claim0.1 sq.claim0.1 b3.var1.3 XC.x.3+ tb.claim0.1 Qt.tables0.1 Fc.claim0.1 rq.claim1.1 c0.tables0.1 b2.tables0.1 yT.claim1.1 Qt.tables0.3 Qt.tables0.2
b3.claim1.1 Qt.tables0.4 b0.fork0.1 sq.claim1.1 b4.lowest0.1 Qt.tables1.1 O2.fork0.1 b2.lowest0.1 tb.claim1.1 O.lowest0.1 cs.fork0.1 b2.var0.1- Fc.claim1.1
cs.fork0.2 JC1.column0.1 EQ.lowest0.3 EQ.lowest0.5 EQ.lowest0.1 c1.tables1.1 EQ.lowest0.2 old.column0.1 EQ.lowest0.4 b3.tables1.1 Qt.tables1.3 rcv.fork0.1
Qt.tables1.2 Qt.tables1.4 b1.fork1.1 lose.lowest0.2 b0.column0.1 O2.fork1.1 b4.lowest1.1 lose.lowest0.1 b3.lowest1.1 cs.fork1.1 O.lowest1.1 nc.column0.1 c1.lists1.1
cs.fork1.2 posU.lowest0.1 c1.lists1.2 JC1.column1.1 nd.column0.1 EQ.lowest1.5 EQ.lowest1.4 EQ.lowest1.1 old.column1.1 Si.S.1 rcv.fork1.1 jk.place1.1 EQ.lowest1.2
JU.lists1.1 b1.column1.1 yi.lists1.1 EQ.lowest1.3 Si.S.2 none.lists1.1 zz.lists1.2 y7.X0.1 b3.var1.1- m0.lists1.1 lose.lowest1.2 nd.column1.1 WLU.X0.1 zz.lists1.1
lose.lowest1.1 b1.x.1 XX.X0.1 posU.lowest1.1 posU.lowest1.2 b0.x.1 ha.x.1 m1.place0.1 Si.S.3 accB.place1.1 XX.X0.2 Y.x.1 sL.place0.1 Si.S.4 sU.place0.1 Y.x.2
XC.x.2 XX.X1.1
"""

SCRATCH = {
    "Si": ("sbuf", [128, SPARE + 8192], "int32"),
    "So": ("sbuf", [128, 4096], "int32"),
    "XX": ("sbuf", [128, X0 + 4096], "bfloat16"),
    "XC": ("sbuf", [128, (STEPS + 1) * 768], "bfloat16"),
    "c0": ("psum", [128, 64, 8], "float32"),
    "c1": ("psum", [128, 64, 8], "float32"),
}
for _dt, _shapes in (
        ("bfloat16", {"Xa": [4096], "on": [256], "SEL": [16, 2, 8], "ER": [16, 128], "LR": [144], "WG": [2, 8], "PM": [4, 4, 32], "W": [32, 144],
                      "BI": [128], "BM": [4, 32], "Id": [4, 32], "mat": [16, 128], "con": [4, 256], "jk": [16], "zz": [512], "Y": [STEPS, 256], "RK": [128],
                      "D0": [4096], "D1": [4096], "Z0": [4096], "Z1": [4096]}),
        ("float16", {"GT": [512], "rE": [256], "G": [4096], "S16": [4096], "yT": [256], "JC": [NT, 16], "sF": [16], "accB": [128], "cF": [256], "rq": [256],
                     "old": [256], "Fc": [256], "Qt": [NT, 2, 8, 16], "EQ": [4, 320], "lose": [4, 320], "DM": [320]}),
        ("float32", {"r128": [128], "EQc": [16], "q16": [16], "Ic": [16], "I8": [16], "col": [8], "m0": [16], "O": [4, 4, 16], "O2": [128],
                     "yto": [256], "yso": [16], "rcv": [STEPS, 16], "cs": [STEPS, 16], "none": [16]}),
        ("int32", {"nc": [256], "ha": [256], "pI": [4], "wI": [1], "sL0": [16], "sL": [16], "m1": [16], "yi": [16], "y7": [16], "xt": [16], "sq": [256], "tb": [256], "nd": [256]}),
        ("uint16", {"AB": [512], "sU": [16], "WLU": [16], "XLU": [16], "posU": [16], "cU": [256], "JC1": [16], "JU": [32]})):
    for _nm in _shapes:
        SCRATCH[_nm] = ("sbuf", [128] + _shapes[_nm], _dt)
for _b in (0, 1, 4, 5):
    SCRATCH["b%d" % _b] = ("psum", [128, 16, 2, 16], "float32")
for _b in (2, 3):
    SCRATCH["b%d" % _b] = ("psum", [128, 8, 4, 16], "float32")

SEMAPHORES = ["eV", "eS", "eP", "eG", "ax%d" % STEPS, "lx%d" % STEPS] + ["m%d" % i for i in range(24)]
for _t in range(STEPS):
    for _nm in ("x%d" % _t, "n%d_0" % _t, "n%d_1" % _t):
        SEMAPHORES += ["a" + _nm, "l" + _nm]

EST = {"cyc": 0.00083 * 1.05, "V": 0.02, "S": 0.04, "ind": 0.12, "ga": 1.2, "sc": 3.5, "pe": 0.00058, "wake": 0.14, "same": 0.19, "net": 3.2, "dma": 1.3, "rate": 450e3}
CASES = ({}, {"pe": 0.0008}, {"cyc": 0.00083 * 1.4, "pe": 0.0008, "ga": 1.5, "sc": 5.0}, {"net": 4.2, "ga": 1.05, "sc": 2.0, "cyc": 0.00083, "pe": 0.00045, "rate": 280e3, "dma": 2.0, "ind": 0.06})
ISSUE = 0.1
SEED = 2
TRIES = 6000
TIED = 0.2
ALIKE = 0.15
SPAN = 3.0
NOISE = 1.0
SLACK = 0.08
COLUMNS = {}
PLAN = {}
SIZE = {"float32": 4, "int32": 4, "bfloat16": 2, "float16": 2, "uint16": 2}


def build(core, T, topo, ops, EST):
    rank = T.rank_of(core)
    cyc = EST["cyc"]
    times, now, group = {}, [-1, "start"], {}

    def at(name, *idx):
        where, shape, dt = SCRATCH[name]
        cut = tuple(slice(*i) if isinstance(i, tuple) else i for i in idx)
        if (name, idx) not in COLUMNS:
            bits = np.zeros(shape[1:], np.uint8)
            bits[cut] = 1
            COLUMNS[(name, idx)] = (int.from_bytes(np.packbits(bits, bitorder="little").tobytes(), "little"), int(bits.sum()))
        m, k = COLUMNS[(name, idx)]
        ap = T[name][(slice(None),) + cut] if idx else T[name][:]
        return {"ap": ap, "acc": (name, m), "n": k, "two": SIZE[dt] == 2, "ps": where == "psum", "off": None, "bytes": 128 * k * SIZE[dt]}

    def ind(win, off):
        return dict(win, ap=win["ap"].indirect(off["ap"]), n=16 * off["n"], off=off["acc"])

    def val(x):
        return x["ap"] if isinstance(x, dict) else x

    def add(q, fn, dur, outs, ins, kind="c", sem=None, cnt=1, hold=None):
        r = [x["acc"] for x in ins if isinstance(x, dict)] + [x["off"] for x in ins + outs if isinstance(x, dict) and x["off"]]
        w = [x["acc"] for x in outs]
        banks = set(x["acc"][0] for x in ins + outs if isinstance(x, dict) and x["ps"])
        buf = (w + r)[0][0]
        name = "%s.%s" % (buf[0] if buf in ("D0", "D1", "Z0", "Z1") else buf, now[1])
        times[name] = times.get(name, 0) + 1
        ops.append({"slot": "%s.%d" % (name, times[name]), "task": now[1], "step": max(now[0], 0), "q": q, "fn": fn, "dur": dur, "r": r, "w": w,
                    "kind": kind, "sem": sem, "cnt": cnt, "banks": banks, "hard": [], "hold": hold})

    def time(q, out, i0, per):
        if out["off"]:
            return EST[q] + EST["ind"] + cyc * EST["sc"] * out["n"]
        if i0["off"]:
            return EST[q] + EST["ind"] + cyc * EST["ga"] * i0["n"]
        return EST[q] + cyc * max(64, per * out["n"])

    def ts(out, i0, s1, op0, s2=None, op1=None):
        a = (val(out), val(i0), val(s1), val(s2), op0) + ((op1,) if op1 is not None else ())
        add("V", lambda e: e.tensor_scalar(*a), time("V", out, i0, 0.5 if out["two"] and i0["two"] else 1), [out], [i0, s1, s2])

    def tt(out, i0, i1, op):
        add("V", lambda e: e.tensor_tensor(val(out), val(i0), val(i1), op), time("V", out, i0, 1 if i0["ps"] or i1["ps"] else 2), [out], [i0, i1])

    def cp(out, i0):
        add("V", lambda e: e.tensor_copy(val(out), val(i0)), time("V", out, i0, 0.5 if out["two"] and i0["two"] else 1), [out], [i0])

    def fill(out, c):
        add("V", lambda e: e.memset(val(out), c), time("V", out, out, 0.5 if out["two"] else 1), [out], [])

    def turn32(out, i0):
        add("V", lambda e: e.transpose(val(out), val(i0)), time("V", out, i0, 1), [out], [i0])

    def scan(out, i0, i1):
        add("V", lambda e: e.tensor_tensor_scan(val(out), val(i0), val(i1), 0.0, A.max, A.add), time("V", out, out, 0.5), [out], [i0, i1])

    def act(out, i0, f, acc=None, **k):
        kw = {n: val(v) for n, v in k.items()}
        if acc:
            kw["accum_out"] = val(acc)
        add("S", lambda e: e.activation(val(out), val(i0), f, **kw), time("S", out, i0, 1), [out] + ([acc] if acc else []), [i0] + list(k.values()))

    def plus(q, out, i0, c):
        if q == "S":
            act(out, i0, F.Identity, bias=c)
        else:
            ts(out, i0, c, A.add)

    def scaled(q, out, i0, c, b=0.0):
        if q == "S":
            act(out, i0, F.Identity, scale=c, bias=b)
        else:
            ts(out, i0, c, A.mult, b, A.add)

    def mms(calls, start=True, stop=True):
        first, m = [], 0
        for j, c in enumerate(calls):
            first.append(start and (j == 0 or c[0]["acc"][1] & ~m != 0))
            if first[j]:
                m = c[0]["acc"][1]
        first.append(stop)

        def run(e):
            last = None
            for j, c in enumerate(calls):
                last = e.matmul(val(c[0]), val(c[1]), val(c[2]), first[j], first[j + 1])
            return last
        outs = [c[0] for c in calls]
        add("P", run, 0.03 + EST["pe"] * sum(max(min(64, c[1]["n"]), c[2]["n"]) for c in calls), outs,
            [c[1] for c in calls] + [c[2] for c in calls] + ([] if start else outs))
        ops[-1].update({"goes on": not start, "open": not stop})
        closed, since = group.setdefault(outs[0]["acc"][0], [[], []])
        if start:
            ops[-1]["hard"] += closed + ([] if stop else since)
            since.append(len(ops) - 1)
        elif stop:
            closed[:], since[:] = [len(ops) - 1], []

    def asel(out, i0, pat, op, base, cm, other=0.0):
        add("G", lambda e: e.affine_select(val(out), val(i0), pat, op, other, base, cm), 0.17 + 2 * cyc * out["n"], [out], [i0])

    def iota(out, pat, cm, **k):
        add("G", lambda e: e.iota(val(out), pat, 0, cm, **k), 0.13 + 2 * cyc * out["n"], [out], [])

    ndma = [0]

    def dma(out, i0, behind=0.0, after=None):
        s = "m%d" % ndma[0]
        ndma[0] += 1
        sb = out if isinstance(out, dict) else i0
        add("Y", lambda e: e.dma_start(val(out), val(i0)), EST["dma"] + (behind + sb["bytes"]) / EST["rate"], [out] if isinstance(out, dict) else [],
            [i0, after], "dma", s, 16, ISSUE)

    def send(out, i0, sem, dst):
        rid, pid = topo.addr(dst)[0], topo.addr(dst)[1]
        eng = topo.engines(core, dst)[:8]
        mask = sum(1 << e for e in eng)
        add("G", lambda e: e.remote_dma(val(out), val(i0), T.sem["a" + sem], T.sem["l" + sem], pid, rid, mask), 0.6, [], [i0], "send", "a" + sem, len(eng))
        add("N", None, EST["net"] + out["bytes"] / 60e3, [out], [i0], "recv", "a" + sem, len(eng))
        ops[-1]["hard"].append(len(ops) - 2)

    behind = 0
    for out, src in ((at("sL0"), T.s0), (at("Si", (SPARE, SPARE + 4096)), T.stm), (at("XX", (X0, X0 + 2048)), T.vx),
                     (at("XX", (X0 + 2048, X0 + 4096)), T.vx), (at("wI"), T.wt), (at("XC", (0, 256)), T.x0)):
        dma(out, src[:], behind)
        behind += out["bytes"]
    for j in range(1, len(ops)):
        ops[j]["hard"].append(j - 1)

    Id, BM, on = at("Id"), at("BM"), at("on", (0, 128))
    kcol, row8, c16, wF, acc, kap, off, top = [at("col", (j, j + 1)) for j in range(8)]
    IdK, Id5, IdH, IdN, IdN16, Id8, Id8i, Id512, IdU, IdLow, IdN8, BMn, CA, CB = [at("mat", j) for j in range(14)]
    con = lambda j, n=256: at("con", j, (0, n))
    fill(at("on"), 1.0)
    iota(at("pI", (0, 1)), [[0, 1]], 1)
    iota(at("q16"), [[16, 16]], 0, allow_small_or_imprecise_dtypes=True)
    iota(at("r128"), [[0, 8], [1, 16]], 0, allow_small_or_imprecise_dtypes=True)
    asel(Id, on, [[-1, 128]], A.is_equal, 0, 1)
    asel(at("BI"), on, [[-16, 8], [0, 16]], A.is_ge, 0, 1)
    asel(BM, at("BI"), [[16, 8], [0, 16]], A.is_ge, 15, -1)
    asel(at("SEL", (0, 16), 0), on, [[-1, 16], [-16, 8]], A.is_equal, 0, 1)
    asel(at("SEL", (0, 16), 1), on, [[-2, 8], [1, 2], [-16, 8]], A.is_equal, -1, 1)
    moved = len(set(c[2] for part in AB_CUT for c in part))
    if moved:
        fill(at("W", (0, W_FILL)), 0.0)
    for r in range(W_FILL, 16 * moved, W_FILL):
        k = min(W_FILL, 16 * moved - r)
        act(at("W", (r, r + k)), at("W", (0, k)), F.Copy)
    for j in range(moved):
        cp(at("W", (16 * j, 16 * j + 16), (15, 143, 16)), at("SEL", (0, 16), j))
    ts(BMn, BM, -HIGH, A.mult)
    asel(at("BI"), BMn, [[1, 128]], A.is_ge, -1, -1)
    asel(CA, at("BI"), [[-1, 128]], A.not_equal, 0, 1, HIGH)
    asel(CB, at("BI"), [[-1, 128]], A.not_equal, 0, 1, 2 * HIGH)
    ts(at("pI", (2, 3)), at("pI", (0, 1)), 15, A.bitwise_and)
    cp(kcol, at("pI", (2, 3)))
    ts(row8, kcol, 0.0, A.is_equal, 0.125, A.mult)
    ts(kap, row8, -16.0, A.mult, -384.0, A.add)
    ts(off, kcol, -1024.0, A.mult, -OFF, A.add)
    ts(top, kcol, -1024.0, A.mult, TOP - OFF, A.add)
    fill(c16, 16.0)
    cp(wF, at("wI"))
    ts(at("EQc"), at("r128", (0, 16)), kcol, A.is_equal)
    for r in range(16):
        scaled(ER_ON[r % len(ER_ON)], at("ER", r), BM, at("EQc", (r, r + 1)))
    fill(at("LR"), 0.0)
    ts(at("LR", (15, 143, 16)), at("BM", (0, 4), (0, 32, 16)), 8.0, A.mult)
    for j in range(2):
        ts(at("WG", j), at("BM", (0, 4), (0, 32, 16)), wF, A.mult, (1.0 - 2 * j) / 4096, A.mult)
    for m, f in ((IdLow, -HIGH), (Id8i, 0.125), (IdN, -1.0), (IdN16, -16.0), (IdU, 1152.0), (IdK, 4096.0), (Id512, 512.0),
                 (Id5, 5.0), (Id8, 8.0), (IdN8, -8.0), (IdH, 0.5)):
        asel(m, Id, [[-1, 128]], A.not_equal, 0, 1, f)
    for j, c in enumerate((-0.5, MAGIC, -MAGIC)):
        fill(con(j, 128 if j else 256), c)
    ts(at("RK"), at("r128"), kcol, A.is_ge)
    ts(at("Ic"), at("q16"), kcol, A.add)
    fill(at("EQ"), 0.0)
    fill(at("DM"), 0.0)
    fill(at("DM", (79, 320, 80)), -4.0)
    ts(at("DM", (77, 320, 80)), at("Ic", (0, 4)), -1.0 / 2048, A.mult, -0.25 - 1.0 / 2048, A.add)
    fill(at("PM"), 0.0)
    for a in range(2):
        for b in range(2):
            act(at("PM", 2 * a + b, (0, 4), (16 * b, 16 * b + 16)), at("BM", (0, 4), (16 * a, 16 * a + 16)), F.Copy)
    lanes = 16 * OFF + 1024 * 120
    for j, c in enumerate((1 + (lanes - OFF) / 512, 1 + (lanes - OFF - TOP) / 512)):
        ts(at("JC", j), at("Ic"), 32.0, A.mult, c - 4096, A.add)
    fill(at("JC", 2), 0.0)
    fill(at("JC", 3), 64.5 + 15 * FLOOR / 512)
    ts(at("I8"), at("Ic"), 8.0, A.mult)
    act(at("accB"), on, F.Identity, scale=kap)
    cp(at("sU"), at("sL0"))

    swin, xwin = at("Si", (SPARE, SPARE + 4096)), at("XX", (X0, X0 + 4096))

    def step(t):
        last = t + 1 == STEPS
        D, Z = "D%d" % (t % 2), "Z%d" % (t % 2)
        x0 = 768 * t
        now[:] = [t, "gathers"]
        times.clear()
        dst = T.cores[(rank + 1 + t % (len(T.cores) - 1)) % len(T.cores)]
        join = [c == "1" and not last for c in JOIN]
        both = ((0, 256),) if join[0] else PARTS
        z1 = lambda lo, hi: at("zz", (lo, hi) if join[0] else (2 * lo, lo + hi))
        z2 = lambda lo, hi: at("zz", (256 + lo, 256 + hi) if join[0] else (lo + hi, 2 * hi))
        for lo, hi in PARTS:
            plus("S", at("cU", (lo, hi)), ind(swin, at("sU", (lo // 16, hi // 16))), 0.0)
        plus("S", at("sF"), at("sU"), -2048.0)
        plus("V", at("cF"), at("cU"), -2048.0)
        for lo, hi, q in G_CUT:
            plus(q, at("G", (16 * lo, 16 * hi)), ind(swin, at("cU", (lo, hi))), -2048.0)
        now[1] = "E"
        E = at("b4", (0, 8))
        whole = [(E, IdN, at("cF")), (E, at("accB"), con(0))] + [(at("b4", (0, 8), (0, 2), r), at("ER", r), at("sF")) for r in range(16)]
        mms(whole)
        scaled("S", at("rE"), E, 1.0 / 16, -15.0 / 32)
        mms(whole + [(E, IdN16, at("rE"))])
        for gi, (lo, hi) in enumerate(PARTS):
            mms([(at("c%d" % gi, (0, 32)), IdLow, at("on"))] + [(at("c%d" % gi, (16 * j, 16 * j + 16)), Id8i, at("cF", (lo, hi))) for j in range(2)], True, False)

        def gathers(gi):
            now[1] = "gathers"
            lo, hi = PARTS[gi]
            ub = "b%d" % (2 + gi)
            bank, o = "b%d" % gi, 2 * lo
            for c0, c1, j, b, q in AB_CUT[gi]:
                wide = at("b%d" % b, (0, (c1 - c0) // 32))
                mms([(wide, at("W", 16 * j + k, (15 - k, 143 - k)), at("G", (16 * c0 + k, 16 * c1, 16))) for k in range(16)])
                plus(q, at("AB", (lo + 128 * j + c0, lo + 128 * j + c1)), wide, 2048.0)
            sides = [j for j in range(2) if j not in [c[2] for c in AB_CUT[gi]]]
            if sides:
                j0, j1 = sides[0], sides[-1] + 1
                mms([(at(bank, (4 * j0, 4 * j1), (0, 2), k), at("G", (16 * lo + k, 16 * hi, 16)), at("SEL", k, (j0, j1))) for k in range(16)])
                plus(GT_ON[gi], at("GT", (o + 128 * j0, o + 128 * j1)), at(bank, (4 * j0, 4 * j1)), 0.0)
                mms([(at(bank, (4 * j, 4 * j + 4)), at("GT", (o + 128 * j, o + 128 * j + 128)), Id) for j in sides])
                plus("V", at("AB", (o + 128 * j0, o + 128 * j1)), at(bank, (4 * j0, 4 * j1)), 2048.0)
            now[1] = "var%d" % gi
            if gi == KEEP - 1:
                dma(at("So"), swin, after=at("AB", (o + 64, o + 128)))
                ops[-1]["hard"] += [j for j in range(len(ops) - 1) if ops[j]["kind"] == "dma"]
            for c0, c1 in X_CUT[gi]:
                plus("S", at("Xa", (16 * c0, 16 * c1)), ind(xwin, at("AB", (lo + c0, lo + c1))), 0.0)
            for c0, c1 in X_CUT[gi]:
                a, b = 16 * c0, 16 * c1
                tt(at(D, (a, b)), ind(xwin, at("AB", (hi + c0, hi + c1))), at("Xa", (a, b)), A.subtract)
            for c0, c1, q in Z_CUT[gi]:
                a, b = 16 * c0, 16 * c1
                if q == "V":
                    ts(at(Z, (a, b)), at(D, (a, b)), 0.0, A.max, 2.0, A.mult)
                else:
                    act(at(Z, (a, b)), at(D, (a, b)), F.Abs)
            mms([(at(ub, (0, 2)), IdU, on)], True, False)
            for c0, c1, src in U_CUT[gi]:
                mms([(dict(at(ub, (0, 2), (0, 4), k), ap=T[ub][c0 - lo:c1 - lo, 0:2, 0:4, k]), at(D if src == "D" else Z, (16 * c0 + k, 16 * c1, 16)),
                      at("WG", int(src == "D"))) for k in range(16)], False, src == "Z")

        def claims(gi):
            lo, hi = PARTS[gi]
            p, q0, q1, k0, k1 = lo // 128, lo // 16, hi // 16, lo // 64, hi // 64
            ub, bank, cb = "b%d" % (2 + gi), "b%d" % gi, "c%d" % gi
            h = lambda nm: at(nm, (lo, hi))
            q = lambda nm: at(nm, (q0, q1))
            qt = lambda j: at("Qt", j, p)
            y, y1 = at(ub, (0, 2)), at(ub, (2, 4))
            now[1] = "claim%d" % gi
            act(h("rq"), y, F.Identity, bias=1.0 / 8192)
            tt(h("yT"), y, h("rq"), A.subtract)
            mms([(y, h("yT"), IdK)])
            act(h("sq"), y, F.Square, bias=c16)
            ts(h("tb"), h("sq"), 5, A.arith_shift_right, 15, A.bitwise_and)
            tt(h("Fc"), h("tb"), at("b4", (lo // 32, hi // 32)), A.is_equal)
            now[1] = "tables%d" % gi
            act(qt(2), y, F.Copy, scale=row8)
            mms([(at(cb, (0, 16)), CA, h("Fc")), (at(cb, (16, 32)), CB, h("Fc"))], False)
            ts(qt(3), at(cb, (0, 16)), -FLOOR, A.max)
            ts(qt(1), at(cb, (16, 32)), off, A.max, top, A.min)
            mms([(y1, h("yT"), Id512), (y1, CA, h("Fc"))])
            ts(qt(0), y1, -HIGH, A.add, off, A.max)
            now[1] = "lowest%d" % gi
            pairs = lambda nm, a0, j: [(at(nm, (a0, a0 + 4), a), at("PM", 2 * a + b), at("Qt", j, p, (b, 8, 2))) for a in range(2) for b in range(2)]
            mms(pairs("b4", 8 + 4 * p, 3))
            turn32(at("O", (k0, k1)), at("b4", (8 + 4 * p, 12 + 4 * p)))
            own = at("O", (k0, k1), (0, 4), 0)
            mms([(at(ub, (4, 6)), IdK, at("RK")), (at(ub, (4, 6)), BM, qt(3)), (at(ub, (6, 8)), BM, qt(3))])
            for d in range(4):
                tt(at("EQ", (k0, k1), (80 * d + (d - 1) % 5, 320, 5)), at("O", (k0, k1), (d, 4)), at(ub, (6, 8) if d else (4, 6), (0, 4 - d)), A.is_equal)
            scaled("S", at("EQ", (k0, k1), (78, 320, 80)), own, 1.0 / 1024, 15 * FLOOR / 1024)
            for k in range(k1 - 1, k0 - 1, -1):
                scan(at("lose", k), at("EQ", k), at("DM"))
            for ka, kb in ((k0, k1),) if POS_CUT[gi] == 1 else ((k0 + 1, k1), (k0, k0 + 1)):
                scaled("S", at("posU", (4 * ka, 4 * kb)), at("lose", (ka, kb), (78, 320, 80)), 8192.0, 2048.0 + SPARE)
            now[1] = "fork%d" % gi
            mms(pairs(bank, 4, 1))
            turn32(at("O2"), at(bank, (4, 8)))
            scaled("S", at("cs", t, (q0, q1)), at("O2", (0, 128, 16)), 8.0, 131072.0 + 6144 + 8 * (lanes - OFF - TOP))
            send(at("rcv", t, (q0, q1)), at("cs", t, (q0, q1)), "n%d_%d" % (t, gi), dst)
            now[1] = "column%d" % gi
            act(q("JC1"), own, F.Relu, scale=8.0, bias=2048.0 + 120 * FLOOR)
            nc = at(bank, (0, 4))
            plus("S", h("old"), ind(at("So") if gi and KEEP else swin, q("JC1")), -2048.0)
            if gi in ROUND:
                mms([(nc, IdN8, qt(0)), (nc, Id, con(0, 128)), (nc, IdN, h("old")), (nc, IdK, con(1, 128)), (nc, IdK, con(2, 128)), (nc, Id8, qt(0)), (nc, Id, h("old"))])
                plus("S", h("nd"), nc, 2048.0)
            else:
                mms([(nc, Id8, qt(0)), (nc, Id, h("old"))])
                plus("S", h("nc"), nc, 2048.0)
                ts(h("nd"), h("nc"), 4095, A.bitwise_and)

        def lists(gi, lo, hi):
            now[1] = "lists%d" % gi
            p0, p1, q0, q1 = lo // 128, hi // 128, lo // 16, hi // 16
            w, n = p1 - p0, q1 - q0
            L = lambda j, k=1: at("c%d" % gi, (32 + w * j, 32 + w * (j + k)))
            q = lambda nm: at(nm, (q0, q1))
            mms([(L(0, NT), IdK, at("JC", (0, NT), (q0, q1))), (L(2), Id5, q("sF"))], True, False)
            for r0 in range(0, 16, LR_CUT[gi]):
                mms([(L(0, NT), at("LR", (15 - r, 143 - r)), at("Qt", (0, NT), (p0, p1), (0, 8), r)) for r in range(r0, r0 + LR_CUT[gi])], False, r0 + LR_CUT[gi] == 16)
            plus("S", q("none"), L(2), 14336.0)
            tt(q("m0"), L(3), q("none"), A.max)
            plus("S", q("yi"), L(0), 2048.0)
            act(at("JU", (2 * q0, 2 * q1)), L(0, 2), F.Relu, scale=1.0 / 8192, bias=2047.5 - 16 * lo)
            for a, b in ((n, 2 * n), (0, n)) if gi else ((0, 2 * n),):
                act(at("zz", (2 * lo + 16 * a, 2 * lo + 16 * b)), ind(at(D, (16 * lo, 16 * hi)), at("JU", (2 * q0 + a, 2 * q0 + b))), F.Abs)

        for gi in range(2):
            gathers(gi)
        for gi, (lo, hi) in enumerate(PARTS):
            claims(gi)
            if not join[0]:
                lists(gi, lo, hi)
        if join[0]:
            lists(1, 0, 256)
        now[1] = "S"
        for j in range(3, -1, -1):
            cp(ind(at("Si"), at("posU", (4 * j, 4 * j + 4))), at("nd", (64 * j, 64 * j + 64)))
        for gi, (lo, hi) in enumerate(((0, 256),) if join[1] else PARTS):
            now[1] = "X%d" % gi
            q = lambda nm: at(nm, (lo // 16, hi // 16))
            ts(q("y7"), q("yi"), X0 + 7, A.bitwise_and)
            tt(q("WLU"), q("y7"), q("I8"), A.add)
        for gi, (lo, hi) in enumerate(((0, 256),) if join[2] else PARTS):
            now[1] = "X%d" % gi
            cp(ind(at("XX", (0, X0 + 8 * hi)), at("WLU", (lo // 16, hi // 16))), z1(lo, hi))
            dma(T.yv[:, 8 * lo:8 * hi] if last else at("XX", (X0 + 2048 + 8 * lo, X0 + 2048 + 8 * hi)), at("XX", (X0 + 8 * lo, X0 + 8 * hi)))
        for gi, (lo, hi) in enumerate(PARTS):
            now[1] = "place%d" % gi
            q = lambda nm: at(nm, (lo // 16, hi // 16))
            tt(q("m1"), q("m0"), at("rcv", t, (lo // 16, hi // 16)), A.max)
            ts(q("sL"), q("m1"), 4095, A.bitwise_and)
            if not last:
                plus("S", q("sU"), q("sL"), 0.0)
        if last:
            cp(at("yso"), at("sL"))
            dma(T.ys[:], at("yso"))
        else:
            act(at("jk"), at("cs", t), F.Sign, acc=acc)
            act(at("accB"), on, F.Identity, scale=kap, bias=acc)
        now[1] = "x"
        xo = at("XC", (x0, x0 + 256))
        half = lambda b, lo, hi: at("b%d" % b, (lo // 32, hi // 32))
        for gi, (c0, c1) in enumerate(PARTS if last else ((0, 256),)):
            mms([(half(0, c0, c1), IdN, at("XC", (x0 + c0, x0 + c1)))] + [(half(0, lo, hi), Id, z2(lo, hi)) for lo, hi in both if c0 <= lo < c1])
            act(at("Y", t, (c0, c1)), half(0, c0, c1), F.Abs)
            send(at("XC", (x0 + 256 + c0, x0 + 256 + c1)), at("Y", t, (c0, c1)), "x%d" % (t + gi), dst)
        yh = half(1, 0, 256)
        mms([(yh, IdH, xo)] + [(half(1, lo, hi), IdH, z1(lo, hi)) for lo, hi in both])
        plus("S", at("ha"), yh, -0.25)
        plus("S", at("XC", (x0 + 512, x0 + 768)), at("ha"), 0.0)
        ts(at("xt"), at("m1"), 9, A.arith_shift_right, 768, A.bitwise_and)
        tt(at("XLU"), at("xt"), at("Ic"), A.add)
        xn = at("XC", (x0 + 768, x0 + 1024))
        plus("S", xn, ind(at("XC", (x0, x0 + 768)), at("XLU")), 0.0)
        if last:
            dma(T.yx[:], xn)

    for t in range(STEPS):
        step(t)

    now[1] = "yt"
    yt, a = at("b0", (0, 8)), 0
    for q, k in YT_CUT:
        b = a + 256 * k
        plus(q, at("S16", (a, b)), at("Si", (SPARE + a, SPARE + b)), -2048.0)
        mms([(yt, Id, at("S16", (c, c + 256))) for c in range(a, b, 256)], a == 0, b == 4096)
        a = b
    plus("V", at("yto"), yt, 16 * 2048.0)
    dma(T.yt[:], at("yto"))


def depends(ops):
    seen = {}
    for i, o in enumerate(ops):
        d = set()
        acc = [(x, False) for x in o["r"]] + [(x, True) for x in o["w"]]
        for (b, m), wr in acc:
            for (j, m2, w2) in seen.get(b, ()):
                if (wr or w2) and m & m2:
                    d.add(j)
        for (b, m), wr in acc:
            lst = seen.setdefault(b, [])
            if wr:
                lst[:] = [x for x in lst if x[1] & ~m]
            lst.append((i, m, wr))
        d.discard(i)
        if o.get("goes on"):
            o["hard"] += [j for j in d if ops[j].get("open")]
            d -= set(o["hard"])
        o["d"] = d


def plan(ops, cases):
    n = len(ops)
    names = sorted(set(o["q"] for o in ops) | set(b for o in ops for b in o["banks"]))
    queue = [names.index(o["q"]) if o["kind"] != "recv" else -1 for o in ops]
    banks = [[names.index(b) for b in sorted(o["banks"])] for o in ops]
    near, hard, before = [], [], []
    for o in ops:
        far = 0
        for j in o["d"]:
            far |= before[j]
        near.append(sorted(j for j in o["d"] if not far >> j & 1))
        hard.append(sorted(j for j in set(o["hard"]) - o["d"] if not far >> j & 1))
        before.append(far | sum(1 << j for j in o["d"]))
    ways = []
    for dur, wake, same in cases:
        hold = [ops[i]["hold"] or dur[i] for i in range(n)]
        ahead = [[(j, dur[j] + (same if queue[j] == queue[i] else wake)) for j in near[i]] + [(j, hold[j]) for j in hard[i]] for i in range(n)]
        ways.append((dur, hold, wake, ahead))
    dur, hold, wake, ahead = ways[0]
    back = [[] for _ in range(n)]
    for i in range(n):
        for j, w in ahead[i]:
            back[j].append((i, dur[i] + w - dur[j]))
    span, rank = np.array(dur), np.arange(n)
    fore = [(i, queue[i], ahead[i], hold[i] - 1e-9, 0.0, banks[i]) for i in range(n)]
    aft = [(i, queue[i], back[i], hold[i] - 1e-9, dur[i] - hold[i], banks[i]) for i in range(n)]

    def fit(order, calls):
        begin = [0.0] * n
        used = [[] for _ in names]
        for x in order:
            i, q, edges, h, late, bs = calls[x]
            s = 0.0
            for j, w in edges:
                w += begin[j]
                if w > s:
                    s = w
            if q >= 0:
                s += late
                u = used[q]
                while True:
                    k = m = len(u)
                    while k and u[k - 1][1] > s:
                        k -= 1
                    while k < m and u[k][0] < s + h:
                        s = u[k][1]
                        k += 1
                    t = s
                    for b in bs:
                        for y, z, p in used[b][-8:]:
                            if p != q and y < s + h + wake and z > s:
                                s = z
                    if s == t:
                        break
                u.insert(k, (s, s + h))
                for b in bs:
                    used[b].append((s, s + h + wake, q))
                s -= late
            begin[i] = s
        return np.array(begin)

    def run(c, order):
        dur, hold, wake, ahead = ways[c]
        begin, free, user = [0.0] * n, [0.0] * len(names), [{} for _ in names]
        top = 0.0
        for i in order:
            q = queue[i]
            s = free[q] if q >= 0 else 0.0
            for j, w in ahead[i]:
                w += begin[j]
                if w > s:
                    s = w
            for b in banks[i]:
                for p, y in user[b].items():
                    if p != q and y > s:
                        s = y
            e = s + dur[i]
            for b in banks[i]:
                user[b][q] = e + wake
            begin[i] = s
            if q >= 0:
                free[q] = s + hold[i]
            if e > top:
                top = e
        return top

    def both(key, limit):
        for i in range(n):
            for j, w in ahead[i]:
                if key[j] > key[i]:
                    key[i] = key[j]
        a = fit(np.lexsort((rank, key)).tolist(), fore)
        b = fit(np.lexsort((-rank, -a - span)).tolist(), aft)
        a = fit(np.lexsort((rank, -b - span)).tolist(), fore)
        top = (a + span).max()
        if top > limit:
            return None
        order = np.lexsort((rank, a)).tolist()
        return sum(run(k, order) for k in range(len(cases))) / len(cases), a, order, top

    rng = np.random.default_rng(SEED)
    slots = {}
    slot = np.array([slots.setdefault(o["slot"], len(slots)) for o in ops])
    step = np.array([o["step"] for o in ops])
    inner = np.array([o["task"] not in ("start", "yt") for o in ops])
    first = [i for i in range(n) if ops[i]["slot"] == "cU.gathers.1"]
    late = -fit(range(n - 1, -1, -1), aft) - span
    turn = ORDER.split()
    place = {x.strip("+-"): j / len(turn) + x.count("+") - x.count("-") for j, x in enumerate(turn)}
    now = best = both([late[i] - 1e3 if o["task"] == "start" else o["step"] + place.get(o["slot"], 0.0) for i, o in enumerate(ops)], 1e9)
    for it in range(TRIES):
        key = now[1]
        tied = it < TIED * TRIES
        if tied or rng.random() < ALIKE:
            t0, mine = key[first], inner & (step == (1 if tied else rng.integers(len(first))))
            rel = np.full(len(slots), 1e9)
            rel[slot[mine]] = (key - t0[step])[mine]
            close = np.abs(rel - rng.random() * 24) < (1 if tied else 2) * SPAN * rng.random()
            if tied:
                rel += close * rng.normal(0, NOISE * rng.random(), len(slots))
            key = np.where(inner & (rel < 1e8 if tied else close)[slot], rel[slot] + t0[step], key)
        else:
            key = key + (np.abs(key - rng.random() * key.max()) < SPAN * rng.random()) * rng.normal(0, NOISE * rng.random(), n)
        new = both(key.tolist(), now[3] + 1.0)
        if new and new[0] <= now[0] + SLACK * (1 - it / TRIES) * rng.random():
            now = new
            if new[0] < best[0]:
                best = new
    extra, users = [], {}
    for i in best[2]:
        for b in sorted(ops[i]["banks"]):
            u = users.setdefault(b, {})
            extra += [(i, j) for q, j in u.items() if q != ops[i]["q"]]
            u[ops[i]["q"]] = i
    return best[2], extra, best[0]


def rank_program(g, core, T, topo):
    if T.rank_of(core) is None:
        return
    ops = []
    build(core, T, topo, ops, EST)
    depends(ops)
    if "order" not in PLAN:
        cases = []
        for c in CASES:
            other, est = [], dict(EST, **c)
            build(core, T, topo, other, est)
            cases.append(([o["dur"] for o in other], est["wake"], est["same"]))
        PLAN["order"] = plan(ops, cases)
    order = PLAN["order"][0]
    for i, j in PLAN["order"][1]:
        ops[i]["d"].add(j)
    eng = {"V": g.vector, "S": g.scalar, "P": g.tensor, "G": g, "Y": g.sync}
    know = {}
    for q in eng:
        know[q] = {}
    count = {}
    token = {}
    clock = {}

    def learn(q, tok):
        k = know[q]
        for s, c in clock.get(tok, {}).items():
            if k.get(s, 0) < c:
                k[s] = c
        if k.get(tok[0], 0) < tok[1]:
            k[tok[0]] = tok[1]

    for i in order:
        o = ops[i]
        if o["kind"] == "recv":
            token[i] = (o["sem"], o["cnt"])
            continue
        q = o["q"]
        e = eng[q]
        want = {}
        for j in o["d"]:
            if ops[j]["kind"] == "send":
                continue
            s, c = token[j]
            want[s] = max(want.get(s, 0), c)
        for s in sorted(want, key=lambda s: (-sum(clock.get((s, want[s]), {}).values()), s)):
            if know[q].get(s, 0) < want[s]:
                e.wait_ge(T.sem[s], want[s])
                learn(q, (s, want[s]))
        ins = o["fn"](e)
        if o["kind"] == "send":
            continue
        if o["kind"] == "dma":
            ins.then_inc(T.sem[o["sem"]], 16)
            token[i] = (o["sem"], 16)
        else:
            s = "e" + q
            count[s] = count.get(s, 0) + 1
            ins.then_inc(T.sem[s], 1)
            token[i] = (s, count[s])
        clock[token[i]] = dict(know[q])
        clock[token[i]][token[i][0]] = token[i][1]
    for s in sorted(count):
        g.wait_ge(T.sem[s], count[s])
    for o in ops:
        if o["kind"] == "dma":
            g.wait_ge(T.sem[o["sem"]], 16)
        if o["kind"] == "send":
            g.wait_ge(T.sem["l" + o["sem"][1:]], o["cnt"])
            g.wait_ge(T.sem[o["sem"]], o["cnt"])
